import numpy as np
import ml_dtypes


def mxq(x, axis, fmt="e4m3"):
    dtype, down = {"e4m3": (ml_dtypes.float8_e4m3fn, 7), "e5m2": (ml_dtypes.float8_e5m2, 14)}[fmt]
    v = np.moveaxis(np.asarray(x, np.float32).astype(ml_dtypes.bfloat16).astype(np.float64), axis, -1)
    blocks = v.reshape(v.shape[:-1] + (-1, 32))
    amax = np.abs(blocks).max(-1, keepdims=True)
    byte = np.maximum(np.where(amax > 0, np.frexp(amax)[1] - 1 + 127, 0) - down, 1)
    scale = np.exp2(byte - 127.0)
    codes = (blocks / scale).astype(np.float32).astype(dtype).astype(np.float64)
    return np.moveaxis((codes * scale).reshape(v.shape), -1, axis)


WIDE = False


def mx_kscale(k):
    if not WIDE:
        return np.ones(k)
    levels = np.array([10, -10, 5, -5, 0])
    if k % 512:
        return np.exp2(np.random.permutation(np.resize(levels, k // 32))).repeat(32)
    a = np.empty((k // 512, 16))
    for p in range(k // 512):
        a[p, :8] = np.random.permutation(np.resize(levels, 8))
        for g in range(8):
            far = levels[np.abs(levels - a[p, g]) >= 10]
            a[p, g + 8] = far[np.random.randint(len(far))]
    return np.exp2(a.ravel()).repeat(32)


def f64(x):
    return np.asarray(x).astype(np.float64)


def striped(idx):
    return np.tile(idx.reshape(-1, 16).T, (8, 1)).astype(np.uint16)


def unstriped(offs):
    return offs[:16].T.reshape(-1).astype(np.int64)


def relu(v):
    return np.maximum(v, 0.0)


K, T, D, S, V, H, N = 1024, 2048, 4, 512, 256, 1024, 512
P = 2 ** 7


def setup_inputs():
    n = np.random.standard_normal
    s = mx_kscale(K)[:, None]
    u = mx_kscale(H)
    q = np.random.permutation(S)
    return {
        "xT": (n((K, T)) * s).astype(np.float32),
        "w1": (n((K, H)) / np.sqrt(K) / s * u).astype(np.float32),
        "w2": (n((H, N)) / np.sqrt(H) / u[:, None]).astype(np.float32),
        "gate": np.tile(np.random.uniform(0.2, 1.0, (D, 1, V)) / np.sqrt(D), (1, P, 1)).astype(np.float32),
        "offs": striped(np.random.permutation(T)[:S]),
        "pos1": striped(q[:V]),
        "pos2": striped(q[V:]),
        "pos3": striped(np.random.permutation(S)[:V]),
        "pos4": striped(np.random.permutation(S)[:V]),
    }


def reference(xT, w1, w2, gate, offs, pos1, pos2, pos3, pos4):
    h = relu(mxq(f64(w1), 0, "e4m3").T @ mxq(f64(xT)[:, unstriped(offs)], 0, "e4m3"))
    z = sum(f64(gate)[d, :1] * h[:, unstriped(p)] for d, p in enumerate((pos1, pos2, pos3, pos4)))
    return mxq(f64(w2), 0, "e4m3").T @ mxq(z, 0, "e4m3")

@@ -1,0 +1,331 @@
+from contextlib import ExitStack
+
+import concourse.mybir as mybir
+from concourse.masks import make_identity
+
+K, T, D, S, V, H, N = 1024, 2048, 4, 512, 256, 1024, 512
+P = 128
+PACK = 4
+K_PASS = P * PACK
+PASSES = K // K_PASS
+BLOCKS = H // P
+HALVES = V // P
+FLOPS = 2 * S * K * H + 2 * V * H * N + 2 * D * V * H
+
+F32 = mybir.dt.float32
+BF16 = mybir.dt.bfloat16
+U32 = mybir.dt.uint32
+U16 = mybir.dt.uint16
+U8 = mybir.dt.uint8
+FP8X4 = mybir.dt.float8_e4m3fn_x4
+RELU = mybir.ActivationFunctionType.Relu
+MULT = mybir.AluOpType.mult
+
+W2_AFTER = (4, 5)
+W1_LOADS = (1, 1, 1, 1, 2, 2)
+
+
+def tile_picked_sage_relu_e_kernel(
+    tc, xT, w1, w2, gate, offs, pos1, pos2, pos3, pos4, out
+):
+    nc = tc.nc
+    with ExitStack() as ctx:
+        lists = ctx.enter_context(tc.tile_pool(name="lists", bufs=1))
+        keep = ctx.enter_context(tc.tile_pool(name="keep", bufs=1))
+        hpool = ctx.enter_context(tc.tile_pool(name="hpool", bufs=4))
+        prods = ctx.enter_context(tc.tile_pool(name="prods", bufs=12))
+        psum = ctx.enter_context(tc.psum_pool(name="psum", bufs=4))
+
+        offs_sb = lists.tile([P, S // 16], U16, name="offs_sb")
+        pos_sb = [lists.tile([P, V // 16], U16, name=f"pos_sb{d}") for d in range(D)]
+
+        ident = keep.tile([P, P], F32, name="ident")
+        make_identity(nc, ident[:])
+        warm = keep.tile([P, 1], F32, name="warm")
+        nc.gpsimd.memset(warm[:], 0.0)
+        warm_out = keep.tile([P, 1], F32, name="warm_out")
+        nc.scalar.activation(warm_out[:], warm[:], RELU)
+
+        x_raw = [[keep.tile([P, T], F32, name=f"x_raw{s}_{j}") for j in range(PACK)] for s in range(PASSES)]
+        w1_raw = [keep.tile([P, PASSES, PACK, n * P], F32, name=f"w1_raw{c}") for c, n in enumerate(W1_LOADS)]
+        w2_raw = [keep.tile([P, PACK, N], F32, name=f"w2_raw{s}") for s in range(PASSES)]
+        gate_rows = keep.tile([P, P], F32, name="gate_rows")
+        nc.gpsimd.memset(gate_rows[:], 0.0)
+        gate_cols = keep.tile([P, D * HALVES], F32, name="gate_cols")
+        gate_sb = keep.tile([P, D, V], F32, name="gate_sb")
+        home = [(c, i) for c, n in enumerate(W1_LOADS) for i in range(n)]
+
+        def load_x(s, j):
+            rows = xT[s * K_PASS : (s + 1) * K_PASS, :].rearrange("(p j) t -> j p t", j=PACK)
+            nc.sync.dma_start(out=x_raw[s][j][:], in_=rows[j])
+
+        def load_w1(c, s):
+            first = sum(W1_LOADS[:c]) * P
+            block = w1[s * K_PASS : (s + 1) * K_PASS, first : first + W1_LOADS[c] * P]
+            nc.sync.dma_start(out=w1_raw[c][:, s], in_=block.rearrange("(p j) m -> p j m", j=PACK))
+
+        nc.sync.dma_start(offs_sb[:], offs)
+        for s in range(PASSES):
+            for j in range(PACK):
+                load_x(s, j)
+                if (s, j) == (0, 1):
+                    for d in range(D):
+                        nc.sync.dma_start(
+                            out=gate_rows[HALVES * d : HALVES * (d + 1), :],
+                            in_=gate[d, 0, :].rearrange("(v n) -> v n", v=HALVES),
+                        )
+                if (s, j) == (0, 3):
+                    for d, pos in enumerate((pos1, pos2, pos3, pos4)):
+                        nc.sync.dma_start(pos_sb[d][:], pos)
+        for c in range(len(W1_LOADS)):
+            for s in range(PASSES):
+                load_w1(c, s)
+        for s in range(PASSES):
+            nc.sync.dma_start(
+                out=w2_raw[s][:], in_=w2[s * K_PASS : (s + 1) * K_PASS, :].rearrange("(p j) n -> p j n", j=PACK)
+            )
+
+        w1_grp = [
+            keep.tile([P, PASSES, P, PACK], BF16, name=f"w1_grp{b}", tag=f"turn{b}", align_bytes=64)
+            for b in range(BLOCKS)
+        ]
+        w1_codes = [keep.tile([P, PASSES, P], U32, name=f"w1_codes{b}", align_bytes=64) for b in range(BLOCKS)]
+        w1_scales = [keep.tile([P, PASSES, P], U8, name=f"w1_scales{b}", align_bytes=64) for b in range(BLOCKS)]
+        w2_grp = {}
+        w2_codes = [keep.tile([P, N], U32, name=f"w2_codes{s}", align_bytes=64) for s in range(PASSES)]
+        w2_scales = [keep.tile([P, N], U8, name=f"w2_scales{s}", align_bytes=64) for s in range(PASSES)]
+
+        def group_w1(b, s):
+            c, i = home[b]
+            nc.scalar.copy(
+                out=w1_grp[b][:, s].rearrange("p (c i) j -> p c j i", i=4),
+                in_=w1_raw[c][:, s, :, i * P : (i + 1) * P].rearrange("p j (c i) -> p c j i", i=4),
+            )
+
+        def quantize_w1(b):
+            nc.vector.quantize_mx(
+                out=w1_codes[b][:].rearrange("p s m -> p (s m)").bitcast(FP8X4),
+                scales=w1_scales[b][:].rearrange("p s m -> p (s m)"),
+                in_=w1_grp[b][:].rearrange("p s m j -> p (s m j)"),
+            )
+
+        def quantize_w1_pass(b, s):
+            nc.vector.quantize_mx(
+                out=w1_codes[b][:, s].bitcast(FP8X4),
+                scales=w1_scales[b][:, s],
+                in_=w1_grp[b][:, s].rearrange("p m j -> p (m j)"),
+            )
+
+        def group_w2(s, n0, n1):
+            if n0 == 0:
+                w2_grp[s] = keep.tile(
+                    [P, N, PACK], BF16, name=f"w2_grp{s}", tag=f"h_turn{W2_AFTER[s]}", align_bytes=64
+                )
+            nc.scalar.copy(
+                out=w2_grp[s][:, n0:n1, :].rearrange("p (c i) j -> p c j i", i=4),
+                in_=w2_raw[s][:, :, n0:n1].rearrange("p j (c i) -> p c j i", i=4),
+            )
+
+        def quantize_w2(s):
+            nc.vector.quantize_mx(
+                out=w2_codes[s][:].bitcast(FP8X4),
+                scales=w2_scales[s][:],
+                in_=w2_grp[s][:].rearrange("p n j -> p (n j)"),
+            )
+
+        spread = psum.tile([P, P], F32, name="spread", tag="bank")
+        nc.tensor.transpose(spread[:], gate_rows[:], ident[:])
+        nc.scalar.copy(out=gate_cols[:], in_=spread[:, : D * HALVES])
+        for g in range(D // 2):
+            spread = psum.tile([P, 2 * V], F32, name="spread", tag="bank")
+            for r in range(2 * HALVES):
+                column = gate_cols[:, 2 * HALVES * g + r : 2 * HALVES * g + r + 1]
+                nc.tensor.transpose(spread[:, r * P : (r + 1) * P], column.to_broadcast([P, P]), ident[:])
+            nc.scalar.copy(out=gate_sb[:, 2 * g : 2 * g + 2, :].rearrange("p d v -> p (d v)"), in_=spread[:])
+
+        x_grp = [keep.tile([P, S, PACK], BF16, name=f"x_grp{s}", align_bytes=64) for s in range(PASSES)]
+        x_codes = [keep.tile([P, S], U32, name=f"x_codes{s}", align_bytes=64) for s in range(PASSES)]
+        x_scales = [keep.tile([P, S], U8, name=f"x_scales{s}", align_bytes=64) for s in range(PASSES)]
+        HALF = S // 2
+        for s in range(PASSES):
+            last = s == PASSES - 1
+            for j in range(PACK):
+                if last and j == PACK - 1:
+                    group_w1(0, 0)
+                    quantize_w1_pass(0, 0)
+                    group_w1(0, 1)
+                    for t in (0, 1):
+                        nc.vector.tensor_copy(
+                            x_grp[s][:, t * HALF : (t + 1) * HALF, j],
+                            x_raw[s][j][:].indirect(offs_sb[:, t * HALF // 16 : (t + 1) * HALF // 16]),
+                        )
+                    quantize_w1_pass(0, 1)
+                else:
+                    nc.vector.tensor_copy(x_grp[s][:, :, j], x_raw[s][j][:].indirect(offs_sb[:]))
+            for t in (0, 1) if last else (None,):
+                cols = slice(0, S) if t is None else slice(t * HALF, (t + 1) * HALF)
+                nc.vector.quantize_mx(
+                    out=x_codes[s][:, cols].bitcast(FP8X4),
+                    scales=x_scales[s][:, cols],
+                    in_=x_grp[s][:, cols, :].rearrange("p t j -> p (t j)"),
+                )
+
+        def project(b):
+            if b in W2_AFTER:
+                h = keep.tile([P, S], F32, name="h_turn", tag=f"h_turn{b}", align_bytes=64)
+            else:
+                h = hpool.tile([P, S], F32, name="h")
+            width = HALF if b == 0 else S
+            for t in range(S // width):
+                acc = psum.tile([P, S], F32, name="acc", tag="bank")
+                nodes = slice(t * width, (t + 1) * width)
+                for s in range(PASSES):
+                    nc.tensor.matmul_mx(
+                        out=acc[:, :width],
+                        lhsT=w1_codes[b][:, s].bitcast(FP8X4),
+                        lhsT_scale=w1_scales[b][:, s],
+                        rhs=x_codes[s][:, nodes].bitcast(FP8X4),
+                        rhs_scale=x_scales[s][:, nodes],
+                        start=(s == 0),
+                        stop=(s == PASSES - 1),
+                    )
+                if b > 0:
+                    nc.scalar.activation(h[:, nodes], acc[:, :width], RELU)
+                else:
+                    nc.vector.tensor_relu(h[:, nodes], acc[:, :width])
+            return h
+
+        z_t = [keep.tile([P, H], BF16, name=f"z_t{v}", align_bytes=64) for v in range(HALVES)]
+        z_grp = [keep.tile([P, V * PACK], BF16, name=f"z_grp{s}", align_bytes=64) for s in range(PASSES)]
+        z_codes = [keep.tile([P, V], U32, name=f"z_codes{s}", align_bytes=64) for s in range(PASSES)]
+        z_scales = [keep.tile([P, V], U8, name=f"z_scales{s}", align_bytes=64) for s in range(PASSES)]
+        out_acc = {}
+
+        def add_transposed(b, d, v, prod):
+            nc.tensor.matmul(
+                z_ps[v][:, (b % PACK) * P : (b % PACK + 1) * P],
+                prod,
+                ident[:],
+                start=(d == 0),
+                stop=(d == D - 1),
+                is_transpose=True,
+            )
+
+        def gather_block(b, h):
+            for d in range(D):
+                if d == 1 and b + 1 < BLOCKS:
+                    prod = keep.tile([P, V], F32, name="prod_turn", tag=f"turn{b + 1}", align_bytes=64)
+                else:
+                    prod = prods.tile([P, V], F32, name="prod")
+                nc.vector.tensor_tensor(prod[:], h[:].indirect(pos_sb[d][:]), gate_sb[:, d, :], MULT)
+                for v in range(HALVES):
+                    add_transposed(b, d, v, prod[:, v * P : (v + 1) * P])
+
+        def gather_half(b, h, v):
+            for d in range(D):
+                prod = prods.tile([P, P], F32, name="prod")
+                nc.vector.tensor_tensor(
+                    prod[:],
+                    h[:].indirect(pos_sb[d][:, v * P // 16 : (v + 1) * P // 16]),
+                    gate_sb[:, d, v * P : (v + 1) * P],
+                    MULT,
+                )
+                add_transposed(b, d, v, prod[:])
+
+        def z_out(s, v, b0, b1):
+            nc.scalar.copy(
+                out=z_t[v][:, s * K_PASS + b0 * P : s * K_PASS + b1 * P], in_=z_ps[v][:, b0 * P : b1 * P]
+            )
+
+        def z_words(s, v):
+            if s == LAST:
+                words = psum.tile([P, 2, P], F32, name="words", tag=f"z_ps{v}", bufs=2)
+            else:
+                words = psum.tile([P, 2, P], F32, name="words", tag="bank")
+            zw = z_t[v][:].bitcast(F32)
+            for u in range(2):
+                nc.tensor.transpose(
+                    words[:, u, :], zw[:, s * (K_PASS // 2) + u : (s + 1) * (K_PASS // 2) : 2], ident[:]
+                )
+            nc.scalar.copy(
+                out=z_grp[s][:, v * K_PASS : (v + 1) * K_PASS].bitcast(F32).rearrange("p (n u) -> p n u", u=2),
+                in_=words[:].rearrange("p u n -> p n u"),
+            )
+
+        def quantize_z(s, v0, v1):
+            nc.vector.quantize_mx(
+                out=z_codes[s][:, v0 * P : v1 * P].bitcast(FP8X4),
+                scales=z_scales[s][:, v0 * P : v1 * P],
+                in_=z_grp[s][:, v0 * K_PASS : v1 * K_PASS],
+            )
+
+        def out_pass(s, m, v):
+            cols = slice(m * P, (m + 1) * P)
+            nodes = slice(v * P, (v + 1) * P)
+            nc.tensor.matmul_mx(
+                out=out_acc[m][:, nodes],
+                lhsT=w2_codes[s][:, cols].bitcast(FP8X4),
+                lhsT_scale=w2_scales[s][:, cols],
+                rhs=z_codes[s][:, nodes].bitcast(FP8X4),
+                rhs_scale=z_scales[s][:, nodes],
+                start=(s == 0),
+                stop=(s == PASSES - 1),
+            )
+
+        LAST = PASSES - 1
+        M_TILES = N // P
+        result = [keep.tile([P, M_TILES, P], F32, name=f"result{v}") for v in range(HALVES)]
+
+        def finish_half(v):
+            z_out(LAST, v, PACK - 1, PACK)
+            z_words(LAST, v)
+            quantize_z(LAST, v, v + 1)
+            for m in range(M_TILES):
+                out_pass(LAST, m, v)
+                copy = (nc.scalar.copy, nc.vector.tensor_copy)[m % 2]
+                copy(out=result[v][:, m, :], in_=out_acc[m][:, v * P : (v + 1) * P])
+                nc.sync.dma_start(out=out[m * P : (m + 1) * P, v * P : (v + 1) * P], in_=result[v][:, m, :])
+                if v + 1 < HALVES:
+                    out_pass(0, m, v + 1)
+
+        h_next = project(0)
+        for s in range(PASSES):
+            group_w1(1, s)
+        quantize_w1(1)
+        for b in range(BLOCKS):
+            if b % PACK == 0:
+                z_ps = [psum.tile([P, K_PASS], F32, name=f"z_ps{v}", tag=f"z_ps{v}", bufs=2) for v in range(HALVES)]
+            h = h_next
+            if b + 2 < BLOCKS:
+                for s in range(PASSES):
+                    group_w1(b + 2, s)
+            if b + 1 < BLOCKS:
+                h_next = project(b + 1)
+            if b == BLOCKS - 1:
+                for v in range(HALVES):
+                    gather_half(b, h, v)
+                    if v == 0:
+                        finish_half(v)
+            else:
+                gather_block(b, h)
+            if b + 2 < BLOCKS:
+                quantize_w1(b + 2)
+            if b == PACK - 1:
+                for v in range(HALVES):
+                    z_out(0, v, 0, PACK)
+            if b == PACK:
+                for v in range(HALVES):
+                    z_words(0, v)
+                quantize_z(0, 0, HALVES)
+            if b in W2_AFTER:
+                s = W2_AFTER.index(b)
+                for n in (0, 1):
+                    group_w2(s, n * HALF, (n + 1) * HALF)
+                quantize_w2(s)
+            if b == 6:
+                for v in range(HALVES):
+                    z_out(LAST, v, 0, PACK - 1)
+                for m in range(M_TILES):
+                    out_acc[m] = psum.tile([P, S], F32, name="out_acc", tag="bank")
+                    out_pass(0, m, 0)
+        finish_half(1)

@@ -21,7 +21,6 @@ FP8X4 = mybir.dt.float8_e4m3fn_x4
 RELU = mybir.ActivationFunctionType.Relu
 MULT = mybir.AluOpType.mult
 
-W2_AFTER = (4, 5)
 W1_LOADS = (1, 1, 1, 1, 2, 2)
 
 
@@ -48,11 +47,13 @@ def tile_picked_sage_relu_e_kernel(
 
         x_raw = [[keep.tile([P, T], F32, name=f"x_raw{s}_{j}") for j in range(PACK)] for s in range(PASSES)]
         w1_raw = [keep.tile([P, PASSES, PACK, n * P], F32, name=f"w1_raw{c}") for c, n in enumerate(W1_LOADS)]
-        w2_raw = [keep.tile([P, PACK, N], F32, name=f"w2_raw{s}") for s in range(PASSES)]
+        w2_raw = [
+            keep.tile([P, PACK, N], F32, name=f"w2_raw{s}", tag=f"w2_turn{s}", align_bytes=64) for s in range(PASSES)
+        ]
         gate_rows = keep.tile([P, P], F32, name="gate_rows")
         nc.gpsimd.memset(gate_rows[:], 0.0)
         gate_cols = keep.tile([P, D * HALVES], F32, name="gate_cols")
-        gate_sb = keep.tile([P, D, V], F32, name="gate_sb")
+        gate_sb = [keep.tile([P, V], F32, name=f"gate_sb{d}", tag=f"gate{d}", align_bytes=64) for d in range(D)]
         home = [(c, i) for c, n in enumerate(W1_LOADS) for i in range(n)]
 
         def load_x(s, j):
@@ -91,8 +92,8 @@ def tile_picked_sage_relu_e_kernel(
         ]
         w1_codes = [keep.tile([P, PASSES, P], U32, name=f"w1_codes{b}", align_bytes=64) for b in range(BLOCKS)]
         w1_scales = [keep.tile([P, PASSES, P], U8, name=f"w1_scales{b}", align_bytes=64) for b in range(BLOCKS)]
-        w2_grp = {}
-        w2_codes = [keep.tile([P, N], U32, name=f"w2_codes{s}", align_bytes=64) for s in range(PASSES)]
+        w2_grp = [keep.tile([P, N, PACK], BF16, name=f"w2_grp{s}", align_bytes=64) for s in range(PASSES)]
+        w2_codes = {}
         w2_scales = [keep.tile([P, N], U8, name=f"w2_scales{s}", align_bytes=64) for s in range(PASSES)]
 
         def group_w1(b, s):
@@ -117,16 +118,13 @@ def tile_picked_sage_relu_e_kernel(
             )
 
         def group_w2(s, n0, n1):
-            if n0 == 0:
-                w2_grp[s] = keep.tile(
-                    [P, N, PACK], BF16, name=f"w2_grp{s}", tag=f"h_turn{W2_AFTER[s]}", align_bytes=64
-                )
             nc.scalar.copy(
                 out=w2_grp[s][:, n0:n1, :].rearrange("p (c i) j -> p c j i", i=4),
                 in_=w2_raw[s][:, :, n0:n1].rearrange("p j (c i) -> p c j i", i=4),
             )
 
         def quantize_w2(s):
+            w2_codes[s] = keep.tile([P, N], U32, name=f"w2_codes{s}", tag=f"gate{2 * s}", align_bytes=64)
             nc.vector.quantize_mx(
                 out=w2_codes[s][:].bitcast(FP8X4),
                 scales=w2_scales[s][:],
@@ -141,7 +139,8 @@ def tile_picked_sage_relu_e_kernel(
             for r in range(2 * HALVES):
                 column = gate_cols[:, 2 * HALVES * g + r : 2 * HALVES * g + r + 1]
                 nc.tensor.transpose(spread[:, r * P : (r + 1) * P], column.to_broadcast([P, P]), ident[:])
-            nc.scalar.copy(out=gate_sb[:, 2 * g : 2 * g + 2, :].rearrange("p d v -> p (d v)"), in_=spread[:])
+            for r in range(2):
+                nc.scalar.copy(out=gate_sb[2 * g + r][:], in_=spread[:, r * V : (r + 1) * V])
 
         x_grp = [keep.tile([P, S, PACK], BF16, name=f"x_grp{s}", align_bytes=64) for s in range(PASSES)]
         x_codes = [keep.tile([P, S], U32, name=f"x_codes{s}", align_bytes=64) for s in range(PASSES)]
@@ -171,8 +170,8 @@ def tile_picked_sage_relu_e_kernel(
                 )
 
         def project(b):
-            if b in W2_AFTER:
-                h = keep.tile([P, S], F32, name="h_turn", tag=f"h_turn{b}", align_bytes=64)
+            if b == BLOCKS - 1:
+                h = keep.tile([P, S], F32, name="h_turn", tag="w2_turn0", align_bytes=64)
             else:
                 h = hpool.tile([P, S], F32, name="h")
             width = HALF if b == 0 else S
@@ -195,9 +194,9 @@ def tile_picked_sage_relu_e_kernel(
                     nc.vector.tensor_relu(h[:, nodes], acc[:, :width])
             return h
 
-        z_t = [keep.tile([P, H], BF16, name=f"z_t{v}", align_bytes=64) for v in range(HALVES)]
+        z_t = {}
         z_grp = [keep.tile([P, V * PACK], BF16, name=f"z_grp{s}", align_bytes=64) for s in range(PASSES)]
-        z_codes = [keep.tile([P, V], U32, name=f"z_codes{s}", align_bytes=64) for s in range(PASSES)]
+        z_codes = {}
         z_scales = [keep.tile([P, V], U8, name=f"z_scales{s}", align_bytes=64) for s in range(PASSES)]
         out_acc = {}
 
@@ -213,11 +212,13 @@ def tile_picked_sage_relu_e_kernel(
 
         def gather_block(b, h):
             for d in range(D):
-                if d == 1 and b + 1 < BLOCKS:
+                if d == 1 and b < 2:
                     prod = keep.tile([P, V], F32, name="prod_turn", tag=f"turn{b + 1}", align_bytes=64)
+                elif d == 3 and b > 0 and b + 2 < BLOCKS:
+                    prod = keep.tile([P, V], F32, name="prod_turn", tag=f"turn{b + 2}", align_bytes=64)
                 else:
                     prod = prods.tile([P, V], F32, name="prod")
-                nc.vector.tensor_tensor(prod[:], h[:].indirect(pos_sb[d][:]), gate_sb[:, d, :], MULT)
+                nc.vector.tensor_tensor(prod[:], h[:].indirect(pos_sb[d][:]), gate_sb[d][:], MULT)
                 for v in range(HALVES):
                     add_transposed(b, d, v, prod[:, v * P : (v + 1) * P])
 
@@ -227,14 +228,18 @@ def tile_picked_sage_relu_e_kernel(
                 nc.vector.tensor_tensor(
                     prod[:],
                     h[:].indirect(pos_sb[d][:, v * P // 16 : (v + 1) * P // 16]),
-                    gate_sb[:, d, v * P : (v + 1) * P],
+                    gate_sb[d][:, v * P : (v + 1) * P],
                     MULT,
                 )
                 add_transposed(b, d, v, prod[:])
 
         def z_out(s, v, b0, b1):
+            if (s, v) not in z_t:
+                tag = "w2_turn1" if (s, v) == (LAST, 0) else f"z_t{s}_{v}"
+                z_t[s, v] = keep.tile([P, 2, P, 2], BF16, name=f"z_t{s}_{v}", tag=tag, align_bytes=64)
             nc.scalar.copy(
-                out=z_t[v][:, s * K_PASS + b0 * P : s * K_PASS + b1 * P], in_=z_ps[v][:, b0 * P : b1 * P]
+                out=z_t[s, v][:, :, b0 * 32 : b1 * 32, :],
+                in_=z_ps[v][:, b0 * P : b1 * P].rearrange("v (p u e) -> v u p e", u=2, e=2),
             )
 
         def z_words(s, v):
@@ -242,11 +247,9 @@ def tile_picked_sage_relu_e_kernel(
                 words = psum.tile([P, 2, P], F32, name="words", tag=f"z_ps{v}", bufs=2)
             else:
                 words = psum.tile([P, 2, P], F32, name="words", tag="bank")
-            zw = z_t[v][:].bitcast(F32)
             for u in range(2):
-                nc.tensor.transpose(
-                    words[:, u, :], zw[:, s * (K_PASS // 2) + u : (s + 1) * (K_PASS // 2) : 2], ident[:]
-                )
+                zw = z_t[s, v][:, u].rearrange("v p e -> v (p e)").bitcast(F32)
+                nc.tensor.transpose(words[:, u, :], zw, ident[:])
             nc.scalar.copy(
                 out=z_grp[s][:, v * K_PASS : (v + 1) * K_PASS].bitcast(F32).rearrange("p (n u) -> p n u", u=2),
                 in_=words[:].rearrange("p u n -> p n u"),
@@ -259,34 +262,21 @@ def tile_picked_sage_relu_e_kernel(
                 in_=z_grp[s][:, v0 * K_PASS : v1 * K_PASS],
             )
 
-        def out_pass(s, m, v):
+        def out_pass(s, m):
             cols = slice(m * P, (m + 1) * P)
-            nodes = slice(v * P, (v + 1) * P)
             nc.tensor.matmul_mx(
-                out=out_acc[m][:, nodes],
+                out=out_acc[m][:, :V],
                 lhsT=w2_codes[s][:, cols].bitcast(FP8X4),
                 lhsT_scale=w2_scales[s][:, cols],
-                rhs=z_codes[s][:, nodes].bitcast(FP8X4),
-                rhs_scale=z_scales[s][:, nodes],
+                rhs=z_codes[s][:].bitcast(FP8X4),
+                rhs_scale=z_scales[s][:],
                 start=(s == 0),
                 stop=(s == PASSES - 1),
             )
 
         LAST = PASSES - 1
         M_TILES = N // P
-        result = [keep.tile([P, M_TILES, P], F32, name=f"result{v}") for v in range(HALVES)]
-
-        def finish_half(v):
-            z_out(LAST, v, PACK - 1, PACK)
-            z_words(LAST, v)
-            quantize_z(LAST, v, v + 1)
-            for m in range(M_TILES):
-                out_pass(LAST, m, v)
-                copy = (nc.scalar.copy, nc.vector.tensor_copy)[m % 2]
-                copy(out=result[v][:, m, :], in_=out_acc[m][:, v * P : (v + 1) * P])
-                nc.sync.dma_start(out=out[m * P : (m + 1) * P, v * P : (v + 1) * P], in_=result[v][:, m, :])
-                if v + 1 < HALVES:
-                    out_pass(0, m, v + 1)
+        result = [keep.tile([P, V], F32, name=f"result{m}") for m in range(M_TILES)]
 
         h_next = project(0)
         for s in range(PASSES):
@@ -301,31 +291,44 @@ def tile_picked_sage_relu_e_kernel(
                     group_w1(b + 2, s)
             if b + 1 < BLOCKS:
                 h_next = project(b + 1)
+            if b + 2 < BLOCKS and b > 0:
+                quantize_w1(b + 2)
             if b == BLOCKS - 1:
                 for v in range(HALVES):
                     gather_half(b, h, v)
-                    if v == 0:
-                        finish_half(v)
+                    z_out(LAST, v, PACK - 1, PACK)
+                    z_words(LAST, v)
             else:
                 gather_block(b, h)
-            if b + 2 < BLOCKS:
-                quantize_w1(b + 2)
+            if b == 0:
+                quantize_w1(2)
             if b == PACK - 1:
                 for v in range(HALVES):
                     z_out(0, v, 0, PACK)
             if b == PACK:
                 for v in range(HALVES):
                     z_words(0, v)
-                quantize_z(0, 0, HALVES)
-            if b in W2_AFTER:
-                s = W2_AFTER.index(b)
-                for n in (0, 1):
-                    group_w2(s, n * HALF, (n + 1) * HALF)
-                quantize_w2(s)
+            if b == 5:
+                for n in range(M_TILES):
+                    group_w2(0, n * P, (n + 1) * P)
             if b == 6:
+                for n in range(M_TILES):
+                    group_w2(1, n * P, (n + 1) * P)
                 for v in range(HALVES):
                     z_out(LAST, v, 0, PACK - 1)
-                for m in range(M_TILES):
-                    out_acc[m] = psum.tile([P, S], F32, name="out_acc", tag="bank")
-                    out_pass(0, m, 0)
-        finish_half(1)
+
+        quantize_w2(0)
+        z_codes[0] = keep.tile([P, V], U32, name="z_codes0", tag="gate1", align_bytes=64)
+        quantize_z(0, 0, HALVES)
+        for m in range(M_TILES):
+            out_acc[m] = psum.tile([P, S], F32, name="out_acc", tag=f"z_ps{m % HALVES}", bufs=2)
+            out_pass(0, m)
+        quantize_w2(1)
+        z_codes[LAST] = keep.tile([P, V], U32, name="z_codes1", align_bytes=64)
+        for v in range(HALVES):
+            quantize_z(LAST, v, v + 1)
+        for m in range(M_TILES):
+            out_pass(LAST, m)
+            copy = (nc.scalar.copy, nc.vector.tensor_copy)[m % 2]
+            copy(out=result[m][:], in_=out_acc[m][:, :V])
+            nc.sync.dma_start(out=out[m * P : (m + 1) * P, :], in_=result[m][:])

@@ -33,7 +33,7 @@ def tile_picked_sage_relu_e_kernel(
         keep = ctx.enter_context(tc.tile_pool(name="keep", bufs=1))
         hpool = ctx.enter_context(tc.tile_pool(name="hpool", bufs=4))
         prods = ctx.enter_context(tc.tile_pool(name="prods", bufs=12))
-        psum = ctx.enter_context(tc.psum_pool(name="psum", bufs=4))
+        psum = ctx.enter_context(tc.psum_pool(name="psum", bufs=3))
 
         offs_sb = lists.tile([P, S // 16], U16, name="offs_sb")
         pos_sb = [lists.tile([P, V // 16], U16, name=f"pos_sb{d}") for d in range(D)]
@@ -46,9 +46,17 @@ def tile_picked_sage_relu_e_kernel(
         nc.scalar.activation(warm_out[:], warm[:], RELU)
 
         x_raw = [[keep.tile([P, T], F32, name=f"x_raw{s}_{j}") for j in range(PACK)] for s in range(PASSES)]
-        w1_raw = [keep.tile([P, PASSES, PACK, n * P], F32, name=f"w1_raw{c}") for c, n in enumerate(W1_LOADS)]
+        w1_raw = [
+            [
+                keep.tile([P, PACK, n * P], F32, name=f"w1_raw{c}_{s}", tag=f"w1_turn{c}_{s}", align_bytes=64)
+                for s in range(PASSES)
+            ]
+            for c, n in enumerate(W1_LOADS)
+        ]
+        w2_loads = [(0, 0, N), (1, 0, N // 2), (1, N // 2, N)]
         w2_raw = [
-            keep.tile([P, PACK, N], F32, name=f"w2_raw{s}", tag=f"w2_turn{s}", align_bytes=64) for s in range(PASSES)
+            keep.tile([P, PACK, n1 - n0], F32, name=f"w2_raw{c}", tag=f"w2_turn{c}", align_bytes=64)
+            for c, (s, n0, n1) in enumerate(w2_loads)
         ]
         gate_rows = keep.tile([P, P], F32, name="gate_rows")
         nc.gpsimd.memset(gate_rows[:], 0.0)
@@ -63,7 +71,7 @@ def tile_picked_sage_relu_e_kernel(
         def load_w1(c, s):
             first = sum(W1_LOADS[:c]) * P
             block = w1[s * K_PASS : (s + 1) * K_PASS, first : first + W1_LOADS[c] * P]
-            nc.sync.dma_start(out=w1_raw[c][:, s], in_=block.rearrange("(p j) m -> p j m", j=PACK))
+            nc.sync.dma_start(out=w1_raw[c][s][:], in_=block.rearrange("(p j) m -> p j m", j=PACK))
 
         nc.sync.dma_start(offs_sb[:], offs)
         for s in range(PASSES):
@@ -81,9 +89,9 @@ def tile_picked_sage_relu_e_kernel(
         for c in range(len(W1_LOADS)):
             for s in range(PASSES):
                 load_w1(c, s)
-        for s in range(PASSES):
+        for c, (s, n0, n1) in enumerate(w2_loads):
             nc.sync.dma_start(
-                out=w2_raw[s][:], in_=w2[s * K_PASS : (s + 1) * K_PASS, :].rearrange("(p j) n -> p j n", j=PACK)
+                out=w2_raw[c][:], in_=w2[s * K_PASS : (s + 1) * K_PASS, n0:n1].rearrange("(p j) n -> p j n", j=PACK)
             )
 
         w1_grp = [
@@ -100,7 +108,7 @@ def tile_picked_sage_relu_e_kernel(
             c, i = home[b]
             nc.scalar.copy(
                 out=w1_grp[b][:, s].rearrange("p (c i) j -> p c j i", i=4),
-                in_=w1_raw[c][:, s, :, i * P : (i + 1) * P].rearrange("p j (c i) -> p c j i", i=4),
+                in_=w1_raw[c][s][:, :, i * P : (i + 1) * P].rearrange("p j (c i) -> p c j i", i=4),
             )
 
         def quantize_w1(b):
@@ -118,9 +126,11 @@ def tile_picked_sage_relu_e_kernel(
             )
 
         def group_w2(s, n0, n1):
+            c = max(i for i, load in enumerate(w2_loads) if load[:2] <= (s, n0))
+            first = w2_loads[c][1]
             nc.scalar.copy(
                 out=w2_grp[s][:, n0:n1, :].rearrange("p (c i) j -> p c j i", i=4),
-                in_=w2_raw[s][:, :, n0:n1].rearrange("p j (c i) -> p c j i", i=4),
+                in_=w2_raw[c][:, :, n0 - first : n1 - first].rearrange("p j (c i) -> p c j i", i=4),
             )
 
         def quantize_w2(s):
@@ -169,14 +179,19 @@ def tile_picked_sage_relu_e_kernel(
                     in_=x_grp[s][:, cols, :].rearrange("p t j -> p (t j)"),
                 )
 
+        held = {5: f"w1_turn{len(W1_LOADS) - 1}_1", 6: "w2_turn0", 7: "w2_turn1"}
+
         def project(b):
-            if b == BLOCKS - 1:
-                h = keep.tile([P, S], F32, name="h_turn", tag="w2_turn0", align_bytes=64)
+            if b in held:
+                h = keep.tile([P, S], F32, name="h_turn", tag=held[b], align_bytes=64)
             else:
                 h = hpool.tile([P, S], F32, name="h")
             width = HALF if b == 0 else S
             for t in range(S // width):
-                acc = psum.tile([P, S], F32, name="acc", tag="bank")
+                if b == BLOCKS - 1:
+                    acc = psum.tile([P, S], F32, name="acc", tag="last", bufs=1)
+                else:
+                    acc = psum.tile([P, S], F32, name="acc", tag="bank")
                 nodes = slice(t * width, (t + 1) * width)
                 for s in range(PASSES):
                     nc.tensor.matmul_mx(
@@ -214,8 +229,6 @@ def tile_picked_sage_relu_e_kernel(
             for d in range(D):
                 if d == 1 and b < 2:
                     prod = keep.tile([P, V], F32, name="prod_turn", tag=f"turn{b + 1}", align_bytes=64)
-                elif d == 3 and b > 0 and b + 2 < BLOCKS:
-                    prod = keep.tile([P, V], F32, name="prod_turn", tag=f"turn{b + 2}", align_bytes=64)
                 else:
                     prod = prods.tile([P, V], F32, name="prod")
                 nc.vector.tensor_tensor(prod[:], h[:].indirect(pos_sb[d][:]), gate_sb[d][:], MULT)
@@ -233,26 +246,28 @@ def tile_picked_sage_relu_e_kernel(
                 )
                 add_transposed(b, d, v, prod[:])
 
-        def z_out(s, v, b0, b1):
-            if (s, v) not in z_t:
-                tag = "w2_turn1" if (s, v) == (LAST, 0) else f"z_t{s}_{v}"
-                z_t[s, v] = keep.tile([P, 2, P, 2], BF16, name=f"z_t{s}_{v}", tag=tag, align_bytes=64)
+        def z_out(banks, s, v, b0, b1):
+            if s not in z_t:
+                tag = "w2_turn2" if s == LAST else f"w1_turn{len(W1_LOADS) - 1}_0"
+                z_t[s] = keep.tile([P, HALVES * K_PASS], BF16, name=f"z_t{s}", tag=tag, align_bytes=64)
+            half = z_t[s][:, v * K_PASS : (v + 1) * K_PASS].rearrange("v (u p e) -> v u p e", u=2, e=2)
             nc.scalar.copy(
-                out=z_t[s, v][:, :, b0 * 32 : b1 * 32, :],
-                in_=z_ps[v][:, b0 * P : b1 * P].rearrange("v (p u e) -> v u p e", u=2, e=2),
+                out=half[:, :, b0 * 32 : b1 * 32, :],
+                in_=banks[v][:, b0 * P : b1 * P].rearrange("v (p u e) -> v u p e", u=2, e=2),
             )
 
-        def z_words(s, v):
+        def z_words(s, v0, v1):
             if s == LAST:
-                words = psum.tile([P, 2, P], F32, name="words", tag=f"z_ps{v}", bufs=2)
+                words = psum.tile([P, v1 - v0, 2, P], F32, name="words", tag=f"z_ps{v0}", bufs=2)
             else:
-                words = psum.tile([P, 2, P], F32, name="words", tag="bank")
-            for u in range(2):
-                zw = z_t[s, v][:, u].rearrange("v p e -> v (p e)").bitcast(F32)
-                nc.tensor.transpose(words[:, u, :], zw, ident[:])
+                words = psum.tile([P, v1 - v0, 2, P], F32, name="words", tag="last", bufs=1)
+            for v in range(v0, v1):
+                for u in range(2):
+                    zw = z_t[s][:, (2 * v + u) * 2 * P : (2 * v + u + 1) * 2 * P].bitcast(F32)
+                    nc.tensor.transpose(words[:, v - v0, u, :], zw, ident[:])
             nc.scalar.copy(
-                out=z_grp[s][:, v * K_PASS : (v + 1) * K_PASS].bitcast(F32).rearrange("p (n u) -> p n u", u=2),
-                in_=words[:].rearrange("p u n -> p n u"),
+                out=z_grp[s][:, v0 * K_PASS : v1 * K_PASS].bitcast(F32).rearrange("p (v n u) -> p v n u", n=P, u=2),
+                in_=words[:].rearrange("p v u n -> p v n u"),
             )
 
         def quantize_z(s, v0, v1):
@@ -278,44 +293,45 @@ def tile_picked_sage_relu_e_kernel(
         M_TILES = N // P
         result = [keep.tile([P, V], F32, name=f"result{m}") for m in range(M_TILES)]
 
+        def group_block(b):
+            for s in range(PASSES):
+                group_w1(b, s)
+
+        def group_w2_pass(s):
+            for n in range(M_TILES):
+                group_w2(s, n * P, (n + 1) * P)
+
+        grouped_in = {0: (2,), 1: (3,), 2: (4,), 3: (5, 6), 4: (7,)}
         h_next = project(0)
-        for s in range(PASSES):
-            group_w1(1, s)
+        group_block(1)
         quantize_w1(1)
         for b in range(BLOCKS):
+            if b == PACK:
+                z_first = z_ps
             if b % PACK == 0:
                 z_ps = [psum.tile([P, K_PASS], F32, name=f"z_ps{v}", tag=f"z_ps{v}", bufs=2) for v in range(HALVES)]
             h = h_next
-            if b + 2 < BLOCKS:
-                for s in range(PASSES):
-                    group_w1(b + 2, s)
-            if b + 1 < BLOCKS:
-                h_next = project(b + 1)
-            if b + 2 < BLOCKS and b > 0:
-                quantize_w1(b + 2)
-            if b == BLOCKS - 1:
-                for v in range(HALVES):
-                    gather_half(b, h, v)
-                    z_out(LAST, v, PACK - 1, PACK)
-                    z_words(LAST, v)
-            else:
-                gather_block(b, h)
-            if b == 0:
-                quantize_w1(2)
-            if b == PACK - 1:
-                for v in range(HALVES):
-                    z_out(0, v, 0, PACK)
+            for c in grouped_in.get(b, ()):
+                group_block(c)
             if b == PACK:
                 for v in range(HALVES):
-                    z_words(0, v)
-            if b == 5:
-                for n in range(M_TILES):
-                    group_w2(0, n * P, (n + 1) * P)
-            if b == 6:
-                for n in range(M_TILES):
-                    group_w2(1, n * P, (n + 1) * P)
+                    z_out(z_first, 0, v, 0, PACK)
+            if b in (5, 6):
+                group_w2_pass(b - 5)
+            if b + 1 < BLOCKS:
+                h_next = project(b + 1)
+            if b == BLOCKS - 1:
                 for v in range(HALVES):
-                    z_out(LAST, v, 0, PACK - 1)
+                    z_out(z_ps, LAST, v, 0, PACK - 1)
+                z_words(0, 0, HALVES)
+                for v in range(HALVES):
+                    gather_half(b, h, v)
+                    z_out(z_ps, LAST, v, PACK - 1, PACK)
+                    z_words(LAST, v, v + 1)
+            else:
+                gather_block(b, h)
+            for c in grouped_in.get(b, ()):
+                quantize_w1(c)
 
         quantize_w2(0)
         z_codes[0] = keep.tile([P, V], U32, name="z_codes0", tag="gate1", align_bytes=64)

@@ -31,7 +31,6 @@ def tile_picked_sage_relu_e_kernel(
     with ExitStack() as ctx:
         lists = ctx.enter_context(tc.tile_pool(name="lists", bufs=1))
         keep = ctx.enter_context(tc.tile_pool(name="keep", bufs=1))
-        hpool = ctx.enter_context(tc.tile_pool(name="hpool", bufs=4))
         prods = ctx.enter_context(tc.tile_pool(name="prods", bufs=12))
         psum = ctx.enter_context(tc.psum_pool(name="psum", bufs=3))
 
@@ -53,14 +52,14 @@ def tile_picked_sage_relu_e_kernel(
             ]
             for c, n in enumerate(W1_LOADS)
         ]
-        w2_loads = [(0, 0, N), (1, 0, N // 2), (1, N // 2, N)]
+        w2_loads = [(s, n0, n0 + N // 2) for s in range(PASSES) for n0 in (0, N // 2)]
         w2_raw = [
             keep.tile([P, PACK, n1 - n0], F32, name=f"w2_raw{c}", tag=f"w2_turn{c}", align_bytes=64)
             for c, (s, n0, n1) in enumerate(w2_loads)
         ]
-        gate_rows = keep.tile([P, P], F32, name="gate_rows")
+        gate_rows = keep.tile([P, V], F32, name="gate_rows")
         nc.gpsimd.memset(gate_rows[:], 0.0)
-        gate_cols = keep.tile([P, D * HALVES], F32, name="gate_cols")
+        gate_cols = keep.tile([P, HALVES, D], F32, name="gate_cols")
         gate_sb = [keep.tile([P, V], F32, name=f"gate_sb{d}", tag=f"gate{d}", align_bytes=64) for d in range(D)]
         home = [(c, i) for c, n in enumerate(W1_LOADS) for i in range(n)]
 
@@ -73,29 +72,26 @@ def tile_picked_sage_relu_e_kernel(
             block = w1[s * K_PASS : (s + 1) * K_PASS, first : first + W1_LOADS[c] * P]
             nc.sync.dma_start(out=w1_raw[c][s][:], in_=block.rearrange("(p j) m -> p j m", j=PACK))
 
-        nc.sync.dma_start(offs_sb[:], offs)
+        lists_after = {0: (0,), 1: (1, 2, 3)}
         for s in range(PASSES):
             for j in range(PACK):
                 load_x(s, j)
+                if (s, j) == (0, 0):
+                    nc.sync.dma_start(offs_sb[:], offs)
                 if (s, j) == (0, 1):
-                    for d in range(D):
-                        nc.sync.dma_start(
-                            out=gate_rows[HALVES * d : HALVES * (d + 1), :],
-                            in_=gate[d, 0, :].rearrange("(v n) -> v n", v=HALVES),
-                        )
-                if (s, j) == (0, 3):
-                    for d, pos in enumerate((pos1, pos2, pos3, pos4)):
-                        nc.sync.dma_start(pos_sb[d][:], pos)
+                    nc.sync.dma_start(out=gate_rows[:D, :], in_=gate[:, 0, :])
         for c in range(len(W1_LOADS)):
             for s in range(PASSES):
                 load_w1(c, s)
+            for d in lists_after.get(c, ()):
+                nc.sync.dma_start(pos_sb[d][:], (pos1, pos2, pos3, pos4)[d])
         for c, (s, n0, n1) in enumerate(w2_loads):
             nc.sync.dma_start(
                 out=w2_raw[c][:], in_=w2[s * K_PASS : (s + 1) * K_PASS, n0:n1].rearrange("(p j) n -> p j n", j=PACK)
             )
 
         w1_grp = [
-            keep.tile([P, PASSES, P, PACK], BF16, name=f"w1_grp{b}", tag=f"turn{b}", align_bytes=64)
+            keep.tile([P, PASSES, P, PACK], BF16, name=f"w1_grp{b}", align_bytes=64)
             for b in range(BLOCKS)
         ]
         w1_codes = [keep.tile([P, PASSES, P], U32, name=f"w1_codes{b}", align_bytes=64) for b in range(BLOCKS)]
@@ -141,21 +137,24 @@ def tile_picked_sage_relu_e_kernel(
                 in_=w2_grp[s][:].rearrange("p n j -> p (n j)"),
             )
 
-        spread = psum.tile([P, P], F32, name="spread", tag="bank")
-        nc.tensor.transpose(spread[:], gate_rows[:], ident[:])
-        nc.scalar.copy(out=gate_cols[:], in_=spread[:, : D * HALVES])
+        spread = psum.tile([P, HALVES, P], F32, name="spread", tag="bank")
+        for v in range(HALVES):
+            nc.tensor.transpose(spread[:, v, :], gate_rows[:, v * P : (v + 1) * P], ident[:])
+        nc.scalar.copy(out=gate_cols[:], in_=spread[:, :, :D])
         for g in range(D // 2):
             spread = psum.tile([P, 2 * V], F32, name="spread", tag="bank")
             for r in range(2 * HALVES):
-                column = gate_cols[:, 2 * HALVES * g + r : 2 * HALVES * g + r + 1]
+                d, v = 2 * g + r // HALVES, r % HALVES
+                column = gate_cols[:, v, d : d + 1]
                 nc.tensor.transpose(spread[:, r * P : (r + 1) * P], column.to_broadcast([P, P]), ident[:])
             for r in range(2):
                 nc.scalar.copy(out=gate_sb[2 * g + r][:], in_=spread[:, r * V : (r + 1) * V])
 
         x_grp = [keep.tile([P, S, PACK], BF16, name=f"x_grp{s}", align_bytes=64) for s in range(PASSES)]
         x_codes = [keep.tile([P, S], U32, name=f"x_codes{s}", align_bytes=64) for s in range(PASSES)]
-        x_scales = [keep.tile([P, S], U8, name=f"x_scales{s}", align_bytes=64) for s in range(PASSES)]
+        x_scales = [keep.tile([P, S], U8, name="x_scales0", align_bytes=64)]
         HALF = S // 2
+        PIECES = (slice(0, HALF), slice(HALF, HALF + P), slice(HALF + P, S))
         for s in range(PASSES):
             last = s == PASSES - 1
             for j in range(PACK):
@@ -171,28 +170,25 @@ def tile_picked_sage_relu_e_kernel(
                     quantize_w1_pass(0, 1)
                 else:
                     nc.vector.tensor_copy(x_grp[s][:, :, j], x_raw[s][j][:].indirect(offs_sb[:]))
-            for t in (0, 1) if last else (None,):
-                cols = slice(0, S) if t is None else slice(t * HALF, (t + 1) * HALF)
+            if last:
+                x_scales.append(keep.tile([P, S], U8, name="x_scales1", tag="w1_turn0_0", align_bytes=64))
+            for cols in PIECES if last else (slice(0, S),):
                 nc.vector.quantize_mx(
                     out=x_codes[s][:, cols].bitcast(FP8X4),
                     scales=x_scales[s][:, cols],
                     in_=x_grp[s][:, cols, :].rearrange("p t j -> p (t j)"),
                 )
 
-        held = {5: f"w1_turn{len(W1_LOADS) - 1}_1", 6: "w2_turn0", 7: "w2_turn1"}
+        held = [f"w1_turn{c}_1" for c in range(1, len(W1_LOADS))] + [f"w2_turn{c}" for c in range(3)]
 
         def project(b):
-            if b in held:
-                h = keep.tile([P, S], F32, name="h_turn", tag=held[b], align_bytes=64)
-            else:
-                h = hpool.tile([P, S], F32, name="h")
-            width = HALF if b == 0 else S
-            for t in range(S // width):
+            h = keep.tile([P, S], F32, name="h_turn", tag=held[b], align_bytes=64)
+            for nodes in PIECES if b == 0 else (slice(0, S),):
+                width = nodes.stop - nodes.start
                 if b == BLOCKS - 1:
                     acc = psum.tile([P, S], F32, name="acc", tag="last", bufs=1)
                 else:
                     acc = psum.tile([P, S], F32, name="acc", tag="bank")
-                nodes = slice(t * width, (t + 1) * width)
                 for s in range(PASSES):
                     nc.tensor.matmul_mx(
                         out=acc[:, :width],
@@ -203,13 +199,13 @@ def tile_picked_sage_relu_e_kernel(
                         start=(s == 0),
                         stop=(s == PASSES - 1),
                     )
-                if b > 0:
+                if nodes.start == 0:
                     nc.scalar.activation(h[:, nodes], acc[:, :width], RELU)
                 else:
                     nc.vector.tensor_relu(h[:, nodes], acc[:, :width])
             return h
 
-        z_t = {}
+        z_t = []
         z_grp = [keep.tile([P, V * PACK], BF16, name=f"z_grp{s}", align_bytes=64) for s in range(PASSES)]
         z_codes = {}
         z_scales = [keep.tile([P, V], U8, name=f"z_scales{s}", align_bytes=64) for s in range(PASSES)]
@@ -227,10 +223,7 @@ def tile_picked_sage_relu_e_kernel(
 
         def gather_block(b, h):
             for d in range(D):
-                if d == 1 and b < 2:
-                    prod = keep.tile([P, V], F32, name="prod_turn", tag=f"turn{b + 1}", align_bytes=64)
-                else:
-                    prod = prods.tile([P, V], F32, name="prod")
+                prod = prods.tile([P, V], F32, name="prod")
                 nc.vector.tensor_tensor(prod[:], h[:].indirect(pos_sb[d][:]), gate_sb[d][:], MULT)
                 for v in range(HALVES):
                     add_transposed(b, d, v, prod[:, v * P : (v + 1) * P])
@@ -247,10 +240,10 @@ def tile_picked_sage_relu_e_kernel(
                 add_transposed(b, d, v, prod[:])
 
         def z_out(banks, s, v, b0, b1):
-            if s not in z_t:
-                tag = "w2_turn2" if s == LAST else f"w1_turn{len(W1_LOADS) - 1}_0"
-                z_t[s] = keep.tile([P, HALVES * K_PASS], BF16, name=f"z_t{s}", tag=tag, align_bytes=64)
-            half = z_t[s][:, v * K_PASS : (v + 1) * K_PASS].rearrange("v (u p e) -> v u p e", u=2, e=2)
+            if not z_t:
+                z_t.append(keep.tile([P, PASSES * HALVES * K_PASS], BF16, name="z_t", tag="w2_turn3", align_bytes=64))
+            first = (s * HALVES + v) * K_PASS
+            half = z_t[0][:, first : first + K_PASS].rearrange("v (u p e) -> v u p e", u=2, e=2)
             nc.scalar.copy(
                 out=half[:, :, b0 * 32 : b1 * 32, :],
                 in_=banks[v][:, b0 * P : b1 * P].rearrange("v (p u e) -> v u p e", u=2, e=2),
@@ -263,7 +256,8 @@ def tile_picked_sage_relu_e_kernel(
                 words = psum.tile([P, v1 - v0, 2, P], F32, name="words", tag="last", bufs=1)
             for v in range(v0, v1):
                 for u in range(2):
-                    zw = z_t[s][:, (2 * v + u) * 2 * P : (2 * v + u + 1) * 2 * P].bitcast(F32)
+                    first = ((s * HALVES + v) * 2 + u) * 2 * P
+                    zw = z_t[0][:, first : first + 2 * P].bitcast(F32)
                     nc.tensor.transpose(words[:, v - v0, u, :], zw, ident[:])
             nc.scalar.copy(
                 out=z_grp[s][:, v0 * K_PASS : v1 * K_PASS].bitcast(F32).rearrange("p (v n u) -> p v n u", n=P, u=2),
@@ -297,14 +291,15 @@ def tile_picked_sage_relu_e_kernel(
             for s in range(PASSES):
                 group_w1(b, s)
 
-        def group_w2_pass(s):
-            for n in range(M_TILES):
-                group_w2(s, n * P, (n + 1) * P)
+        def group_w2_load(c):
+            s, n0, n1 = w2_loads[c]
+            for n in range(n0, n1, P):
+                group_w2(s, n, n + P)
 
-        grouped_in = {0: (2,), 1: (3,), 2: (4,), 3: (5, 6), 4: (7,)}
-        h_next = project(0)
+        grouped_in = {0: (2,), 1: (3,), 2: (4, 5), 3: (6, 7)}
         group_block(1)
         quantize_w1(1)
+        h_next = project(0)
         for b in range(BLOCKS):
             if b == PACK:
                 z_first = z_ps
@@ -313,14 +308,14 @@ def tile_picked_sage_relu_e_kernel(
             h = h_next
             for c in grouped_in.get(b, ()):
                 group_block(c)
-            if b == PACK:
-                for v in range(HALVES):
-                    z_out(z_first, 0, v, 0, PACK)
-            if b in (5, 6):
-                group_w2_pass(b - 5)
+            if b in (4, 5, 6):
+                group_w2_load(b - 4)
             if b + 1 < BLOCKS:
                 h_next = project(b + 1)
             if b == BLOCKS - 1:
+                group_w2_load(3)
+                for v in range(HALVES):
+                    z_out(z_first, 0, v, 0, PACK)
                 for v in range(HALVES):
                     z_out(z_ps, LAST, v, 0, PACK - 1)
                 z_words(0, 0, HALVES)

@@ -271,21 +271,21 @@ def tile_picked_sage_relu_e_kernel(
                 in_=z_grp[s][:, v0 * K_PASS : v1 * K_PASS],
             )
 
-        def out_pass(s, m):
+        def out_pass(acc, s, m, v, start):
             cols = slice(m * P, (m + 1) * P)
+            nodes = slice(v * P, (v + 1) * P)
             nc.tensor.matmul_mx(
-                out=out_acc[m][:, :V],
+                out=acc,
                 lhsT=w2_codes[s][:, cols].bitcast(FP8X4),
                 lhsT_scale=w2_scales[s][:, cols],
-                rhs=z_codes[s][:].bitcast(FP8X4),
-                rhs_scale=z_scales[s][:],
-                start=(s == 0),
-                stop=(s == PASSES - 1),
+                rhs=z_codes[s][:, nodes].bitcast(FP8X4),
+                rhs_scale=z_scales[s][:, nodes],
+                start=start,
+                stop=not start,
             )
 
         LAST = PASSES - 1
         M_TILES = N // P
-        result = [keep.tile([P, V], F32, name=f"result{m}") for m in range(M_TILES)]
 
         def group_block(b):
             for s in range(PASSES):
@@ -332,14 +332,25 @@ def tile_picked_sage_relu_e_kernel(
         z_codes[0] = keep.tile([P, V], U32, name="z_codes0", tag="gate1", align_bytes=64)
         quantize_z(0, 0, HALVES)
         for m in range(M_TILES):
-            out_acc[m] = psum.tile([P, S], F32, name="out_acc", tag=f"z_ps{m % HALVES}", bufs=2)
-            out_pass(0, m)
+            out_acc[m] = psum.tile([P, P], F32, name="out_acc", tag=f"z_ps{m % HALVES}", bufs=2)
+            out_pass(out_acc[m][:], 0, m, 1, True)
         quantize_w2(1)
         z_codes[LAST] = keep.tile([P, V], U32, name="z_codes1", align_bytes=64)
         for v in range(HALVES):
             quantize_z(LAST, v, v + 1)
+        out_rows = out.rearrange("(m p) v -> p m v", p=P)
+        for pair in range(M_TILES // 2):
+            acc = psum.tile([P, 2, P], F32, name="acc", tag="bank")
+            for i in range(2):
+                out_pass(acc[:, i, :], LAST, 2 * pair + i, 0, True)
+                out_pass(acc[:, i, :], 0, 2 * pair + i, 0, False)
+            result = keep.tile([P, 2, P], F32, name=f"result0_{pair}")
+            copy = (nc.scalar.copy, nc.vector.tensor_copy)[pair]
+            copy(out=result[:], in_=acc[:])
+            nc.sync.dma_start(out=out_rows[:, 2 * pair : 2 * pair + 2, :P], in_=result[:])
         for m in range(M_TILES):
-            out_pass(LAST, m)
-            copy = (nc.scalar.copy, nc.vector.tensor_copy)[m % 2]
-            copy(out=result[m][:], in_=out_acc[m][:, :V])
-            nc.sync.dma_start(out=out[m * P : (m + 1) * P, :], in_=result[m][:])
+            out_pass(out_acc[m][:], LAST, m, 1, False)
+            result = keep.tile([P, P], F32, name=f"result1_{m}")
+            copy = (nc.vector.tensor_copy, nc.scalar.copy)[m % 2]
+            copy(out=result[:], in_=out_acc[m][:])
+            nc.sync.dma_start(out=out_rows[:, m, P:], in_=result[:])

@@ -21,7 +21,7 @@ FP8X4 = mybir.dt.float8_e4m3fn_x4
 RELU = mybir.ActivationFunctionType.Relu
 MULT = mybir.AluOpType.mult
 
-W1_LOADS = (1, 1, 1, 1, 2, 2)
+W1_LOADS = (1,) * BLOCKS
 
 
 def tile_picked_sage_relu_e_kernel(
@@ -52,7 +52,7 @@ def tile_picked_sage_relu_e_kernel(
             ]
             for c, n in enumerate(W1_LOADS)
         ]
-        w2_loads = [(s, n0, n0 + N // 2) for s in range(PASSES) for n0 in (0, N // 2)]
+        w2_loads = [(0, 0, 2 * P), (0, 2 * P, N), (1, 0, P), (1, P, 2 * P), (1, 2 * P, N)]
         w2_raw = [
             keep.tile([P, PACK, n1 - n0], F32, name=f"w2_raw{c}", tag=f"w2_turn{c}", align_bytes=64)
             for c, (s, n0, n1) in enumerate(w2_loads)
@@ -96,7 +96,7 @@ def tile_picked_sage_relu_e_kernel(
         ]
         w1_codes = [keep.tile([P, PASSES, P], U32, name=f"w1_codes{b}", align_bytes=64) for b in range(BLOCKS)]
         w1_scales = [keep.tile([P, PASSES, P], U8, name=f"w1_scales{b}", align_bytes=64) for b in range(BLOCKS)]
-        w2_grp = [keep.tile([P, N, PACK], BF16, name=f"w2_grp{s}", align_bytes=64) for s in range(PASSES)]
+        w2_grp = [keep.tile([P, N // (s + 1), PACK], BF16, name=f"w2_grp{s}", align_bytes=64) for s in range(PASSES)]
         w2_codes = {}
         w2_scales = [keep.tile([P, N], U8, name=f"w2_scales{s}", align_bytes=64) for s in range(PASSES)]
 
@@ -129,12 +129,13 @@ def tile_picked_sage_relu_e_kernel(
                 in_=w2_raw[c][:, :, n0 - first : n1 - first].rearrange("p j (c i) -> p c j i", i=4),
             )
 
-        def quantize_w2(s):
-            w2_codes[s] = keep.tile([P, N], U32, name=f"w2_codes{s}", tag=f"gate{2 * s}", align_bytes=64)
+        def quantize_w2(s, n0, n1, grouped):
+            if n0 == 0:
+                w2_codes[s] = keep.tile([P, N], U32, name=f"w2_codes{s}", tag=f"gate{2 * s}", align_bytes=64)
             nc.vector.quantize_mx(
-                out=w2_codes[s][:].bitcast(FP8X4),
-                scales=w2_scales[s][:],
-                in_=w2_grp[s][:].rearrange("p n j -> p (n j)"),
+                out=w2_codes[s][:, n0:n1].bitcast(FP8X4),
+                scales=w2_scales[s][:, n0:n1],
+                in_=grouped[:].rearrange("p n j -> p (n j)"),
             )
 
         spread = psum.tile([P, HALVES, P], F32, name="spread", tag="bank")
@@ -179,7 +180,7 @@ def tile_picked_sage_relu_e_kernel(
                     in_=x_grp[s][:, cols, :].rearrange("p t j -> p (t j)"),
                 )
 
-        held = [f"w1_turn{c}_1" for c in range(1, len(W1_LOADS))] + [f"w2_turn{c}" for c in range(3)]
+        held = [f"w1_turn{c}_1" for c in (1, 2, 4, 5, 6)] + [f"w2_turn{c}" for c in range(3)]
 
         def project(b):
             h = keep.tile([P, S], F32, name="h_turn", tag=held[b], align_bytes=64)
@@ -251,7 +252,7 @@ def tile_picked_sage_relu_e_kernel(
 
         def z_words(s, v0, v1):
             if s == LAST:
-                words = psum.tile([P, v1 - v0, 2, P], F32, name="words", tag=f"z_ps{v0}", bufs=2)
+                words = psum.tile([P, v1 - v0, 2, P], F32, name="words", tag=f"z_ps0_{v0}", bufs=1)
             else:
                 words = psum.tile([P, v1 - v0, 2, P], F32, name="words", tag="last", bufs=1)
             for v in range(v0, v1):
@@ -296,7 +297,7 @@ def tile_picked_sage_relu_e_kernel(
             for n in range(n0, n1, P):
                 group_w2(s, n, n + P)
 
-        grouped_in = {0: (2,), 1: (3,), 2: (4, 5), 3: (6, 7)}
+        grouped_in = {0: (2,), 1: (3, 4), 2: (5,), 3: (6,), 4: (7,)}
         group_block(1)
         quantize_w1(1)
         h_next = project(0)
@@ -304,7 +305,9 @@ def tile_picked_sage_relu_e_kernel(
             if b == PACK:
                 z_first = z_ps
             if b % PACK == 0:
-                z_ps = [psum.tile([P, K_PASS], F32, name=f"z_ps{v}", tag=f"z_ps{v}", bufs=2) for v in range(HALVES)]
+                z_ps = [
+                    psum.tile([P, K_PASS], F32, name="z_ps", tag=f"z_ps{b // PACK}_{v}", bufs=1) for v in range(HALVES)
+                ]
             h = h_next
             for c in grouped_in.get(b, ()):
                 group_block(c)
@@ -328,13 +331,20 @@ def tile_picked_sage_relu_e_kernel(
             for c in grouped_in.get(b, ()):
                 quantize_w1(c)
 
-        quantize_w2(0)
+        quantize_w2(0, 0, N, w2_grp[0])
         z_codes[0] = keep.tile([P, V], U32, name="z_codes0", tag="gate1", align_bytes=64)
         quantize_z(0, 0, HALVES)
-        for m in range(M_TILES):
-            out_acc[m] = psum.tile([P, P], F32, name="out_acc", tag=f"z_ps{m % HALVES}", bufs=2)
+        w2_late = keep.tile([P, N // 2, PACK], BF16, name="w2_late", tag="gate3", align_bytes=64)
+        nc.vector.tensor_copy(
+            out=w2_late[:].rearrange("p (c i) j -> p c j i", i=4),
+            in_=w2_raw[-1][:].rearrange("p j (c i) -> p c j i", i=4),
+        )
+        early = ("z_ps1_1", "z_ps0_0", "z_ps0_1")
+        for m, tag in enumerate(early):
+            out_acc[m] = psum.tile([P, P], F32, name="out_acc", tag=tag, bufs=1)
             out_pass(out_acc[m][:], 0, m, 1, True)
-        quantize_w2(1)
+        quantize_w2(1, 0, N // 2, w2_grp[1])
+        quantize_w2(1, N // 2, N, w2_late)
         z_codes[LAST] = keep.tile([P, V], U32, name="z_codes1", align_bytes=64)
         for v in range(HALVES):
             quantize_z(LAST, v, v + 1)
@@ -349,7 +359,12 @@ def tile_picked_sage_relu_e_kernel(
             copy(out=result[:], in_=acc[:])
             nc.sync.dma_start(out=out_rows[:, 2 * pair : 2 * pair + 2, :P], in_=result[:])
         for m in range(M_TILES):
-            out_pass(out_acc[m][:], LAST, m, 1, False)
+            if m in out_acc:
+                out_pass(out_acc[m][:], LAST, m, 1, False)
+            else:
+                out_acc[m] = psum.tile([P, P], F32, name="out_acc", tag="z_ps1_0", bufs=1)
+                out_pass(out_acc[m][:], LAST, m, 1, True)
+                out_pass(out_acc[m][:], 0, m, 1, False)
             result = keep.tile([P, P], F32, name=f"result1_{m}")
             copy = (nc.vector.tensor_copy, nc.scalar.copy)[m % 2]
             copy(out=result[:], in_=out_acc[m][:])

@@ -52,7 +52,7 @@ def tile_picked_sage_relu_e_kernel(
             ]
             for c, n in enumerate(W1_LOADS)
         ]
-        w2_loads = [(0, 0, 2 * P), (0, 2 * P, N), (1, 0, P), (1, P, 2 * P), (1, 2 * P, N)]
+        w2_loads = [(s, n0, n0 + N // 2) for s in range(PASSES) for n0 in (0, N // 2)]
         w2_raw = [
             keep.tile([P, PACK, n1 - n0], F32, name=f"w2_raw{c}", tag=f"w2_turn{c}", align_bytes=64)
             for c, (s, n0, n1) in enumerate(w2_loads)
@@ -96,7 +96,7 @@ def tile_picked_sage_relu_e_kernel(
         ]
         w1_codes = [keep.tile([P, PASSES, P], U32, name=f"w1_codes{b}", align_bytes=64) for b in range(BLOCKS)]
         w1_scales = [keep.tile([P, PASSES, P], U8, name=f"w1_scales{b}", align_bytes=64) for b in range(BLOCKS)]
-        w2_grp = [keep.tile([P, N // (s + 1), PACK], BF16, name=f"w2_grp{s}", align_bytes=64) for s in range(PASSES)]
+        w2_grp = [keep.tile([P, N, PACK], BF16, name=f"w2_grp{s}", align_bytes=64) for s in range(PASSES)]
         w2_codes = {}
         w2_scales = [keep.tile([P, N], U8, name=f"w2_scales{s}", align_bytes=64) for s in range(PASSES)]
 
@@ -129,13 +129,12 @@ def tile_picked_sage_relu_e_kernel(
                 in_=w2_raw[c][:, :, n0 - first : n1 - first].rearrange("p j (c i) -> p c j i", i=4),
             )
 
-        def quantize_w2(s, n0, n1, grouped):
-            if n0 == 0:
-                w2_codes[s] = keep.tile([P, N], U32, name=f"w2_codes{s}", tag=f"gate{2 * s}", align_bytes=64)
+        def quantize_w2(s):
+            w2_codes[s] = keep.tile([P, N], U32, name=f"w2_codes{s}", tag=f"gate{2 * s}", align_bytes=64)
             nc.vector.quantize_mx(
-                out=w2_codes[s][:, n0:n1].bitcast(FP8X4),
-                scales=w2_scales[s][:, n0:n1],
-                in_=grouped[:].rearrange("p n j -> p (n j)"),
+                out=w2_codes[s][:].bitcast(FP8X4),
+                scales=w2_scales[s][:],
+                in_=w2_grp[s][:].rearrange("p n j -> p (n j)"),
             )
 
         spread = psum.tile([P, HALVES, P], F32, name="spread", tag="bank")
@@ -331,20 +330,14 @@ def tile_picked_sage_relu_e_kernel(
             for c in grouped_in.get(b, ()):
                 quantize_w1(c)
 
-        quantize_w2(0, 0, N, w2_grp[0])
+        quantize_w2(0)
         z_codes[0] = keep.tile([P, V], U32, name="z_codes0", tag="gate1", align_bytes=64)
         quantize_z(0, 0, HALVES)
-        w2_late = keep.tile([P, N // 2, PACK], BF16, name="w2_late", tag="gate3", align_bytes=64)
-        nc.vector.tensor_copy(
-            out=w2_late[:].rearrange("p (c i) j -> p c j i", i=4),
-            in_=w2_raw[-1][:].rearrange("p j (c i) -> p c j i", i=4),
-        )
         early = ("z_ps1_1", "z_ps0_0", "z_ps0_1")
         for m, tag in enumerate(early):
             out_acc[m] = psum.tile([P, P], F32, name="out_acc", tag=tag, bufs=1)
             out_pass(out_acc[m][:], 0, m, 1, True)
-        quantize_w2(1, 0, N // 2, w2_grp[1])
-        quantize_w2(1, N // 2, N, w2_late)
+        quantize_w2(1)
         z_codes[LAST] = keep.tile([P, V], U32, name="z_codes1", align_bytes=64)
         for v in range(HALVES):
             quantize_z(LAST, v, v + 1)

@@ -72,12 +72,13 @@ def tile_picked_sage_relu_e_kernel(
             block = w1[s * K_PASS : (s + 1) * K_PASS, first : first + W1_LOADS[c] * P]
             nc.sync.dma_start(out=w1_raw[c][s][:], in_=block.rearrange("(p j) m -> p j m", j=PACK))
 
-        lists_after = {0: (0,), 1: (1, 2, 3)}
+        lists_after = {1: (1, 2, 3)}
         for s in range(PASSES):
             for j in range(PACK):
                 load_x(s, j)
                 if (s, j) == (0, 0):
                     nc.sync.dma_start(offs_sb[:], offs)
+                    nc.sync.dma_start(pos_sb[0][:], pos1)
                 if (s, j) == (0, 1):
                     nc.sync.dma_start(out=gate_rows[:D, :], in_=gate[:, 0, :])
         for c in range(len(W1_LOADS)):
@@ -179,7 +180,7 @@ def tile_picked_sage_relu_e_kernel(
                     in_=x_grp[s][:, cols, :].rearrange("p t j -> p (t j)"),
                 )
 
-        held = [f"w1_turn{c}_1" for c in (1, 2, 4, 5, 6)] + [f"w2_turn{c}" for c in range(3)]
+        held = ["h0"] + [f"w1_turn{c}_1" for c in (2, 4, 5, 6)] + [f"w2_turn{c}" for c in range(3)]
 
         def project(b):
             h = keep.tile([P, S], F32, name="h_turn", tag=held[b], align_bytes=64)
@@ -199,7 +200,7 @@ def tile_picked_sage_relu_e_kernel(
                         start=(s == 0),
                         stop=(s == PASSES - 1),
                     )
-                if nodes.start == 0:
+                if b > 0:
                     nc.scalar.activation(h[:, nodes], acc[:, :width], RELU)
                 else:
                     nc.vector.tensor_relu(h[:, nodes], acc[:, :width])
@@ -223,7 +224,10 @@ def tile_picked_sage_relu_e_kernel(
 
         def gather_block(b, h):
             for d in range(D):
-                prod = prods.tile([P, V], F32, name="prod")
+                if (b, d) == (0, 1):
+                    prod = keep.tile([P, V], F32, name="prod_held", tag="w1_turn1_1", align_bytes=64)
+                else:
+                    prod = prods.tile([P, V], F32, name="prod")
                 nc.vector.tensor_tensor(prod[:], h[:].indirect(pos_sb[d][:]), gate_sb[d][:], MULT)
                 for v in range(HALVES):
                     add_transposed(b, d, v, prod[:, v * P : (v + 1) * P])
@@ -297,9 +301,9 @@ def tile_picked_sage_relu_e_kernel(
                 group_w2(s, n, n + P)
 
         grouped_in = {0: (2,), 1: (3, 4), 2: (5,), 3: (6,), 4: (7,)}
+        h_next = project(0)
         group_block(1)
         quantize_w1(1)
-        h_next = project(0)
         for b in range(BLOCKS):
             if b == PACK:
                 z_first = z_ps

@@ -31,7 +31,7 @@ def tile_picked_sage_relu_e_kernel(
     with ExitStack() as ctx:
         lists = ctx.enter_context(tc.tile_pool(name="lists", bufs=1))
         keep = ctx.enter_context(tc.tile_pool(name="keep", bufs=1))
-        prods = ctx.enter_context(tc.tile_pool(name="prods", bufs=12))
+        prods = ctx.enter_context(tc.tile_pool(name="prods", bufs=(BLOCKS + 1) * D))
         psum = ctx.enter_context(tc.psum_pool(name="psum", bufs=3))
 
         offs_sb = lists.tile([P, S // 16], U16, name="offs_sb")
@@ -180,7 +180,7 @@ def tile_picked_sage_relu_e_kernel(
                     in_=x_grp[s][:, cols, :].rearrange("p t j -> p (t j)"),
                 )
 
-        held = ["h0"] + [f"w1_turn{c}_1" for c in (2, 4, 5, 6)] + [f"w2_turn{c}" for c in range(3)]
+        held = ["h0"] + [f"w1_turn{c}_1" for c in (2, 3, 5, 6)] + [f"w2_turn{c}" for c in range(3)]
 
         def project(b):
             h = keep.tile([P, S], F32, name="h_turn", tag=held[b], align_bytes=64)
@@ -300,7 +300,7 @@ def tile_picked_sage_relu_e_kernel(
             for n in range(n0, n1, P):
                 group_w2(s, n, n + P)
 
-        grouped_in = {0: (2,), 1: (3, 4), 2: (5,), 3: (6,), 4: (7,)}
+        grouped_in = {0: (2,), 1: (3,), 2: (4, 5), 3: (6,), 4: (7,)}
         h_next = project(0)
         group_block(1)
         quantize_w1(1)

@@ -8,8 +8,12 @@ P = 128
 PACK = 4
 K_PASS = P * PACK
 PASSES = K // K_PASS
+LAST = PASSES - 1
 BLOCKS = H // P
 HALVES = V // P
+M_TILES = N // P
+LIST_COL = 16
+RUN = 4
 FLOPS = 2 * S * K * H + 2 * V * H * N + 2 * D * V * H
 
 F32 = mybir.dt.float32
@@ -21,7 +25,11 @@ FP8X4 = mybir.dt.float8_e4m3fn_x4
 RELU = mybir.ActivationFunctionType.Relu
 MULT = mybir.AluOpType.mult
 
-W1_LOADS = (1,) * BLOCKS
+NODE_PIECES = (slice(0, 2 * P), slice(2 * P, 3 * P), slice(3 * P, S))
+W2_COLS = N // 2
+W2_LOADS = [(s, n0) for s in range(PASSES) for n0 in range(0, N, W2_COLS)]
+W1_IN_STEP = {0: (2,), 1: (3,), 2: (4, 5), 3: (6,), 4: (7,)}
+FIRST_W2_STEP = BLOCKS - len(W2_LOADS)
 
 
 def tile_picked_sage_relu_e_kernel(
@@ -34,100 +42,82 @@ def tile_picked_sage_relu_e_kernel(
         prods = ctx.enter_context(tc.tile_pool(name="prods", bufs=(BLOCKS + 1) * D))
         psum = ctx.enter_context(tc.psum_pool(name="psum", bufs=3))
 
-        offs_sb = lists.tile([P, S // 16], U16, name="offs_sb")
-        pos_sb = [lists.tile([P, V // 16], U16, name=f"pos_sb{d}") for d in range(D)]
+        offs_sb = lists.tile([P, S // LIST_COL], U16, name="offs_sb")
+        pos_sb = [lists.tile([P, V // LIST_COL], U16, name=f"pos_sb{d}") for d in range(D)]
 
         ident = keep.tile([P, P], F32, name="ident")
         make_identity(nc, ident[:])
-        warm = keep.tile([P, 1], F32, name="warm")
-        nc.gpsimd.memset(warm[:], 0.0)
-        warm_out = keep.tile([P, 1], F32, name="warm_out")
-        nc.scalar.activation(warm_out[:], warm[:], RELU)
 
         x_raw = [[keep.tile([P, T], F32, name=f"x_raw{s}_{j}") for j in range(PACK)] for s in range(PASSES)]
         w1_raw = [
             [
-                keep.tile([P, PACK, n * P], F32, name=f"w1_raw{c}_{s}", tag=f"w1_turn{c}_{s}", align_bytes=64)
+                keep.tile([P, PACK, P], F32, name=f"w1_raw{b}_{s}", tag=f"w1_slot{b}_{s}", align_bytes=64)
                 for s in range(PASSES)
             ]
-            for c, n in enumerate(W1_LOADS)
+            for b in range(BLOCKS)
         ]
-        w2_loads = [(s, n0, n0 + N // 2) for s in range(PASSES) for n0 in (0, N // 2)]
         w2_raw = [
-            keep.tile([P, PACK, n1 - n0], F32, name=f"w2_raw{c}", tag=f"w2_turn{c}", align_bytes=64)
-            for c, (s, n0, n1) in enumerate(w2_loads)
+            keep.tile([P, PACK, W2_COLS], F32, name=f"w2_raw{c}", tag=f"w2_slot{c}", align_bytes=64)
+            for c in range(len(W2_LOADS))
         ]
         gate_rows = keep.tile([P, V], F32, name="gate_rows")
         nc.gpsimd.memset(gate_rows[:], 0.0)
         gate_cols = keep.tile([P, HALVES, D], F32, name="gate_cols")
         gate_sb = [keep.tile([P, V], F32, name=f"gate_sb{d}", tag=f"gate{d}", align_bytes=64) for d in range(D)]
-        home = [(c, i) for c, n in enumerate(W1_LOADS) for i in range(n)]
 
-        def load_x(s, j):
-            rows = xT[s * K_PASS : (s + 1) * K_PASS, :].rearrange("(p j) t -> j p t", j=PACK)
-            nc.sync.dma_start(out=x_raw[s][j][:], in_=rows[j])
-
-        def load_w1(c, s):
-            first = sum(W1_LOADS[:c]) * P
-            block = w1[s * K_PASS : (s + 1) * K_PASS, first : first + W1_LOADS[c] * P]
-            nc.sync.dma_start(out=w1_raw[c][s][:], in_=block.rearrange("(p j) m -> p j m", j=PACK))
-
-        lists_after = {1: (1, 2, 3)}
         for s in range(PASSES):
+            rows = xT[s * K_PASS : (s + 1) * K_PASS, :].rearrange("(p j) t -> j p t", j=PACK)
             for j in range(PACK):
-                load_x(s, j)
+                nc.sync.dma_start(out=x_raw[s][j][:], in_=rows[j])
                 if (s, j) == (0, 0):
                     nc.sync.dma_start(offs_sb[:], offs)
                     nc.sync.dma_start(pos_sb[0][:], pos1)
                 if (s, j) == (0, 1):
                     nc.sync.dma_start(out=gate_rows[:D, :], in_=gate[:, 0, :])
-        for c in range(len(W1_LOADS)):
+        for b in range(BLOCKS):
             for s in range(PASSES):
-                load_w1(c, s)
-            for d in lists_after.get(c, ()):
-                nc.sync.dma_start(pos_sb[d][:], (pos1, pos2, pos3, pos4)[d])
-        for c, (s, n0, n1) in enumerate(w2_loads):
-            nc.sync.dma_start(
-                out=w2_raw[c][:], in_=w2[s * K_PASS : (s + 1) * K_PASS, n0:n1].rearrange("(p j) n -> p j n", j=PACK)
-            )
+                block = w1[s * K_PASS : (s + 1) * K_PASS, b * P : (b + 1) * P]
+                nc.sync.dma_start(out=w1_raw[b][s][:], in_=block.rearrange("(p j) m -> p j m", j=PACK))
+            if b == 1:
+                for d, pos in ((1, pos2), (2, pos3), (3, pos4)):
+                    nc.sync.dma_start(pos_sb[d][:], pos)
+        for c, (s, n0) in enumerate(W2_LOADS):
+            cols = w2[s * K_PASS : (s + 1) * K_PASS, n0 : n0 + W2_COLS]
+            nc.sync.dma_start(out=w2_raw[c][:], in_=cols.rearrange("(p j) n -> p j n", j=PACK))
 
-        w1_grp = [
-            keep.tile([P, PASSES, P, PACK], BF16, name=f"w1_grp{b}", align_bytes=64)
-            for b in range(BLOCKS)
-        ]
+        w1_il = [keep.tile([P, PASSES, P, PACK], BF16, name=f"w1_il{b}", align_bytes=64) for b in range(BLOCKS)]
         w1_codes = [keep.tile([P, PASSES, P], U32, name=f"w1_codes{b}", align_bytes=64) for b in range(BLOCKS)]
         w1_scales = [keep.tile([P, PASSES, P], U8, name=f"w1_scales{b}", align_bytes=64) for b in range(BLOCKS)]
-        w2_grp = [keep.tile([P, N, PACK], BF16, name=f"w2_grp{s}", align_bytes=64) for s in range(PASSES)]
+        w2_il = [keep.tile([P, N, PACK], BF16, name=f"w2_il{s}", align_bytes=64) for s in range(PASSES)]
         w2_codes = {}
         w2_scales = [keep.tile([P, N], U8, name=f"w2_scales{s}", align_bytes=64) for s in range(PASSES)]
 
-        def group_w1(b, s):
-            c, i = home[b]
+        def interleave(dst, src):
             nc.scalar.copy(
-                out=w1_grp[b][:, s].rearrange("p (c i) j -> p c j i", i=4),
-                in_=w1_raw[c][s][:, :, i * P : (i + 1) * P].rearrange("p j (c i) -> p c j i", i=4),
+                out=dst.rearrange("p (c i) j -> p c j i", i=RUN), in_=src.rearrange("p j (c i) -> p c j i", i=RUN)
             )
+
+        def interleave_w1(b):
+            for s in range(PASSES):
+                interleave(w1_il[b][:, s], w1_raw[b][s][:])
+
+        def interleave_w2(c):
+            s, n0 = W2_LOADS[c]
+            for n in range(0, W2_COLS, P):
+                interleave(w2_il[s][:, n0 + n : n0 + n + P, :], w2_raw[c][:, :, n : n + P])
 
         def quantize_w1(b):
             nc.vector.quantize_mx(
                 out=w1_codes[b][:].rearrange("p s m -> p (s m)").bitcast(FP8X4),
                 scales=w1_scales[b][:].rearrange("p s m -> p (s m)"),
-                in_=w1_grp[b][:].rearrange("p s m j -> p (s m j)"),
+                in_=w1_il[b][:].rearrange("p s m j -> p (s m j)"),
             )
 
         def quantize_w1_pass(b, s):
             nc.vector.quantize_mx(
                 out=w1_codes[b][:, s].bitcast(FP8X4),
                 scales=w1_scales[b][:, s],
-                in_=w1_grp[b][:, s].rearrange("p m j -> p (m j)"),
-            )
-
-        def group_w2(s, n0, n1):
-            c = max(i for i, load in enumerate(w2_loads) if load[:2] <= (s, n0))
-            first = w2_loads[c][1]
-            nc.scalar.copy(
-                out=w2_grp[s][:, n0:n1, :].rearrange("p (c i) j -> p c j i", i=4),
-                in_=w2_raw[c][:, :, n0 - first : n1 - first].rearrange("p j (c i) -> p c j i", i=4),
+                in_=w1_il[b][:, s].rearrange("p m j -> p (m j)"),
             )
 
         def quantize_w2(s):
@@ -135,56 +125,62 @@ def tile_picked_sage_relu_e_kernel(
             nc.vector.quantize_mx(
                 out=w2_codes[s][:].bitcast(FP8X4),
                 scales=w2_scales[s][:],
-                in_=w2_grp[s][:].rearrange("p n j -> p (n j)"),
+                in_=w2_il[s][:].rearrange("p n j -> p (n j)"),
             )
 
         spread = psum.tile([P, HALVES, P], F32, name="spread", tag="bank")
         for v in range(HALVES):
             nc.tensor.transpose(spread[:, v, :], gate_rows[:, v * P : (v + 1) * P], ident[:])
         nc.scalar.copy(out=gate_cols[:], in_=spread[:, :, :D])
-        for g in range(D // 2):
-            spread = psum.tile([P, 2 * V], F32, name="spread", tag="bank")
-            for r in range(2 * HALVES):
-                d, v = 2 * g + r // HALVES, r % HALVES
-                column = gate_cols[:, v, d : d + 1]
-                nc.tensor.transpose(spread[:, r * P : (r + 1) * P], column.to_broadcast([P, P]), ident[:])
+        for d0 in range(0, D, 2):
+            spread = psum.tile([P, 2, V], F32, name="spread", tag="bank")
             for r in range(2):
-                nc.scalar.copy(out=gate_sb[2 * g + r][:], in_=spread[:, r * V : (r + 1) * V])
+                for v in range(HALVES):
+                    column = gate_cols[:, v, d0 + r : d0 + r + 1]
+                    nc.tensor.transpose(spread[:, r, v * P : (v + 1) * P], column.to_broadcast([P, P]), ident[:])
+            for r in range(2):
+                nc.scalar.copy(out=gate_sb[d0 + r][:], in_=spread[:, r, :])
 
-        x_grp = [keep.tile([P, S, PACK], BF16, name=f"x_grp{s}", align_bytes=64) for s in range(PASSES)]
+        x_il = [keep.tile([P, S, PACK], BF16, name=f"x_il{s}", align_bytes=64) for s in range(PASSES)]
         x_codes = [keep.tile([P, S], U32, name=f"x_codes{s}", align_bytes=64) for s in range(PASSES)]
         x_scales = [keep.tile([P, S], U8, name="x_scales0", align_bytes=64)]
-        HALF = S // 2
-        PIECES = (slice(0, HALF), slice(HALF, HALF + P), slice(HALF + P, S))
-        for s in range(PASSES):
-            last = s == PASSES - 1
-            for j in range(PACK):
-                if last and j == PACK - 1:
-                    group_w1(0, 0)
-                    quantize_w1_pass(0, 0)
-                    group_w1(0, 1)
-                    for t in (0, 1):
-                        nc.vector.tensor_copy(
-                            x_grp[s][:, t * HALF : (t + 1) * HALF, j],
-                            x_raw[s][j][:].indirect(offs_sb[:, t * HALF // 16 : (t + 1) * HALF // 16]),
-                        )
-                    quantize_w1_pass(0, 1)
-                else:
-                    nc.vector.tensor_copy(x_grp[s][:, :, j], x_raw[s][j][:].indirect(offs_sb[:]))
-            if last:
-                x_scales.append(keep.tile([P, S], U8, name="x_scales1", tag="w1_turn0_0", align_bytes=64))
-            for cols in PIECES if last else (slice(0, S),):
-                nc.vector.quantize_mx(
-                    out=x_codes[s][:, cols].bitcast(FP8X4),
-                    scales=x_scales[s][:, cols],
-                    in_=x_grp[s][:, cols, :].rearrange("p t j -> p (t j)"),
-                )
 
-        held = ["h0"] + [f"w1_turn{c}_1" for c in (2, 3, 5, 6)] + [f"w2_turn{c}" for c in range(3)]
+        def gather_nodes(s, j, n0, n1):
+            entries = offs_sb[:, n0 // LIST_COL : n1 // LIST_COL]
+            nc.vector.tensor_copy(x_il[s][:, n0:n1, j], x_raw[s][j][:].indirect(entries))
+
+        def quantize_nodes(s, nodes):
+            nc.vector.quantize_mx(
+                out=x_codes[s][:, nodes].bitcast(FP8X4),
+                scales=x_scales[s][:, nodes],
+                in_=x_il[s][:, nodes, :].rearrange("p t j -> p (t j)"),
+            )
+
+        for j in range(PACK):
+            gather_nodes(0, j, 0, S)
+        quantize_nodes(0, slice(0, S))
+        for j in range(PACK - 1):
+            gather_nodes(LAST, j, 0, S)
+        interleave(w1_il[0][:, 0], w1_raw[0][0][:])
+        quantize_w1_pass(0, 0)
+        interleave(w1_il[0][:, LAST], w1_raw[0][LAST][:])
+        for n0 in range(0, S, S // 2):
+            gather_nodes(LAST, PACK - 1, n0, n0 + S // 2)
+        quantize_w1_pass(0, LAST)
+        x_scales.append(keep.tile([P, S], U8, name="x_scales1", tag="w1_slot0_0", align_bytes=64))
+        for nodes in NODE_PIECES:
+            quantize_nodes(LAST, nodes)
+
+        def h_slot(b):
+            if b == 0:
+                return "h0"
+            if b - 1 >= FIRST_W2_STEP:
+                return f"w2_slot{b - 1 - FIRST_W2_STEP}"
+            return f"w1_slot{W1_IN_STEP[b - 1][-1]}_{LAST}"
 
         def project(b):
-            h = keep.tile([P, S], F32, name="h_turn", tag=held[b], align_bytes=64)
-            for nodes in PIECES if b == 0 else (slice(0, S),):
+            h = keep.tile([P, S], F32, name="h", tag=h_slot(b), align_bytes=64)
+            for nodes in NODE_PIECES if b == 0 else (slice(0, S),):
                 width = nodes.stop - nodes.start
                 if b == BLOCKS - 1:
                     acc = psum.tile([P, S], F32, name="acc", tag="last", bufs=1)
@@ -198,23 +194,22 @@ def tile_picked_sage_relu_e_kernel(
                         rhs=x_codes[s][:, nodes].bitcast(FP8X4),
                         rhs_scale=x_scales[s][:, nodes],
                         start=(s == 0),
-                        stop=(s == PASSES - 1),
+                        stop=(s == LAST),
                     )
-                if b > 0:
-                    nc.scalar.activation(h[:, nodes], acc[:, :width], RELU)
-                else:
+                if b == 0:
                     nc.vector.tensor_relu(h[:, nodes], acc[:, :width])
+                else:
+                    nc.scalar.activation(h[:, nodes], acc[:, :width], RELU)
             return h
 
-        z_t = []
-        z_grp = [keep.tile([P, V * PACK], BF16, name=f"z_grp{s}", align_bytes=64) for s in range(PASSES)]
+        sums = {}
+        z_il = [keep.tile([P, V * PACK], BF16, name=f"z_il{s}", align_bytes=64) for s in range(PASSES)]
         z_codes = {}
         z_scales = [keep.tile([P, V], U8, name=f"z_scales{s}", align_bytes=64) for s in range(PASSES)]
-        out_acc = {}
 
         def add_transposed(b, d, v, prod):
             nc.tensor.matmul(
-                z_ps[v][:, (b % PACK) * P : (b % PACK + 1) * P],
+                sums[b // PACK][v][:, (b % PACK) * P : (b % PACK + 1) * P],
                 prod,
                 ident[:],
                 start=(d == 0),
@@ -225,7 +220,7 @@ def tile_picked_sage_relu_e_kernel(
         def gather_block(b, h):
             for d in range(D):
                 if (b, d) == (0, 1):
-                    prod = keep.tile([P, V], F32, name="prod_held", tag="w1_turn1_1", align_bytes=64)
+                    prod = keep.tile([P, V], F32, name="prod_held", tag=f"w1_slot1_{LAST}", align_bytes=64)
                 else:
                     prod = prods.tile([P, V], F32, name="prod")
                 nc.vector.tensor_tensor(prod[:], h[:].indirect(pos_sb[d][:]), gate_sb[d][:], MULT)
@@ -235,36 +230,28 @@ def tile_picked_sage_relu_e_kernel(
         def gather_half(b, h, v):
             for d in range(D):
                 prod = prods.tile([P, P], F32, name="prod")
-                nc.vector.tensor_tensor(
-                    prod[:],
-                    h[:].indirect(pos_sb[d][:, v * P // 16 : (v + 1) * P // 16]),
-                    gate_sb[d][:, v * P : (v + 1) * P],
-                    MULT,
-                )
+                entries = pos_sb[d][:, v * P // LIST_COL : (v + 1) * P // LIST_COL]
+                nc.vector.tensor_tensor(prod[:], h[:].indirect(entries), gate_sb[d][:, v * P : (v + 1) * P], MULT)
                 add_transposed(b, d, v, prod[:])
 
-        def z_out(banks, s, v, b0, b1):
-            if not z_t:
-                z_t.append(keep.tile([P, PASSES * HALVES * K_PASS], BF16, name="z_t", tag="w2_turn3", align_bytes=64))
+        def round_z(z_rows, s, v, b0, b1):
             first = (s * HALVES + v) * K_PASS
-            half = z_t[0][:, first : first + K_PASS].rearrange("v (u p e) -> v u p e", u=2, e=2)
+            dst = z_rows[:, first : first + K_PASS].rearrange("t (u p e) -> t u p e", u=2, e=2)
+            per_block = P // PACK
             nc.scalar.copy(
-                out=half[:, :, b0 * 32 : b1 * 32, :],
-                in_=banks[v][:, b0 * P : b1 * P].rearrange("v (p u e) -> v u p e", u=2, e=2),
+                out=dst[:, :, b0 * per_block : b1 * per_block, :],
+                in_=sums[s][v][:, b0 * P : b1 * P].rearrange("t (p u e) -> t u p e", u=2, e=2),
             )
 
-        def z_words(s, v0, v1):
-            if s == LAST:
-                words = psum.tile([P, v1 - v0, 2, P], F32, name="words", tag=f"z_ps0_{v0}", bufs=1)
-            else:
-                words = psum.tile([P, v1 - v0, 2, P], F32, name="words", tag="last", bufs=1)
+        def turn_z(z_rows, s, v0, v1, bank):
+            words = psum.tile([P, v1 - v0, 2, P], F32, name="words", tag=bank, bufs=1)
             for v in range(v0, v1):
                 for u in range(2):
-                    first = ((s * HALVES + v) * 2 + u) * 2 * P
-                    zw = z_t[0][:, first : first + 2 * P].bitcast(F32)
-                    nc.tensor.transpose(words[:, v - v0, u, :], zw, ident[:])
+                    first = (s * HALVES + v) * K_PASS + u * (K_PASS // 2)
+                    run = z_rows[:, first : first + K_PASS // 2].bitcast(F32)
+                    nc.tensor.transpose(words[:, v - v0, u, :], run, ident[:])
             nc.scalar.copy(
-                out=z_grp[s][:, v0 * K_PASS : v1 * K_PASS].bitcast(F32).rearrange("p (v n u) -> p v n u", n=P, u=2),
+                out=z_il[s][:, v0 * K_PASS : v1 * K_PASS].bitcast(F32).rearrange("p (v n u) -> p v n u", n=P, u=2),
                 in_=words[:].rearrange("p v u n -> p v n u"),
             )
 
@@ -272,94 +259,81 @@ def tile_picked_sage_relu_e_kernel(
             nc.vector.quantize_mx(
                 out=z_codes[s][:, v0 * P : v1 * P].bitcast(FP8X4),
                 scales=z_scales[s][:, v0 * P : v1 * P],
-                in_=z_grp[s][:, v0 * K_PASS : v1 * K_PASS],
+                in_=z_il[s][:, v0 * K_PASS : v1 * K_PASS],
             )
 
         def out_pass(acc, s, m, v, start):
             cols = slice(m * P, (m + 1) * P)
-            nodes = slice(v * P, (v + 1) * P)
+            targets = slice(v * P, (v + 1) * P)
             nc.tensor.matmul_mx(
                 out=acc,
                 lhsT=w2_codes[s][:, cols].bitcast(FP8X4),
                 lhsT_scale=w2_scales[s][:, cols],
-                rhs=z_codes[s][:, nodes].bitcast(FP8X4),
-                rhs_scale=z_scales[s][:, nodes],
+                rhs=z_codes[s][:, targets].bitcast(FP8X4),
+                rhs_scale=z_scales[s][:, targets],
                 start=start,
                 stop=not start,
             )
 
-        LAST = PASSES - 1
-        M_TILES = N // P
-
-        def group_block(b):
-            for s in range(PASSES):
-                group_w1(b, s)
-
-        def group_w2_load(c):
-            s, n0, n1 = w2_loads[c]
-            for n in range(n0, n1, P):
-                group_w2(s, n, n + P)
-
-        grouped_in = {0: (2,), 1: (3,), 2: (4, 5), 3: (6,), 4: (7,)}
         h_next = project(0)
-        group_block(1)
+        interleave_w1(1)
         quantize_w1(1)
         for b in range(BLOCKS):
-            if b == PACK:
-                z_first = z_ps
             if b % PACK == 0:
-                z_ps = [
-                    psum.tile([P, K_PASS], F32, name="z_ps", tag=f"z_ps{b // PACK}_{v}", bufs=1) for v in range(HALVES)
+                sums[b // PACK] = [
+                    psum.tile([P, K_PASS], F32, name="sums", tag=f"sums{b // PACK}_{v}", bufs=1) for v in range(HALVES)
                 ]
             h = h_next
-            for c in grouped_in.get(b, ()):
-                group_block(c)
-            if b in (4, 5, 6):
-                group_w2_load(b - 4)
+            for ahead in W1_IN_STEP.get(b, ()):
+                interleave_w1(ahead)
+            if b >= FIRST_W2_STEP:
+                interleave_w2(b - FIRST_W2_STEP)
             if b + 1 < BLOCKS:
                 h_next = project(b + 1)
-            if b == BLOCKS - 1:
-                group_w2_load(3)
-                for v in range(HALVES):
-                    z_out(z_first, 0, v, 0, PACK)
-                for v in range(HALVES):
-                    z_out(z_ps, LAST, v, 0, PACK - 1)
-                z_words(0, 0, HALVES)
-                for v in range(HALVES):
-                    gather_half(b, h, v)
-                    z_out(z_ps, LAST, v, PACK - 1, PACK)
-                    z_words(LAST, v, v + 1)
-            else:
                 gather_block(b, h)
-            for c in grouped_in.get(b, ()):
-                quantize_w1(c)
+            for ahead in W1_IN_STEP.get(b, ()):
+                quantize_w1(ahead)
+
+        z_rows = keep.tile(
+            [P, PASSES * HALVES * K_PASS], BF16, name="z_rows", tag=f"w2_slot{len(W2_LOADS) - 1}", align_bytes=64
+        )
+        for v in range(HALVES):
+            round_z(z_rows, 0, v, 0, PACK)
+        for v in range(HALVES):
+            round_z(z_rows, LAST, v, 0, PACK - 1)
+        turn_z(z_rows, 0, 0, HALVES, "last")
+        for v in range(HALVES):
+            gather_half(BLOCKS - 1, h, v)
+            round_z(z_rows, LAST, v, PACK - 1, PACK)
+            turn_z(z_rows, LAST, v, v + 1, f"sums0_{v}")
 
         quantize_w2(0)
         z_codes[0] = keep.tile([P, V], U32, name="z_codes0", tag="gate1", align_bytes=64)
         quantize_z(0, 0, HALVES)
-        early = ("z_ps1_1", "z_ps0_0", "z_ps0_1")
-        for m, tag in enumerate(early):
-            out_acc[m] = psum.tile([P, P], F32, name="out_acc", tag=tag, bufs=1)
+        ahead_banks = (f"sums{LAST}_1", "sums0_0", "sums0_1")
+        out_acc = []
+        for m, bank in enumerate(ahead_banks):
+            out_acc.append(psum.tile([P, P], F32, name="out_acc", tag=bank, bufs=1))
             out_pass(out_acc[m][:], 0, m, 1, True)
-        quantize_w2(1)
+        quantize_w2(LAST)
         z_codes[LAST] = keep.tile([P, V], U32, name="z_codes1", align_bytes=64)
         for v in range(HALVES):
             quantize_z(LAST, v, v + 1)
+
         out_rows = out.rearrange("(m p) v -> p m v", p=P)
-        for pair in range(M_TILES // 2):
+        for pair, copy in enumerate((nc.scalar.copy, nc.vector.tensor_copy)):
             acc = psum.tile([P, 2, P], F32, name="acc", tag="bank")
             for i in range(2):
                 out_pass(acc[:, i, :], LAST, 2 * pair + i, 0, True)
                 out_pass(acc[:, i, :], 0, 2 * pair + i, 0, False)
             result = keep.tile([P, 2, P], F32, name=f"result0_{pair}")
-            copy = (nc.scalar.copy, nc.vector.tensor_copy)[pair]
             copy(out=result[:], in_=acc[:])
             nc.sync.dma_start(out=out_rows[:, 2 * pair : 2 * pair + 2, :P], in_=result[:])
         for m in range(M_TILES):
-            if m in out_acc:
+            if m < len(ahead_banks):
                 out_pass(out_acc[m][:], LAST, m, 1, False)
             else:
-                out_acc[m] = psum.tile([P, P], F32, name="out_acc", tag="z_ps1_0", bufs=1)
+                out_acc.append(psum.tile([P, P], F32, name="out_acc", tag=f"sums{LAST}_0", bufs=1))
                 out_pass(out_acc[m][:], LAST, m, 1, True)
                 out_pass(out_acc[m][:], 0, m, 1, False)
             result = keep.tile([P, P], F32, name=f"result1_{m}")

@@ -25,10 +25,19 @@ FP8X4 = mybir.dt.float8_e4m3fn_x4
 RELU = mybir.ActivationFunctionType.Relu
 MULT = mybir.AluOpType.mult
 
-NODE_PIECES = (slice(0, 2 * P), slice(2 * P, 3 * P), slice(3 * P, S))
+W1_GROUPS = ((0,), (1,), (2,), (3, 4), (5, 6), (7,))
+ACC_BANKS = (
+    ("sums0_0", "sums0_1", "sums1_0", "sums1_1"),
+    ("r0", "r1"),
+    ("r2", "last"),
+    ("r0", "r1"),
+    ("r2",),
+    ("r0",),
+    ("r1",),
+    ("last",),
+)
 W2_COLS = N // 2
 W2_LOADS = [(s, n0) for s in range(PASSES) for n0 in range(0, N, W2_COLS)]
-W1_IN_STEP = {0: (2,), 1: (3,), 2: (4, 5), 3: (6,), 4: (7,)}
 FIRST_W2_STEP = BLOCKS - len(W2_LOADS)
 
 
@@ -40,7 +49,7 @@ def tile_picked_sage_relu_e_kernel(
         lists = ctx.enter_context(tc.tile_pool(name="lists", bufs=1))
         keep = ctx.enter_context(tc.tile_pool(name="keep", bufs=1))
         prods = ctx.enter_context(tc.tile_pool(name="prods", bufs=(BLOCKS + 1) * D))
-        psum = ctx.enter_context(tc.psum_pool(name="psum", bufs=3))
+        psum = ctx.enter_context(tc.psum_pool(name="psum", bufs=1))
 
         offs_sb = lists.tile([P, S // LIST_COL], U16, name="offs_sb")
         pos_sb = [lists.tile([P, V // LIST_COL], U16, name=f"pos_sb{d}") for d in range(D)]
@@ -51,10 +60,10 @@ def tile_picked_sage_relu_e_kernel(
         x_raw = [[keep.tile([P, T], F32, name=f"x_raw{s}_{j}") for j in range(PACK)] for s in range(PASSES)]
         w1_raw = [
             [
-                keep.tile([P, PACK, P], F32, name=f"w1_raw{b}_{s}", tag=f"w1_slot{b}_{s}", align_bytes=64)
+                keep.tile([P, PACK, len(group) * P], F32, name=f"w1_raw{g}_{s}", tag=f"w1_slot{g}_{s}", align_bytes=64)
                 for s in range(PASSES)
             ]
-            for b in range(BLOCKS)
+            for g, group in enumerate(W1_GROUPS)
         ]
         w2_raw = [
             keep.tile([P, PACK, W2_COLS], F32, name=f"w2_raw{c}", tag=f"w2_slot{c}", align_bytes=64)
@@ -71,14 +80,15 @@ def tile_picked_sage_relu_e_kernel(
                 nc.sync.dma_start(out=x_raw[s][j][:], in_=rows[j])
                 if (s, j) == (0, 0):
                     nc.sync.dma_start(offs_sb[:], offs)
-                    nc.sync.dma_start(pos_sb[0][:], pos1)
                 if (s, j) == (0, 1):
                     nc.sync.dma_start(out=gate_rows[:D, :], in_=gate[:, 0, :])
-        for b in range(BLOCKS):
+        for g, group in enumerate(W1_GROUPS):
             for s in range(PASSES):
-                block = w1[s * K_PASS : (s + 1) * K_PASS, b * P : (b + 1) * P]
-                nc.sync.dma_start(out=w1_raw[b][s][:], in_=block.rearrange("(p j) m -> p j m", j=PACK))
-            if b == 1:
+                cols = w1[s * K_PASS : (s + 1) * K_PASS, group[0] * P : (group[-1] + 1) * P]
+                nc.sync.dma_start(out=w1_raw[g][s][:], in_=cols.rearrange("(p j) m -> p j m", j=PACK))
+            if g == 0:
+                nc.sync.dma_start(pos_sb[0][:], pos1)
+            if g == 1:
                 for d, pos in ((1, pos2), (2, pos3), (3, pos4)):
                     nc.sync.dma_start(pos_sb[d][:], pos)
         for c, (s, n0) in enumerate(W2_LOADS):
@@ -97,9 +107,9 @@ def tile_picked_sage_relu_e_kernel(
                 out=dst.rearrange("p (c i) j -> p c j i", i=RUN), in_=src.rearrange("p j (c i) -> p c j i", i=RUN)
             )
 
-        def interleave_w1(b):
-            for s in range(PASSES):
-                interleave(w1_il[b][:, s], w1_raw[b][s][:])
+        def interleave_w1(g, s):
+            for i, b in enumerate(W1_GROUPS[g]):
+                interleave(w1_il[b][:, s], w1_raw[g][s][:, :, i * P : (i + 1) * P])
 
         def interleave_w2(c):
             s, n0 = W2_LOADS[c]
@@ -128,12 +138,12 @@ def tile_picked_sage_relu_e_kernel(
                 in_=w2_il[s][:].rearrange("p n j -> p (n j)"),
             )
 
-        spread = psum.tile([P, HALVES, P], F32, name="spread", tag="bank")
+        spread = psum.tile([P, HALVES, P], F32, name="spread", tag="r0", bufs=1)
         for v in range(HALVES):
             nc.tensor.transpose(spread[:, v, :], gate_rows[:, v * P : (v + 1) * P], ident[:])
         nc.scalar.copy(out=gate_cols[:], in_=spread[:, :, :D])
         for d0 in range(0, D, 2):
-            spread = psum.tile([P, 2, V], F32, name="spread", tag="bank")
+            spread = psum.tile([P, 2, V], F32, name="spread", tag=f"r{1 + d0 // 2}", bufs=1)
             for r in range(2):
                 for v in range(HALVES):
                     column = gate_cols[:, v, d0 + r : d0 + r + 1]
@@ -143,7 +153,14 @@ def tile_picked_sage_relu_e_kernel(
 
         x_il = [keep.tile([P, S, PACK], BF16, name=f"x_il{s}", align_bytes=64) for s in range(PASSES)]
         x_codes = [keep.tile([P, S], U32, name=f"x_codes{s}", align_bytes=64) for s in range(PASSES)]
-        x_scales = [keep.tile([P, S], U8, name="x_scales0", align_bytes=64)]
+        x_scales0 = keep.tile([P, S], U8, name="x_scales0", align_bytes=64)
+        x_scales1 = []
+
+        def node_scales(s, nodes):
+            if s == 0:
+                return x_scales0[:, nodes]
+            half = nodes.start // (S // 2)
+            return x_scales1[half][:, nodes.start - half * (S // 2) : nodes.stop - half * (S // 2)]
 
         def gather_nodes(s, j, n0, n1):
             entries = offs_sb[:, n0 // LIST_COL : n1 // LIST_COL]
@@ -152,7 +169,7 @@ def tile_picked_sage_relu_e_kernel(
         def quantize_nodes(s, nodes):
             nc.vector.quantize_mx(
                 out=x_codes[s][:, nodes].bitcast(FP8X4),
-                scales=x_scales[s][:, nodes],
+                scales=node_scales(s, nodes),
                 in_=x_il[s][:, nodes, :].rearrange("p t j -> p (t j)"),
             )
 
@@ -161,45 +178,50 @@ def tile_picked_sage_relu_e_kernel(
         quantize_nodes(0, slice(0, S))
         for j in range(PACK - 1):
             gather_nodes(LAST, j, 0, S)
-        interleave(w1_il[0][:, 0], w1_raw[0][0][:])
+        interleave_w1(0, 0)
+        interleave_w1(0, LAST)
+        gather_nodes(LAST, PACK - 1, 0, S)
         quantize_w1_pass(0, 0)
-        interleave(w1_il[0][:, LAST], w1_raw[0][LAST][:])
-        for n0 in range(0, S, S // 2):
-            gather_nodes(LAST, PACK - 1, n0, n0 + S // 2)
+        x_scales1.append(keep.tile([P, S // 2], U8, name="x_scales1", tag="w1_slot0_0", align_bytes=64))
+        quantize_nodes(LAST, slice(0, 2 * P))
         quantize_w1_pass(0, LAST)
-        x_scales.append(keep.tile([P, S], U8, name="x_scales1", tag="w1_slot0_0", align_bytes=64))
-        for nodes in NODE_PIECES:
-            quantize_nodes(LAST, nodes)
+        x_scales1.append(keep.tile([P, S // 2], U8, name="x_scales1", tag=f"w1_slot0_{LAST}", align_bytes=64))
+        quantize_nodes(LAST, slice(2 * P, 3 * P))
+        quantize_nodes(LAST, slice(3 * P, S))
 
-        def h_slot(b):
-            if b == 0:
-                return "h0"
-            if b - 1 >= FIRST_W2_STEP:
-                return f"w2_slot{b - 1 - FIRST_W2_STEP}"
-            return f"w1_slot{W1_IN_STEP[b - 1][-1]}_{LAST}"
+        accs = {}
 
-        def project(b):
-            h = keep.tile([P, S], F32, name="h", tag=h_slot(b), align_bytes=64)
-            for nodes in NODE_PIECES if b == 0 else (slice(0, S),):
+        def pieces(b):
+            width = S // len(ACC_BANKS[b])
+            return [slice(n0, n0 + width) for n0 in range(0, S, width)]
+
+        def project(b, s):
+            if s == 0:
+                accs[b] = [
+                    psum.tile([P, S // len(ACC_BANKS[b])], F32, name="acc", tag=bank, bufs=1) for bank in ACC_BANKS[b]
+                ]
+            for acc, nodes in zip(accs[b], pieces(b)):
                 width = nodes.stop - nodes.start
-                if b == BLOCKS - 1:
-                    acc = psum.tile([P, S], F32, name="acc", tag="last", bufs=1)
-                else:
-                    acc = psum.tile([P, S], F32, name="acc", tag="bank")
-                for s in range(PASSES):
+                step = width if s == 0 else min(width, S // 2)
+                for n0 in range(0, width, step):
+                    part = slice(nodes.start + n0, nodes.start + n0 + step)
                     nc.tensor.matmul_mx(
-                        out=acc[:, :width],
+                        out=acc[:, n0 : n0 + step],
                         lhsT=w1_codes[b][:, s].bitcast(FP8X4),
                         lhsT_scale=w1_scales[b][:, s],
-                        rhs=x_codes[s][:, nodes].bitcast(FP8X4),
-                        rhs_scale=x_scales[s][:, nodes],
+                        rhs=x_codes[s][:, part].bitcast(FP8X4),
+                        rhs_scale=node_scales(s, part),
                         start=(s == 0),
-                        stop=(s == LAST),
+                        stop=(s == LAST and n0 + step == width),
                     )
-                if b == 0:
-                    nc.vector.tensor_relu(h[:, nodes], acc[:, :width])
+
+        def relu(b, slot):
+            h = keep.tile([P, S], F32, name="h", tag=slot, align_bytes=64)
+            for i, (acc, nodes) in enumerate(zip(accs[b], pieces(b))):
+                if b == 0 and i % 2 == 0:
+                    nc.vector.tensor_relu(h[:, nodes], acc[:])
                 else:
-                    nc.scalar.activation(h[:, nodes], acc[:, :width], RELU)
+                    nc.scalar.activation(h[:, nodes], acc[:], RELU)
             return h
 
         sums = {}
@@ -217,15 +239,14 @@ def tile_picked_sage_relu_e_kernel(
                 is_transpose=True,
             )
 
-        def gather_block(b, h):
-            for d in range(D):
-                if (b, d) == (0, 1):
-                    prod = keep.tile([P, V], F32, name="prod_held", tag=f"w1_slot1_{LAST}", align_bytes=64)
-                else:
-                    prod = prods.tile([P, V], F32, name="prod")
-                nc.vector.tensor_tensor(prod[:], h[:].indirect(pos_sb[d][:]), gate_sb[d][:], MULT)
-                for v in range(HALVES):
-                    add_transposed(b, d, v, prod[:, v * P : (v + 1) * P])
+        def gather(b, d, h, held_by=None):
+            if held_by:
+                prod = keep.tile([P, V], F32, name="prod_held", tag=held_by, align_bytes=64)
+            else:
+                prod = prods.tile([P, V], F32, name="prod")
+            nc.vector.tensor_tensor(prod[:], h[:].indirect(pos_sb[d][:]), gate_sb[d][:], MULT)
+            for v in range(HALVES):
+                add_transposed(b, d, v, prod[:, v * P : (v + 1) * P])
 
         def gather_half(b, h, v):
             for d in range(D):
@@ -275,24 +296,44 @@ def tile_picked_sage_relu_e_kernel(
                 stop=not start,
             )
 
-        h_next = project(0)
-        interleave_w1(1)
-        quantize_w1(1)
-        for b in range(BLOCKS):
-            if b % PACK == 0:
-                sums[b // PACK] = [
-                    psum.tile([P, K_PASS], F32, name="sums", tag=f"sums{b // PACK}_{v}", bufs=1) for v in range(HALVES)
-                ]
-            h = h_next
-            for ahead in W1_IN_STEP.get(b, ()):
-                interleave_w1(ahead)
-            if b >= FIRST_W2_STEP:
+        def open_sums(s):
+            sums[s] = [psum.tile([P, K_PASS], F32, name="sums", tag=f"sums{s}_{v}", bufs=1) for v in range(HALVES)]
+
+        project(0, 0)
+        project(0, LAST)
+        interleave_w1(1, 0)
+        quantize_w1_pass(1, 0)
+        h = relu(0, "w1_slot1_0")
+        project(1, 0)
+        interleave_w1(1, LAST)
+        open_sums(0)
+        for b in range(BLOCKS - 1):
+            tight = b < 3
+            if b == PACK:
+                open_sums(LAST)
+            if tight:
+                gather(b, 0, h)
+                quantize_w1_pass(b + 1, LAST)
+                project(b + 1, LAST)
+            if b < FIRST_W2_STEP:
+                interleave_w1(b + 2, 0)
+                h_next = relu(b + 1, f"w1_slot{b + 2}_0")
+                interleave_w1(b + 2, LAST)
+            else:
                 interleave_w2(b - FIRST_W2_STEP)
-            if b + 1 < BLOCKS:
-                h_next = project(b + 1)
-                gather_block(b, h)
-            for ahead in W1_IN_STEP.get(b, ()):
-                quantize_w1(ahead)
+                h_next = relu(b + 1, f"w2_slot{b - FIRST_W2_STEP}")
+            for d in range(1 if tight else 0, D):
+                gather(b, d, h, f"w1_slot{b + 1}_{LAST}" if tight and d == 1 else None)
+            if b < 2:
+                quantize_w1_pass(b + 2, 0)
+                project(b + 2, 0)
+            else:
+                for ahead in {2: (4,), 3: (5, 6), 4: (7,)}.get(b, ()):
+                    quantize_w1(ahead)
+                    for s in range(PASSES):
+                        project(ahead, s)
+            h = h_next
+        interleave_w2(len(W2_LOADS) - 1)
 
         z_rows = keep.tile(
             [P, PASSES * HALVES * K_PASS], BF16, name="z_rows", tag=f"w2_slot{len(W2_LOADS) - 1}", align_bytes=64
@@ -322,7 +363,7 @@ def tile_picked_sage_relu_e_kernel(
 
         out_rows = out.rearrange("(m p) v -> p m v", p=P)
         for pair, copy in enumerate((nc.scalar.copy, nc.vector.tensor_copy)):
-            acc = psum.tile([P, 2, P], F32, name="acc", tag="bank")
+            acc = psum.tile([P, 2, P], F32, name="acc", tag=f"r{pair}", bufs=1)
             for i in range(2):
                 out_pass(acc[:, i, :], LAST, 2 * pair + i, 0, True)
                 out_pass(acc[:, i, :], 0, 2 * pair + i, 0, False)

@@ -38,6 +38,7 @@ ACC_BANKS = (
 )
 W2_COLS = N // 2
 W2_LOADS = [(s, n0) for s in range(PASSES) for n0 in range(0, N, W2_COLS)]
+SHARED_LOAD = 3
 FIRST_W2_STEP = BLOCKS - len(W2_LOADS)
 
 
@@ -48,6 +49,7 @@ def tile_picked_sage_relu_e_kernel(
     with ExitStack() as ctx:
         lists = ctx.enter_context(tc.tile_pool(name="lists", bufs=1))
         keep = ctx.enter_context(tc.tile_pool(name="keep", bufs=1))
+        placed = ctx.enter_context(tc.tile_pool(name="placed", bufs=1))
         prods = ctx.enter_context(tc.tile_pool(name="prods", bufs=(BLOCKS + 1) * D))
         psum = ctx.enter_context(tc.psum_pool(name="psum", bufs=1))
 
@@ -66,7 +68,9 @@ def tile_picked_sage_relu_e_kernel(
             for g, group in enumerate(W1_GROUPS)
         ]
         w2_raw = [
-            keep.tile([P, PACK, W2_COLS], F32, name=f"w2_raw{c}", tag=f"w2_slot{c}", align_bytes=64)
+            placed.tile([P, PACK, W2_COLS], F32, name="w2_shared", offset=0, align_bytes=64)
+            if c == SHARED_LOAD
+            else keep.tile([P, PACK, W2_COLS], F32, name=f"w2_raw{c}", tag=f"w2_slot{c}", align_bytes=64)
             for c in range(len(W2_LOADS))
         ]
         gate_rows = keep.tile([P, V], F32, name="gate_rows")
@@ -130,12 +134,14 @@ def tile_picked_sage_relu_e_kernel(
                 in_=w1_il[b][:, s].rearrange("p m j -> p (m j)"),
             )
 
-        def quantize_w2(s):
-            w2_codes[s] = keep.tile([P, N], U32, name=f"w2_codes{s}", tag=f"gate{2 * s}", align_bytes=64)
+        def quantize_w2(s, n0, n1, slot):
+            codes = keep.tile([P, n1 - n0], U32, name="w2_codes", tag=slot, align_bytes=64)
+            for n in range(n0, n1, P):
+                w2_codes[s, n // P] = codes[:, n - n0 : n - n0 + P]
             nc.vector.quantize_mx(
-                out=w2_codes[s][:].bitcast(FP8X4),
-                scales=w2_scales[s][:],
-                in_=w2_il[s][:].rearrange("p n j -> p (n j)"),
+                out=codes[:].bitcast(FP8X4),
+                scales=w2_scales[s][:, n0:n1],
+                in_=w2_il[s][:, n0:n1, :].rearrange("p n j -> p (n j)"),
             )
 
         spread = psum.tile([P, HALVES, P], F32, name="spread", tag="r0", bufs=1)
@@ -216,7 +222,10 @@ def tile_picked_sage_relu_e_kernel(
                     )
 
         def relu(b, slot):
-            h = keep.tile([P, S], F32, name="h", tag=slot, align_bytes=64)
+            if slot:
+                h = keep.tile([P, S], F32, name="h", tag=slot, align_bytes=64)
+            else:
+                h = placed.tile([P, S], F32, name="h_last", offset=0, align_bytes=64)
             for i, (acc, nodes) in enumerate(zip(accs[b], pieces(b))):
                 if b == 0 and i % 2 == 0:
                     nc.vector.tensor_relu(h[:, nodes], acc[:])
@@ -225,13 +234,14 @@ def tile_picked_sage_relu_e_kernel(
             return h
 
         sums = {}
+        last_sums = []
         z_il = [keep.tile([P, V * PACK], BF16, name=f"z_il{s}", align_bytes=64) for s in range(PASSES)]
         z_codes = {}
         z_scales = [keep.tile([P, V], U8, name=f"z_scales{s}", align_bytes=64) for s in range(PASSES)]
 
         def add_transposed(b, d, v, prod):
             nc.tensor.matmul(
-                sums[b // PACK][v][:, (b % PACK) * P : (b % PACK + 1) * P],
+                last_sums[v][:] if b == BLOCKS - 1 else sums[b // PACK][v][:, (b % PACK) * P : (b % PACK + 1) * P],
                 prod,
                 ident[:],
                 start=(d == 0),
@@ -250,25 +260,29 @@ def tile_picked_sage_relu_e_kernel(
 
         def gather_half(b, h, v):
             for d in range(D):
-                prod = prods.tile([P, P], F32, name="prod")
+                if (v, d) == (HALVES - 1, 0):
+                    prod = keep.tile([P, P], F32, name="prod_tail", tag="tail", align_bytes=64)
+                else:
+                    prod = prods.tile([P, P], F32, name="prod")
                 entries = pos_sb[d][:, v * P // LIST_COL : (v + 1) * P // LIST_COL]
                 nc.vector.tensor_tensor(prod[:], h[:].indirect(entries), gate_sb[d][:, v * P : (v + 1) * P], MULT)
                 add_transposed(b, d, v, prod[:])
 
         def round_z(z_rows, s, v, b0, b1):
-            first = (s * HALVES + v) * K_PASS
+            first = v * K_PASS
+            src = last_sums[v][:] if (s, b0) == (LAST, PACK - 1) else sums[s][v][:, b0 * P : b1 * P]
             dst = z_rows[:, first : first + K_PASS].rearrange("t (u p e) -> t u p e", u=2, e=2)
             per_block = P // PACK
             nc.scalar.copy(
                 out=dst[:, :, b0 * per_block : b1 * per_block, :],
-                in_=sums[s][v][:, b0 * P : b1 * P].rearrange("t (p u e) -> t u p e", u=2, e=2),
+                in_=src.rearrange("t (p u e) -> t u p e", u=2, e=2),
             )
 
         def turn_z(z_rows, s, v0, v1, bank):
             words = psum.tile([P, v1 - v0, 2, P], F32, name="words", tag=bank, bufs=1)
             for v in range(v0, v1):
                 for u in range(2):
-                    first = (s * HALVES + v) * K_PASS + u * (K_PASS // 2)
+                    first = v * K_PASS + u * (K_PASS // 2)
                     run = z_rows[:, first : first + K_PASS // 2].bitcast(F32)
                     nc.tensor.transpose(words[:, v - v0, u, :], run, ident[:])
             nc.scalar.copy(
@@ -288,7 +302,7 @@ def tile_picked_sage_relu_e_kernel(
             targets = slice(v * P, (v + 1) * P)
             nc.tensor.matmul_mx(
                 out=acc,
-                lhsT=w2_codes[s][:, cols].bitcast(FP8X4),
+                lhsT=w2_codes[s, m].bitcast(FP8X4),
                 lhsT_scale=w2_scales[s][:, cols],
                 rhs=z_codes[s][:, targets].bitcast(FP8X4),
                 rhs_scale=z_scales[s][:, targets],
@@ -319,11 +333,21 @@ def tile_picked_sage_relu_e_kernel(
                 interleave_w1(b + 2, 0)
                 h_next = relu(b + 1, f"w1_slot{b + 2}_0")
                 interleave_w1(b + 2, LAST)
-            else:
+            elif b < BLOCKS - 2:
                 interleave_w2(b - FIRST_W2_STEP)
                 h_next = relu(b + 1, f"w2_slot{b - FIRST_W2_STEP}")
+            else:
+                interleave_w2(SHARED_LOAD - 1)
+                z_rows0 = keep.tile(
+                    [P, HALVES * K_PASS], BF16, name="z_rows0", tag=f"w2_slot{SHARED_LOAD - 1}", align_bytes=64
+                )
+                for v in range(HALVES):
+                    round_z(z_rows0, 0, v, 0, PACK)
+                interleave_w2(SHARED_LOAD)
+                h_next = relu(b + 1, None)
             for d in range(1 if tight else 0, D):
-                gather(b, d, h, f"w1_slot{b + 1}_{LAST}" if tight and d == 1 else None)
+                held_by = f"w1_slot{b + 1}_{LAST}" if tight and d == 1 else None
+                gather(b, d, h, held_by)
             if b < 2:
                 quantize_w1_pass(b + 2, 0)
                 project(b + 2, 0)
@@ -333,51 +357,51 @@ def tile_picked_sage_relu_e_kernel(
                     for s in range(PASSES):
                         project(ahead, s)
             h = h_next
-        interleave_w2(len(W2_LOADS) - 1)
 
-        z_rows = keep.tile(
-            [P, PASSES * HALVES * K_PASS], BF16, name="z_rows", tag=f"w2_slot{len(W2_LOADS) - 1}", align_bytes=64
-        )
-        for v in range(HALVES):
-            round_z(z_rows, 0, v, 0, PACK)
+        z_rows = placed.tile([P, HALVES * K_PASS], BF16, name="z_rows1", offset=S * 4, align_bytes=64)
         for v in range(HALVES):
             round_z(z_rows, LAST, v, 0, PACK - 1)
-        turn_z(z_rows, 0, 0, HALVES, "last")
+        turn_z(z_rows0, 0, 0, HALVES, "last")
         for v in range(HALVES):
+            last_sums.append(psum.tile([P, P], F32, name="last_sums", tag=f"r{v}", bufs=1))
             gather_half(BLOCKS - 1, h, v)
             round_z(z_rows, LAST, v, PACK - 1, PACK)
-            turn_z(z_rows, LAST, v, v + 1, f"sums0_{v}")
-
-        quantize_w2(0)
-        z_codes[0] = keep.tile([P, V], U32, name="z_codes0", tag="gate1", align_bytes=64)
-        quantize_z(0, 0, HALVES)
-        ahead_banks = (f"sums{LAST}_1", "sums0_0", "sums0_1")
-        out_acc = []
-        for m, bank in enumerate(ahead_banks):
-            out_acc.append(psum.tile([P, P], F32, name="out_acc", tag=bank, bufs=1))
-            out_pass(out_acc[m][:], 0, m, 1, True)
-        quantize_w2(LAST)
-        z_codes[LAST] = keep.tile([P, V], U32, name="z_codes1", align_bytes=64)
-        for v in range(HALVES):
-            quantize_z(LAST, v, v + 1)
+            turn_z(z_rows, LAST, v, v + 1, f"sums0_{1 - v}")
 
         out_rows = out.rearrange("(m p) v -> p m v", p=P)
-        for pair, copy in enumerate((nc.scalar.copy, nc.vector.tensor_copy)):
-            acc = psum.tile([P, 2, P], F32, name="acc", tag=f"r{pair}", bufs=1)
-            for i in range(2):
-                out_pass(acc[:, i, :], LAST, 2 * pair + i, 0, True)
-                out_pass(acc[:, i, :], 0, 2 * pair + i, 0, False)
-            result = keep.tile([P, 2, P], F32, name=f"result0_{pair}")
-            copy(out=result[:], in_=acc[:])
-            nc.sync.dma_start(out=out_rows[:, 2 * pair : 2 * pair + 2, :P], in_=result[:])
+        out_acc = {}
+
+        def open_out(v, m, s, bank):
+            out_acc[v, m] = psum.tile([P, P], F32, name="out_acc", tag=bank, bufs=1)
+            out_pass(out_acc[v, m][:], s, m, v, True)
+
+        def close_out(v, m, s, copy):
+            out_pass(out_acc[v, m][:], s, m, v, False)
+            result = keep.tile([P, P], F32, name=f"result{v}_{m}")
+            copy(out=result[:], in_=out_acc[v, m][:])
+            nc.sync.dma_start(out=out_rows[:, m, v * P : (v + 1) * P], in_=result[:])
+
+        z_codes[0] = keep.tile([P, V], U32, name="z_codes0", tag="gate0", align_bytes=64)
+        quantize_z(0, 0, HALVES)
+        for m, slot in enumerate(("gate1", "tail")):
+            quantize_w2(0, m * P, (m + 1) * P, slot)
+            for v in range(HALVES):
+                open_out(v, m, 0, ("r2", "last", "sums1_0", "sums1_1")[2 * m + v])
+        quantize_w2(LAST, 0, N, "gate2")
+        z_codes[LAST] = keep.tile([P, V], U32, name="z_codes1", align_bytes=64)
+        quantize_z(LAST, 0, 1)
+        quantize_w2(0, N // 2, N, "gate3")
+        quantize_z(LAST, 1, 2)
+        for m in range(2):
+            close_out(0, m, LAST, nc.scalar.copy)
+        pair = psum.tile([P, 2, P], F32, name="pair", tag="r0", bufs=1)
+        for i in range(2):
+            out_pass(pair[:, i, :], LAST, 2 + i, 0, True)
+            out_pass(pair[:, i, :], 0, 2 + i, 0, False)
+        result = keep.tile([P, 2, P], F32, name="result_pair")
+        nc.vector.tensor_copy(out=result[:], in_=pair[:])
+        nc.sync.dma_start(out=out_rows[:, 2:, :P], in_=result[:])
+        for m, bank in ((2, "r1"), (3, "sums0_1")):
+            open_out(1, m, 0, bank)
         for m in range(M_TILES):
-            if m < len(ahead_banks):
-                out_pass(out_acc[m][:], LAST, m, 1, False)
-            else:
-                out_acc.append(psum.tile([P, P], F32, name="out_acc", tag=f"sums{LAST}_0", bufs=1))
-                out_pass(out_acc[m][:], LAST, m, 1, True)
-                out_pass(out_acc[m][:], 0, m, 1, False)
-            result = keep.tile([P, P], F32, name=f"result1_{m}")
-            copy = (nc.vector.tensor_copy, nc.scalar.copy)[m % 2]
-            copy(out=result[:], in_=out_acc[m][:])
-            nc.sync.dma_start(out=out_rows[:, m, P:], in_=result[:])
+            close_out(1, m, LAST, (nc.vector.tensor_copy, nc.scalar.copy)[m % 2])

@@ -260,8 +260,8 @@ def tile_picked_sage_relu_e_kernel(
 
         def gather_half(b, h, v):
             for d in range(D):
-                if (v, d) == (HALVES - 1, 0):
-                    prod = keep.tile([P, P], F32, name="prod_tail", tag="tail", align_bytes=64)
+                if v == HALVES - 1 and d < 2:
+                    prod = keep.tile([P, P], F32, name="prod_tail", tag=f"tail{d}", align_bytes=64)
                 else:
                     prod = prods.tile([P, P], F32, name="prod")
                 entries = pos_sb[d][:, v * P // LIST_COL : (v + 1) * P // LIST_COL]
@@ -383,25 +383,26 @@ def tile_picked_sage_relu_e_kernel(
 
         z_codes[0] = keep.tile([P, V], U32, name="z_codes0", tag="gate0", align_bytes=64)
         quantize_z(0, 0, HALVES)
-        for m, slot in enumerate(("gate1", "tail")):
+        for m, slot in enumerate(("gate1", "tail0")):
             quantize_w2(0, m * P, (m + 1) * P, slot)
             for v in range(HALVES):
                 open_out(v, m, 0, ("r2", "last", "sums1_0", "sums1_1")[2 * m + v])
-        quantize_w2(LAST, 0, N, "gate2")
+        quantize_w2(0, N // 2, N, "gate2")
+        for m, bank in ((2, "r1"), (3, "sums0_1")):
+            open_out(0, m, 0, bank)
+        quantize_w2(LAST, 0, N // 2, "gate3")
         z_codes[LAST] = keep.tile([P, V], U32, name="z_codes1", align_bytes=64)
         quantize_z(LAST, 0, 1)
-        quantize_w2(0, N // 2, N, "gate3")
+        quantize_w2(LAST, N // 2, N, "tail1")
         quantize_z(LAST, 1, 2)
         for m in range(2):
             close_out(0, m, LAST, nc.scalar.copy)
-        pair = psum.tile([P, 2, P], F32, name="pair", tag="r0", bufs=1)
-        for i in range(2):
-            out_pass(pair[:, i, :], LAST, 2 + i, 0, True)
-            out_pass(pair[:, i, :], 0, 2 + i, 0, False)
         result = keep.tile([P, 2, P], F32, name="result_pair")
-        nc.vector.tensor_copy(out=result[:], in_=pair[:])
+        for i, copy in enumerate((nc.vector.tensor_copy, nc.scalar.copy)):
+            out_pass(out_acc[0, 2 + i][:], LAST, 2 + i, 0, False)
+            copy(out=result[:, i, :], in_=out_acc[0, 2 + i][:])
         nc.sync.dma_start(out=out_rows[:, 2:, :P], in_=result[:])
-        for m, bank in ((2, "r1"), (3, "sums0_1")):
+        for m, bank in ((3, "sums0_0"), (2, "r2")):
             open_out(1, m, 0, bank)
         for m in range(M_TILES):
             close_out(1, m, LAST, (nc.vector.tensor_copy, nc.scalar.copy)[m % 2])

@@ -59,7 +59,8 @@ def tile_picked_sage_relu_e_kernel(
         ident = keep.tile([P, P], F32, name="ident")
         make_identity(nc, ident[:])
 
-        x_raw = [[keep.tile([P, T], F32, name=f"x_raw{s}_{j}") for j in range(PACK)] for s in range(PASSES)]
+        x_pairs = [keep.tile([P, 2, T], F32, name=f"x_pair{u}") for u in range(PACK // 2)]
+        x_raw = [keep.tile([P, T], F32, name=f"x_raw{j}", tag=f"x_slot{j}", align_bytes=64) for j in range(PACK)]
         w1_raw = [
             [
                 keep.tile([P, PACK, len(group) * P], F32, name=f"w1_raw{g}_{s}", tag=f"w1_slot{g}_{s}", align_bytes=64)
@@ -78,14 +79,14 @@ def tile_picked_sage_relu_e_kernel(
         gate_cols = keep.tile([P, HALVES, D], F32, name="gate_cols")
         gate_sb = [keep.tile([P, V], F32, name=f"gate_sb{d}", tag=f"gate{d}", align_bytes=64) for d in range(D)]
 
-        for s in range(PASSES):
-            rows = xT[s * K_PASS : (s + 1) * K_PASS, :].rearrange("(p j) t -> j p t", j=PACK)
-            for j in range(PACK):
-                nc.sync.dma_start(out=x_raw[s][j][:], in_=rows[j])
-                if (s, j) == (0, 0):
-                    nc.sync.dma_start(offs_sb[:], offs)
-                if (s, j) == (0, 1):
-                    nc.sync.dma_start(out=gate_rows[:D, :], in_=gate[:, 0, :])
+        rows = xT[:K_PASS, :].rearrange("(p j) t -> p j t", j=PACK)
+        nc.sync.dma_start(out=x_pairs[0][:], in_=rows[:, :2, :])
+        nc.sync.dma_start(offs_sb[:], offs)
+        nc.sync.dma_start(out=x_pairs[1][:], in_=rows[:, 2:, :])
+        nc.sync.dma_start(out=gate_rows[:D, :], in_=gate[:, 0, :])
+        rows = xT[K_PASS:, :].rearrange("(p j) t -> j p t", j=PACK)
+        for j in range(PACK):
+            nc.sync.dma_start(out=x_raw[j][:], in_=rows[j])
         for g, group in enumerate(W1_GROUPS):
             for s in range(PASSES):
                 cols = w1[s * K_PASS : (s + 1) * K_PASS, group[0] * P : (group[-1] + 1) * P]
@@ -158,7 +159,10 @@ def tile_picked_sage_relu_e_kernel(
                 nc.scalar.copy(out=gate_sb[d0 + r][:], in_=spread[:, r, :])
 
         x_il = [keep.tile([P, S, PACK], BF16, name=f"x_il{s}", align_bytes=64) for s in range(PASSES)]
-        x_codes = [keep.tile([P, S], U32, name=f"x_codes{s}", align_bytes=64) for s in range(PASSES)]
+        x_codes = [
+            keep.tile([P, S], U32, name="x_codes0", tag="x_slot1", align_bytes=64),
+            keep.tile([P, S], U32, name="x_codes1", align_bytes=64),
+        ]
         x_scales0 = keep.tile([P, S], U8, name="x_scales0", align_bytes=64)
         x_scales1 = []
 
@@ -170,7 +174,7 @@ def tile_picked_sage_relu_e_kernel(
 
         def gather_nodes(s, j, n0, n1):
             entries = offs_sb[:, n0 // LIST_COL : n1 // LIST_COL]
-            nc.vector.tensor_copy(x_il[s][:, n0:n1, j], x_raw[s][j][:].indirect(entries))
+            nc.vector.tensor_copy(x_il[s][:, n0:n1, j], x_raw[j][:].indirect(entries))
 
         def quantize_nodes(s, nodes):
             nc.vector.quantize_mx(
@@ -179,11 +183,14 @@ def tile_picked_sage_relu_e_kernel(
                 in_=x_il[s][:, nodes, :].rearrange("p t j -> p (t j)"),
             )
 
+        picked = keep.tile([P, PACK, S], F32, name="picked")
         for j in range(PACK):
-            gather_nodes(0, j, 0, S)
+            nc.vector.tensor_copy(picked[:, j, :], x_pairs[j // 2][:, j % 2, :].indirect(offs_sb[:]))
+        interleave(x_il[0][:], picked[:])
+        gather_nodes(LAST, 0, 0, S)
+        gather_nodes(LAST, 1, 0, S)
         quantize_nodes(0, slice(0, S))
-        for j in range(PACK - 1):
-            gather_nodes(LAST, j, 0, S)
+        gather_nodes(LAST, 2, 0, S)
         interleave_w1(0, 0)
         interleave_w1(0, LAST)
         gather_nodes(LAST, PACK - 1, 0, S)

@@ -160,7 +160,7 @@ def tile_picked_sage_relu_e_kernel(
 
         x_il = [keep.tile([P, S, PACK], BF16, name=f"x_il{s}", align_bytes=64) for s in range(PASSES)]
         x_codes = [
-            keep.tile([P, S], U32, name="x_codes0", tag="x_slot1", align_bytes=64),
+            keep.tile([P, S], U32, name="x_codes0", tag="x_slot0", align_bytes=64),
             keep.tile([P, S], U32, name="x_codes1", align_bytes=64),
         ]
         x_scales0 = keep.tile([P, S], U8, name="x_scales0", align_bytes=64)
@@ -184,12 +184,17 @@ def tile_picked_sage_relu_e_kernel(
             )
 
         picked = keep.tile([P, PACK, S], F32, name="picked")
-        for j in range(PACK):
-            nc.vector.tensor_copy(picked[:, j, :], x_pairs[j // 2][:, j % 2, :].indirect(offs_sb[:]))
-        interleave(x_il[0][:], picked[:])
+        for j in range(2):
+            nc.vector.tensor_copy(picked[:, j, :], x_pairs[0][:, j, :].indirect(offs_sb[:]))
+        for n0 in (0, S // 2):
+            nodes = slice(n0, n0 + S // 2)
+            entries = offs_sb[:, nodes.start // LIST_COL : nodes.stop // LIST_COL]
+            for j in range(2):
+                nc.vector.tensor_copy(picked[:, 2 + j, nodes], x_pairs[1][:, j, :].indirect(entries))
+            interleave(x_il[0][:, nodes, :], picked[:, :, nodes])
         gather_nodes(LAST, 0, 0, S)
-        gather_nodes(LAST, 1, 0, S)
         quantize_nodes(0, slice(0, S))
+        gather_nodes(LAST, 1, 0, S)
         gather_nodes(LAST, 2, 0, S)
         interleave_w1(0, 0)
         interleave_w1(0, LAST)
@@ -382,11 +387,12 @@ def tile_picked_sage_relu_e_kernel(
             out_acc[v, m] = psum.tile([P, P], F32, name="out_acc", tag=bank, bufs=1)
             out_pass(out_acc[v, m][:], s, m, v, True)
 
-        def close_out(v, m, s, copy):
-            out_pass(out_acc[v, m][:], s, m, v, False)
-            result = keep.tile([P, P], F32, name=f"result{v}_{m}")
-            copy(out=result[:], in_=out_acc[v, m][:])
-            nc.sync.dma_start(out=out_rows[:, m, v * P : (v + 1) * P], in_=result[:])
+        def close_pair(v, m0, copies):
+            result = keep.tile([P, 2, P], F32, name=f"result{v}_{m0}")
+            for i, copy in enumerate(copies):
+                out_pass(out_acc[v, m0 + i][:], LAST, m0 + i, v, False)
+                copy(out=result[:, i, :], in_=out_acc[v, m0 + i][:])
+            nc.sync.dma_start(out=out_rows[:, m0 : m0 + 2, v * P : (v + 1) * P], in_=result[:])
 
         z_codes[0] = keep.tile([P, V], U32, name="z_codes0", tag="gate0", align_bytes=64)
         quantize_z(0, 0, HALVES)
@@ -402,14 +408,9 @@ def tile_picked_sage_relu_e_kernel(
         quantize_z(LAST, 0, 1)
         quantize_w2(LAST, N // 2, N, "tail1")
         quantize_z(LAST, 1, 2)
-        for m in range(2):
-            close_out(0, m, LAST, nc.scalar.copy)
-        result = keep.tile([P, 2, P], F32, name="result_pair")
-        for i, copy in enumerate((nc.vector.tensor_copy, nc.scalar.copy)):
-            out_pass(out_acc[0, 2 + i][:], LAST, 2 + i, 0, False)
-            copy(out=result[:, i, :], in_=out_acc[0, 2 + i][:])
-        nc.sync.dma_start(out=out_rows[:, 2:, :P], in_=result[:])
+        close_pair(0, 0, (nc.scalar.copy, nc.scalar.copy))
+        close_pair(0, 2, (nc.vector.tensor_copy, nc.scalar.copy))
         for m, bank in ((3, "sums0_0"), (2, "r2")):
             open_out(1, m, 0, bank)
-        for m in range(M_TILES):
-            close_out(1, m, LAST, (nc.vector.tensor_copy, nc.scalar.copy)[m % 2])
+        for m0 in (0, 2):
+            close_pair(1, m0, (nc.vector.tensor_copy, nc.scalar.copy))

@@ -30,7 +30,7 @@ ACC_BANKS = (
     ("sums0_0", "sums0_1", "sums1_0", "sums1_1"),
     ("r0", "r1"),
     ("r2", "last"),
-    ("r0", "r1"),
+    ("r0",),
     ("r2",),
     ("r0",),
     ("r1",),
@@ -112,8 +112,8 @@ def tile_picked_sage_relu_e_kernel(
                 out=dst.rearrange("p (c i) j -> p c j i", i=RUN), in_=src.rearrange("p j (c i) -> p c j i", i=RUN)
             )
 
-        def interleave_w1(g, s):
-            for i, b in enumerate(W1_GROUPS[g]):
+        def interleave_w1(g, s, members=slice(None)):
+            for i, b in list(enumerate(W1_GROUPS[g]))[members]:
                 interleave(w1_il[b][:, s], w1_raw[g][s][:, :, i * P : (i + 1) * P])
 
         def interleave_w2(c):
@@ -334,14 +334,19 @@ def tile_picked_sage_relu_e_kernel(
         interleave_w1(1, LAST)
         open_sums(0)
         for b in range(BLOCKS - 1):
-            tight = b < 3
+            tight = b < 2
             if b == PACK:
                 open_sums(LAST)
             if tight:
                 gather(b, 0, h)
                 quantize_w1_pass(b + 1, LAST)
                 project(b + 1, LAST)
-            if b < FIRST_W2_STEP:
+            if b == 1:
+                interleave_w1(3, 0)
+                interleave_w1(3, LAST, slice(0, 1))
+                h_next = relu(2, "w1_slot3_0")
+                interleave_w1(3, LAST, slice(1, 2))
+            elif b < FIRST_W2_STEP:
                 interleave_w1(b + 2, 0)
                 h_next = relu(b + 1, f"w1_slot{b + 2}_0")
                 interleave_w1(b + 2, LAST)
@@ -360,14 +365,14 @@ def tile_picked_sage_relu_e_kernel(
             for d in range(1 if tight else 0, D):
                 held_by = f"w1_slot{b + 1}_{LAST}" if tight and d == 1 else None
                 gather(b, d, h, held_by)
-            if b < 2:
-                quantize_w1_pass(b + 2, 0)
-                project(b + 2, 0)
-            else:
-                for ahead in {2: (4,), 3: (5, 6), 4: (7,)}.get(b, ()):
-                    quantize_w1(ahead)
-                    for s in range(PASSES):
-                        project(ahead, s)
+                if d == D - 2:
+                    for ahead in {1: (3,), 2: (4,), 3: (5, 6), 4: (7,)}.get(b, ()):
+                        quantize_w1(ahead)
+                        for s in range(PASSES):
+                            project(ahead, s)
+            if b == 0:
+                quantize_w1_pass(2, 0)
+                project(2, 0)
             h = h_next
 
         z_rows = placed.tile([P, HALVES * K_PASS], BF16, name="z_rows1", offset=S * 4, align_bytes=64)

@@ -11,9 +11,9 @@ PASSES = K // K_PASS
 LAST = PASSES - 1
 BLOCKS = H // P
 HALVES = V // P
-M_TILES = N // P
+PAIRS = D // 2
 LIST_COL = 16
-RUN = 4
+HALF_PAIR = V * 4
 FLOPS = 2 * S * K * H + 2 * V * H * N + 2 * D * V * H
 
 F32 = mybir.dt.float32
@@ -23,23 +23,15 @@ U16 = mybir.dt.uint16
 U8 = mybir.dt.uint8
 FP8X4 = mybir.dt.float8_e4m3fn_x4
 RELU = mybir.ActivationFunctionType.Relu
+COPY = mybir.ActivationFunctionType.Copy
 MULT = mybir.AluOpType.mult
+ADD = mybir.AluOpType.add
 
 W1_GROUPS = ((0,), (1,), (2,), (3, 4), (5, 6), (7,))
-ACC_BANKS = (
-    ("sums0_0", "sums0_1", "sums1_0", "sums1_1"),
-    ("r0", "r1"),
-    ("r2", "last"),
-    ("r0",),
-    ("r2",),
-    ("r0",),
-    ("r1",),
-    ("last",),
-)
-W2_COLS = N // 2
-W2_LOADS = [(s, n0) for s in range(PASSES) for n0 in range(0, N, W2_COLS)]
-SHARED_LOAD = 3
-FIRST_W2_STEP = BLOCKS - len(W2_LOADS)
+SCALAR_BLOCKS = 2
+ACC_BANKS = (("a", "b", "c", "d"), ("h0", "h1"), ("c",), ("d",), ("h0",), ("h1",), ("h0",), ("h1",))
+SUM_BANKS = (("a", "b"), ("c", "d"))
+VECTOR_TURNS = (2, 1, 1, 1, 2, 2, 1, 2)
 
 
 def tile_picked_sage_relu_e_kernel(
@@ -50,7 +42,9 @@ def tile_picked_sage_relu_e_kernel(
         lists = ctx.enter_context(tc.tile_pool(name="lists", bufs=1))
         keep = ctx.enter_context(tc.tile_pool(name="keep", bufs=1))
         placed = ctx.enter_context(tc.tile_pool(name="placed", bufs=1))
-        prods = ctx.enter_context(tc.tile_pool(name="prods", bufs=(BLOCKS + 1) * D))
+        regions = ctx.enter_context(tc.tile_pool(name="regions", bufs=1))
+        hidden = ctx.enter_context(tc.tile_pool(name="hidden", bufs=4))
+        fetched = ctx.enter_context(tc.tile_pool(name="fetched", bufs=3))
         psum = ctx.enter_context(tc.psum_pool(name="psum", bufs=1))
 
         offs_sb = lists.tile([P, S // LIST_COL], U16, name="offs_sb")
@@ -68,16 +62,10 @@ def tile_picked_sage_relu_e_kernel(
             ]
             for g, group in enumerate(W1_GROUPS)
         ]
-        w2_raw = [
-            placed.tile([P, PACK, W2_COLS], F32, name="w2_shared", offset=0, align_bytes=64)
-            if c == SHARED_LOAD
-            else keep.tile([P, PACK, W2_COLS], F32, name=f"w2_raw{c}", tag=f"w2_slot{c}", align_bytes=64)
-            for c in range(len(W2_LOADS))
-        ]
+        w2_raw = [keep.tile([P, PACK, N], F32, name=f"w2_raw{s}", align_bytes=64) for s in range(PASSES)]
         gate_rows = keep.tile([P, V], F32, name="gate_rows")
         nc.gpsimd.memset(gate_rows[:], 0.0)
         gate_cols = keep.tile([P, HALVES, D], F32, name="gate_cols")
-        gate_sb = [keep.tile([P, V], F32, name=f"gate_sb{d}", tag=f"gate{d}", align_bytes=64) for d in range(D)]
 
         rows = xT[:K_PASS, :].rearrange("(p j) t -> p j t", j=PACK)
         nc.sync.dma_start(out=x_pairs[0][:], in_=rows[:, :2, :])
@@ -96,30 +84,33 @@ def tile_picked_sage_relu_e_kernel(
             if g == 1:
                 for d, pos in ((1, pos2), (2, pos3), (3, pos4)):
                     nc.sync.dma_start(pos_sb[d][:], pos)
-        for c, (s, n0) in enumerate(W2_LOADS):
-            cols = w2[s * K_PASS : (s + 1) * K_PASS, n0 : n0 + W2_COLS]
-            nc.sync.dma_start(out=w2_raw[c][:], in_=cols.rearrange("(p j) n -> p j n", j=PACK))
+        for s in range(PASSES):
+            rows = w2[s * K_PASS : (s + 1) * K_PASS, :]
+            nc.sync.dma_start(out=w2_raw[s][:], in_=rows.rearrange("(p j) n -> p j n", j=PACK))
 
-        w1_il = [keep.tile([P, PASSES, P, PACK], BF16, name=f"w1_il{b}", align_bytes=64) for b in range(BLOCKS)]
-        w1_codes = [keep.tile([P, PASSES, P], U32, name=f"w1_codes{b}", align_bytes=64) for b in range(BLOCKS)]
-        w1_scales = [keep.tile([P, PASSES, P], U8, name=f"w1_scales{b}", align_bytes=64) for b in range(BLOCKS)]
+        w1_il = [
+            regions.tile([P, PASSES, P, PACK], BF16, name=f"w1_il{b}", offset=(4 * b + 1) * HALF_PAIR, align_bytes=64)
+            for b in range(BLOCKS)
+        ]
+        w1_codes = [keep.tile([P, PASSES, P], U32, name="w1_codes", tag=f"codes{b}", align_bytes=64) for b in range(BLOCKS)]
+        w1_scales = [keep.tile([P, PASSES, P], U8, name="w1_scales", tag=f"scales{b}", align_bytes=64) for b in range(BLOCKS)]
         w2_il = [keep.tile([P, N, PACK], BF16, name=f"w2_il{s}", align_bytes=64) for s in range(PASSES)]
-        w2_codes = {}
-        w2_scales = [keep.tile([P, N], U8, name=f"w2_scales{s}", align_bytes=64) for s in range(PASSES)]
+        w2_codes = [keep.tile([P, N], U32, name=f"w2_codes{s}", align_bytes=64) for s in range(PASSES)]
+        w2_scales = {}
 
-        def interleave(dst, src):
+        def interleave_on_scalar(dst, src):
             nc.scalar.copy(
-                out=dst.rearrange("p (c i) j -> p c j i", i=RUN), in_=src.rearrange("p j (c i) -> p c j i", i=RUN)
+                out=dst.rearrange("p (c i) j -> p c j i", i=4), in_=src.rearrange("p j (c i) -> p c j i", i=4)
             )
 
-        def interleave_w1(g, s, members=slice(None)):
-            for i, b in list(enumerate(W1_GROUPS[g]))[members]:
-                interleave(w1_il[b][:, s], w1_raw[g][s][:, :, i * P : (i + 1) * P])
+        def interleave_on_gpsimd(dst, src):
+            nc.gpsimd.tensor_scalar(dst, src.rearrange("p j c -> p c j"), 1.0, 0.0, MULT, ADD)
 
-        def interleave_w2(c):
-            s, n0 = W2_LOADS[c]
-            for n in range(0, W2_COLS, P):
-                interleave(w2_il[s][:, n0 + n : n0 + n + P, :], w2_raw[c][:, :, n : n + P])
+        def interleave_w1(b, s):
+            g = [b in group for group in W1_GROUPS].index(True)
+            i = b - W1_GROUPS[g][0]
+            move = interleave_on_scalar if b < SCALAR_BLOCKS else interleave_on_gpsimd
+            move(w1_il[b][:, s], w1_raw[g][s][:, :, i * P : (i + 1) * P])
 
         def quantize_w1(b):
             nc.vector.quantize_mx(
@@ -135,28 +126,25 @@ def tile_picked_sage_relu_e_kernel(
                 in_=w1_il[b][:, s].rearrange("p m j -> p (m j)"),
             )
 
-        def quantize_w2(s, n0, n1, slot):
-            codes = keep.tile([P, n1 - n0], U32, name="w2_codes", tag=slot, align_bytes=64)
+        def quantize_w2(s, n0, n1, scales):
             for n in range(n0, n1, P):
-                w2_codes[s, n // P] = codes[:, n - n0 : n - n0 + P]
+                w2_scales[s, n // P] = scales[:, n - n0 : n - n0 + P]
             nc.vector.quantize_mx(
-                out=codes[:].bitcast(FP8X4),
-                scales=w2_scales[s][:, n0:n1],
+                out=w2_codes[s][:, n0:n1].bitcast(FP8X4),
+                scales=scales[:],
                 in_=w2_il[s][:, n0:n1, :].rearrange("p n j -> p (n j)"),
             )
 
-        spread = psum.tile([P, HALVES, P], F32, name="spread", tag="r0", bufs=1)
+        turned = psum.tile([P, HALVES, P], F32, name="turned", tag="a")
         for v in range(HALVES):
-            nc.tensor.transpose(spread[:, v, :], gate_rows[:, v * P : (v + 1) * P], ident[:])
-        nc.scalar.copy(out=gate_cols[:], in_=spread[:, :, :D])
-        for d0 in range(0, D, 2):
-            spread = psum.tile([P, 2, V], F32, name="spread", tag=f"r{1 + d0 // 2}", bufs=1)
+            nc.tensor.transpose(turned[:, v, :], gate_rows[:, v * P : (v + 1) * P], ident[:])
+        nc.scalar.copy(out=gate_cols[:], in_=turned[:, :, :D])
+        gate_ps = [psum.tile([P, 2, V], F32, name="gate_ps", tag=f"g{q}") for q in range(PAIRS)]
+        for q in range(PAIRS):
             for r in range(2):
                 for v in range(HALVES):
-                    column = gate_cols[:, v, d0 + r : d0 + r + 1]
-                    nc.tensor.transpose(spread[:, r, v * P : (v + 1) * P], column.to_broadcast([P, P]), ident[:])
-            for r in range(2):
-                nc.scalar.copy(out=gate_sb[d0 + r][:], in_=spread[:, r, :])
+                    column = gate_cols[:, v, 2 * q + r : 2 * q + r + 1]
+                    nc.tensor.transpose(gate_ps[q][:, r, v * P : (v + 1) * P], column.to_broadcast([P, P]), ident[:])
 
         x_il = [keep.tile([P, S, PACK], BF16, name=f"x_il{s}", align_bytes=64) for s in range(PASSES)]
         x_codes = [
@@ -171,10 +159,6 @@ def tile_picked_sage_relu_e_kernel(
                 return x_scales0[:, nodes]
             half = nodes.start // (S // 2)
             return x_scales1[half][:, nodes.start - half * (S // 2) : nodes.stop - half * (S // 2)]
-
-        def gather_nodes(s, j, n0, n1):
-            entries = offs_sb[:, n0 // LIST_COL : n1 // LIST_COL]
-            nc.vector.tensor_copy(x_il[s][:, n0:n1, j], x_raw[j][:].indirect(entries))
 
         def quantize_nodes(s, nodes):
             nc.vector.quantize_mx(
@@ -191,14 +175,13 @@ def tile_picked_sage_relu_e_kernel(
             entries = offs_sb[:, nodes.start // LIST_COL : nodes.stop // LIST_COL]
             for j in range(2):
                 nc.vector.tensor_copy(picked[:, 2 + j, nodes], x_pairs[1][:, j, :].indirect(entries))
-            interleave(x_il[0][:, nodes, :], picked[:, :, nodes])
-        gather_nodes(LAST, 0, 0, S)
-        quantize_nodes(0, slice(0, S))
-        gather_nodes(LAST, 1, 0, S)
-        gather_nodes(LAST, 2, 0, S)
+            interleave_on_scalar(x_il[0][:, nodes, :], picked[:, :, nodes])
+        for j in range(PACK):
+            nc.vector.tensor_copy(x_il[LAST][:, :, j], x_raw[j][:].indirect(offs_sb[:]))
+            if j == 0:
+                quantize_nodes(0, slice(0, S))
         interleave_w1(0, 0)
         interleave_w1(0, LAST)
-        gather_nodes(LAST, PACK - 1, 0, S)
         quantize_w1_pass(0, 0)
         x_scales1.append(keep.tile([P, S // 2], U8, name="x_scales1", tag="w1_slot0_0", align_bytes=64))
         quantize_nodes(LAST, slice(0, 2 * P))
@@ -215,9 +198,7 @@ def tile_picked_sage_relu_e_kernel(
 
         def project(b, s):
             if s == 0:
-                accs[b] = [
-                    psum.tile([P, S // len(ACC_BANKS[b])], F32, name="acc", tag=bank, bufs=1) for bank in ACC_BANKS[b]
-                ]
+                accs[b] = [psum.tile([P, S // len(ACC_BANKS[b])], F32, name="acc", tag=bank) for bank in ACC_BANKS[b]]
             for acc, nodes in zip(accs[b], pieces(b)):
                 width = nodes.stop - nodes.start
                 step = width if s == 0 else min(width, S // 2)
@@ -233,11 +214,11 @@ def tile_picked_sage_relu_e_kernel(
                         stop=(s == LAST and n0 + step == width),
                     )
 
-        def relu(b, slot):
+        def relu(b, slot=None):
             if slot:
-                h = keep.tile([P, S], F32, name="h", tag=slot, align_bytes=64)
+                h = keep.tile([P, S], F32, name="h_held", tag=slot, align_bytes=64)
             else:
-                h = placed.tile([P, S], F32, name="h_last", offset=0, align_bytes=64)
+                h = hidden.tile([P, S], F32, name="h")
             for i, (acc, nodes) in enumerate(zip(accs[b], pieces(b))):
                 if b == 0 and i % 2 == 0:
                     nc.vector.tensor_relu(h[:, nodes], acc[:])
@@ -248,37 +229,54 @@ def tile_picked_sage_relu_e_kernel(
         sums = {}
         last_sums = []
         z_il = [keep.tile([P, V * PACK], BF16, name=f"z_il{s}", align_bytes=64) for s in range(PASSES)]
-        z_codes = {}
-        z_scales = [keep.tile([P, V], U8, name=f"z_scales{s}", align_bytes=64) for s in range(PASSES)]
+        z_codes = [keep.tile([P, V], U32, name=f"z_codes{s}", align_bytes=64) for s in range(PASSES)]
+        z_scales = {}
 
-        def add_transposed(b, d, v, prod):
-            nc.tensor.matmul(
-                last_sums[v][:] if b == BLOCKS - 1 else sums[b // PACK][v][:, (b % PACK) * P : (b % PACK + 1) * P],
-                prod,
-                ident[:],
-                start=(d == 0),
-                stop=(d == D - 1),
-                is_transpose=True,
-            )
-
-        def gather(b, d, h, held_by=None):
-            if held_by:
-                prod = keep.tile([P, V], F32, name="prod_held", tag=held_by, align_bytes=64)
+        def gather(b, d, h, dst, targets):
+            entries = pos_sb[d][:, targets.start // LIST_COL : targets.stop // LIST_COL]
+            if d < VECTOR_TURNS[b]:
+                nc.vector.tensor_copy(dst, h[:].indirect(entries))
             else:
-                prod = prods.tile([P, V], F32, name="prod")
-            nc.vector.tensor_tensor(prod[:], h[:].indirect(pos_sb[d][:]), gate_sb[d][:], MULT)
-            for v in range(HALVES):
-                add_transposed(b, d, v, prod[:, v * P : (v + 1) * P])
+                nc.scalar.activation(dst, h[:].indirect(entries), COPY)
 
-        def gather_half(b, h, v):
+        def add_transposed(acc, d, prod):
+            nc.tensor.matmul(acc, prod, ident[:], start=(d == 0), stop=(d == D - 1), is_transpose=True)
+
+        def aggregate(b, h):
+            if b == 0:
+                pairs = [fetched.tile([P, 2, V], F32, name="pair") for q in range(PAIRS)]
+            else:
+                slots = (f"codes{b + 1}", f"scales{b + 1}")
+                pairs = [keep.tile([P, 2, V], F32, name="pair", tag=slot, align_bytes=64) for slot in slots]
             for d in range(D):
-                if v == HALVES - 1 and d < 2:
-                    prod = keep.tile([P, P], F32, name="prod_tail", tag=f"tail{d}", align_bytes=64)
+                gather(b, d, h, pairs[d // 2][:, d % 2, :], slice(0, V))
+            for q, pair in enumerate(pairs):
+                prod = pair
+                ahead = b + 2 + (q if b > 0 else 0)
+                if ahead < BLOCKS and (b, q) != (0, 1):
+                    first = (4 * ahead + 2 * q) * HALF_PAIR
+                    prod = regions.tile([P, 2, V], F32, name=f"prod{b}_{q}", offset=first, align_bytes=64)
+                nc.vector.tensor_tensor(prod[:], pair[:], gate_ps[q][:], MULT)
+                for v in range(HALVES):
+                    acc = sums[b // PACK][v][:, (b % PACK) * P : (b % PACK + 1) * P]
+                    for r in range(2):
+                        add_transposed(acc, 2 * q + r, prod[:, r, v * P : (v + 1) * P])
+
+        def aggregate_half(b, h, v):
+            targets = slice(v * P, (v + 1) * P)
+            pairs = []
+            for q in range(PAIRS):
+                if (v, q) == (HALVES - 1, PAIRS - 1):
+                    pairs.append(placed.tile([P, 2, P], F32, name="last_pair", offset=0, align_bytes=64))
                 else:
-                    prod = prods.tile([P, P], F32, name="prod")
-                entries = pos_sb[d][:, v * P // LIST_COL : (v + 1) * P // LIST_COL]
-                nc.vector.tensor_tensor(prod[:], h[:].indirect(entries), gate_sb[d][:, v * P : (v + 1) * P], MULT)
-                add_transposed(b, d, v, prod[:])
+                    pairs.append(fetched.tile([P, 2, P], F32, name="pair"))
+            for d in range(D):
+                gather(b, d, h, pairs[d // 2][:, d % 2, :], targets)
+            for q, pair in enumerate(pairs):
+                prod = keep.tile([P, 2, P], F32, name="prod", tag=f"prod{v}_{q}", align_bytes=64)
+                nc.vector.tensor_tensor(prod[:], pair[:], gate_ps[q][:, :, targets], MULT)
+                for r in range(2):
+                    add_transposed(last_sums[v][:], 2 * q + r, prod[:, r, :])
 
         def round_z(z_rows, s, v, b0, b1):
             first = v * K_PASS
@@ -291,7 +289,7 @@ def tile_picked_sage_relu_e_kernel(
             )
 
         def turn_z(z_rows, s, v0, v1, bank):
-            words = psum.tile([P, v1 - v0, 2, P], F32, name="words", tag=bank, bufs=1)
+            words = psum.tile([P, v1 - v0, 2, P], F32, name="words", tag=bank)
             for v in range(v0, v1):
                 for u in range(2):
                     first = v * K_PASS + u * (K_PASS // 2)
@@ -310,12 +308,11 @@ def tile_picked_sage_relu_e_kernel(
             )
 
         def out_pass(acc, s, m, v, start):
-            cols = slice(m * P, (m + 1) * P)
             targets = slice(v * P, (v + 1) * P)
             nc.tensor.matmul_mx(
                 out=acc,
-                lhsT=w2_codes[s, m].bitcast(FP8X4),
-                lhsT_scale=w2_scales[s][:, cols],
+                lhsT=w2_codes[s][:, m * P : (m + 1) * P].bitcast(FP8X4),
+                lhsT_scale=w2_scales[s, m],
                 rhs=z_codes[s][:, targets].bitcast(FP8X4),
                 rhs_scale=z_scales[s][:, targets],
                 start=start,
@@ -323,7 +320,7 @@ def tile_picked_sage_relu_e_kernel(
             )
 
         def open_sums(s):
-            sums[s] = [psum.tile([P, K_PASS], F32, name="sums", tag=f"sums{s}_{v}", bufs=1) for v in range(HALVES)]
+            sums[s] = [psum.tile([P, K_PASS], F32, name="sums", tag=bank) for bank in SUM_BANKS[s]]
 
         project(0, 0)
         project(0, LAST)
@@ -332,65 +329,50 @@ def tile_picked_sage_relu_e_kernel(
         h = relu(0, "w1_slot1_0")
         project(1, 0)
         interleave_w1(1, LAST)
-        open_sums(0)
+        quantize_w1_pass(1, LAST)
+        project(1, LAST)
+        z_rows = [keep.tile([P, HALVES * K_PASS], BF16, name=f"z_rows{s}", align_bytes=64) for s in range(PASSES)]
         for b in range(BLOCKS - 1):
-            tight = b < 2
-            if b == PACK:
-                open_sums(LAST)
-            if tight:
-                gather(b, 0, h)
-                quantize_w1_pass(b + 1, LAST)
-                project(b + 1, LAST)
-            if b == 1:
-                interleave_w1(3, 0)
-                interleave_w1(3, LAST, slice(0, 1))
-                h_next = relu(2, "w1_slot3_0")
-                interleave_w1(3, LAST, slice(1, 2))
-            elif b < FIRST_W2_STEP:
-                interleave_w1(b + 2, 0)
-                h_next = relu(b + 1, f"w1_slot{b + 2}_0")
-                interleave_w1(b + 2, LAST)
-            elif b < BLOCKS - 2:
-                interleave_w2(b - FIRST_W2_STEP)
-                h_next = relu(b + 1, f"w2_slot{b - FIRST_W2_STEP}")
-            else:
-                interleave_w2(SHARED_LOAD - 1)
-                z_rows0 = keep.tile(
-                    [P, HALVES * K_PASS], BF16, name="z_rows0", tag=f"w2_slot{SHARED_LOAD - 1}", align_bytes=64
-                )
-                for v in range(HALVES):
-                    round_z(z_rows0, 0, v, 0, PACK)
-                interleave_w2(SHARED_LOAD)
-                h_next = relu(b + 1, None)
-            for d in range(1 if tight else 0, D):
-                held_by = f"w1_slot{b + 1}_{LAST}" if tight and d == 1 else None
-                gather(b, d, h, held_by)
-                if d == D - 2:
-                    for ahead in {1: (3,), 2: (4,), 3: (5, 6), 4: (7,)}.get(b, ()):
-                        quantize_w1(ahead)
-                        for s in range(PASSES):
-                            project(ahead, s)
+            if b % PACK == 0:
+                open_sums(b // PACK)
+            for ahead in {0: (2,), 1: (3, 4)}.get(b, (b + 3,)):
+                if ahead < BLOCKS:
+                    for s in range(PASSES):
+                        interleave_w1(ahead, s)
+                    quantize_w1(ahead)
+            if b + 2 < BLOCKS:
+                for s in range(PASSES):
+                    project(b + 2, s)
+            elif b + 2 == BLOCKS:
+                for s in range(PASSES):
+                    for n0 in range(0, N, N // 2):
+                        interleave_on_gpsimd(w2_il[s][:, n0 : n0 + N // 2, :], w2_raw[s][:, :, n0 : n0 + N // 2])
             if b == 0:
-                quantize_w1_pass(2, 0)
-                project(2, 0)
-            h = h_next
+                aggregate(b, h)
+                h = relu(1)
+            else:
+                h_next = relu(b + 1)
+                aggregate(b, h)
+                h = h_next
+            if b in (PACK, PACK + 1):
+                round_z(z_rows[0], 0, b - PACK, 0, PACK)
+        turn_z(z_rows[0], 0, 0, HALVES, "a")
 
-        z_rows = placed.tile([P, HALVES * K_PASS], BF16, name="z_rows1", offset=S * 4, align_bytes=64)
+        for v, bank in enumerate(("b", "h0")):
+            last_sums.append(psum.tile([P, P], F32, name="last_sums", tag=bank))
+            aggregate_half(BLOCKS - 1, h, v)
         for v in range(HALVES):
-            round_z(z_rows, LAST, v, 0, PACK - 1)
-        turn_z(z_rows0, 0, 0, HALVES, "last")
-        for v in range(HALVES):
-            last_sums.append(psum.tile([P, P], F32, name="last_sums", tag=f"r{v}", bufs=1))
-            gather_half(BLOCKS - 1, h, v)
-            round_z(z_rows, LAST, v, PACK - 1, PACK)
-            turn_z(z_rows, LAST, v, v + 1, f"sums0_{1 - v}")
+            round_z(z_rows[LAST], LAST, v, 0, PACK - 1)
+        for v, bank in enumerate(("a", "h1")):
+            round_z(z_rows[LAST], LAST, v, PACK - 1, PACK)
+            turn_z(z_rows[LAST], LAST, v, v + 1, bank)
 
         out_rows = out.rearrange("(m p) v -> p m v", p=P)
         out_acc = {}
 
-        def open_out(v, m, s, bank):
-            out_acc[v, m] = psum.tile([P, P], F32, name="out_acc", tag=bank, bufs=1)
-            out_pass(out_acc[v, m][:], s, m, v, True)
+        def open_out(v, m, bank):
+            out_acc[v, m] = psum.tile([P, P], F32, name="out_acc", tag=bank)
+            out_pass(out_acc[v, m][:], 0, m, v, True)
 
         def close_pair(v, m0, copies):
             result = keep.tile([P, 2, P], F32, name=f"result{v}_{m0}")
@@ -399,23 +381,26 @@ def tile_picked_sage_relu_e_kernel(
                 copy(out=result[:, i, :], in_=out_acc[v, m0 + i][:])
             nc.sync.dma_start(out=out_rows[:, m0 : m0 + 2, v * P : (v + 1) * P], in_=result[:])
 
-        z_codes[0] = keep.tile([P, V], U32, name="z_codes0", tag="gate0", align_bytes=64)
+        def held_scales(name, first, width):
+            return placed.tile([P, width], U8, name=name, offset=first, align_bytes=64)
+
+        z_scales[0] = held_scales("z_scales0", 0, V)
         quantize_z(0, 0, HALVES)
-        for m, slot in enumerate(("gate1", "tail0")):
-            quantize_w2(0, m * P, (m + 1) * P, slot)
+        for m in range(2):
+            quantize_w2(0, m * P, (m + 1) * P, held_scales(f"w2_scales0_{m}", V + m * P, P))
             for v in range(HALVES):
-                open_out(v, m, 0, ("r2", "last", "sums1_0", "sums1_1")[2 * m + v])
-        quantize_w2(0, N // 2, N, "gate2")
-        for m, bank in ((2, "r1"), (3, "sums0_1")):
-            open_out(0, m, 0, bank)
-        quantize_w2(LAST, 0, N // 2, "gate3")
-        z_codes[LAST] = keep.tile([P, V], U32, name="z_codes1", align_bytes=64)
+                open_out(v, m, ("g0", "g1", "c", "d")[2 * m + v])
+        quantize_w2(0, N // 2, N, held_scales("w2_scales0_2", 2 * V, V))
+        for m, bank in ((2, "h0"), (3, "a")):
+            open_out(0, m, bank)
+        quantize_w2(LAST, 0, N // 2, held_scales("w2_scales1_0", 3 * V, V))
+        z_scales[LAST] = keep.tile([P, V], U8, name="z_scales1", align_bytes=64)
         quantize_z(LAST, 0, 1)
-        quantize_w2(LAST, N // 2, N, "tail1")
+        quantize_w2(LAST, N // 2, N, keep.tile([P, V], U8, name="w2_scales1_2", tag="prod1_0", align_bytes=64))
         quantize_z(LAST, 1, 2)
         close_pair(0, 0, (nc.scalar.copy, nc.scalar.copy))
         close_pair(0, 2, (nc.vector.tensor_copy, nc.scalar.copy))
-        for m, bank in ((3, "sums0_0"), (2, "r2")):
-            open_out(1, m, 0, bank)
+        for m, bank in ((3, "h1"), (2, "g0")):
+            open_out(1, m, bank)
         for m0 in (0, 2):
             close_pair(1, m0, (nc.vector.tensor_copy, nc.scalar.copy))

@@ -13,7 +13,7 @@ BLOCKS = H // P
 HALVES = V // P
 PAIRS = D // 2
 LIST_COL = 16
-HALF_PAIR = V * 4
+OVERLAP = 64
 FLOPS = 2 * S * K * H + 2 * V * H * N + 2 * D * V * H
 
 F32 = mybir.dt.float32
@@ -27,11 +27,12 @@ COPY = mybir.ActivationFunctionType.Copy
 MULT = mybir.AluOpType.mult
 ADD = mybir.AluOpType.add
 
-W1_GROUPS = ((0,), (1,), (2,), (3, 4), (5, 6), (7,))
-SCALAR_BLOCKS = 2
-ACC_BANKS = (("a", "b", "c", "d"), ("h0", "h1"), ("c",), ("d",), ("h0",), ("h1",), ("h0",), ("h1",))
+W1_GROUPS = ((0,), (1,), (2,), (3, 4), (5, 6, 7))
+LATE = len(W1_GROUPS) - 1
+FUSED_BLOCKS = 2
+ACC_BANKS = (("a", "b", "c", "d"), ("h0", "h1"), ("c", "d"), ("h0",), ("h1",), ("h0",), ("h1",), ("h0",))
 SUM_BANKS = (("a", "b"), ("c", "d"))
-VECTOR_TURNS = (2, 1, 1, 1, 2, 2, 1, 2)
+VECTOR_SHARE = {2: 128, 3: 0, 4: 128, 5: 256, 6: 256}
 
 
 def tile_picked_sage_relu_e_kernel(
@@ -43,8 +44,10 @@ def tile_picked_sage_relu_e_kernel(
         keep = ctx.enter_context(tc.tile_pool(name="keep", bufs=1))
         placed = ctx.enter_context(tc.tile_pool(name="placed", bufs=1))
         regions = ctx.enter_context(tc.tile_pool(name="regions", bufs=1))
+        raws = ctx.enter_context(tc.tile_pool(name="raws", bufs=1))
         hidden = ctx.enter_context(tc.tile_pool(name="hidden", bufs=4))
-        fetched = ctx.enter_context(tc.tile_pool(name="fetched", bufs=3))
+        fetched = ctx.enter_context(tc.tile_pool(name="fetched", bufs=6))
+        prods = ctx.enter_context(tc.tile_pool(name="prods", bufs=6))
         psum = ctx.enter_context(tc.psum_pool(name="psum", bufs=1))
 
         offs_sb = lists.tile([P, S // LIST_COL], U16, name="offs_sb")
@@ -57,11 +60,13 @@ def tile_picked_sage_relu_e_kernel(
         x_raw = [keep.tile([P, T], F32, name=f"x_raw{j}", tag=f"x_slot{j}", align_bytes=64) for j in range(PACK)]
         w1_raw = [
             [
-                keep.tile([P, PACK, len(group) * P], F32, name=f"w1_raw{g}_{s}", tag=f"w1_slot{g}_{s}", align_bytes=64)
+                keep.tile([P, PACK, len(group) * P], F32, name="w1_raw", tag=f"w1_slot{g}_{s}", align_bytes=64)
                 for s in range(PASSES)
             ]
-            for g, group in enumerate(W1_GROUPS)
+            for g, group in enumerate(W1_GROUPS[:LATE])
         ]
+        late_cols = len(W1_GROUPS[LATE]) * P
+        late_raw = raws.tile([P, PASSES, PACK, late_cols], F32, name="late_raw", offset=0, align_bytes=64)
         w2_raw = [keep.tile([P, PACK, N], F32, name=f"w2_raw{s}", align_bytes=64) for s in range(PASSES)]
         gate_rows = keep.tile([P, V], F32, name="gate_rows")
         nc.gpsimd.memset(gate_rows[:], 0.0)
@@ -78,7 +83,8 @@ def tile_picked_sage_relu_e_kernel(
         for g, group in enumerate(W1_GROUPS):
             for s in range(PASSES):
                 cols = w1[s * K_PASS : (s + 1) * K_PASS, group[0] * P : (group[-1] + 1) * P]
-                nc.sync.dma_start(out=w1_raw[g][s][:], in_=cols.rearrange("(p j) m -> p j m", j=PACK))
+                dst = late_raw[:, s] if g == LATE else w1_raw[g][s][:]
+                nc.sync.dma_start(out=dst, in_=cols.rearrange("(p j) m -> p j m", j=PACK))
             if g == 0:
                 nc.sync.dma_start(pos_sb[0][:], pos1)
             if g == 1:
@@ -88,15 +94,30 @@ def tile_picked_sage_relu_e_kernel(
             rows = w2[s * K_PASS : (s + 1) * K_PASS, :]
             nc.sync.dma_start(out=w2_raw[s][:], in_=rows.rearrange("(p j) n -> p j n", j=PACK))
 
+        first_late = W1_GROUPS[LATE][0]
         w1_il = [
-            regions.tile([P, PASSES, P, PACK], BF16, name=f"w1_il{b}", offset=(4 * b + 1) * HALF_PAIR, align_bytes=64)
-            for b in range(BLOCKS)
+            keep.tile([P, PASSES, P, PACK], BF16, name=f"w1_il{b}", align_bytes=64) for b in range(first_late - 1)
         ]
-        w1_codes = [keep.tile([P, PASSES, P], U32, name="w1_codes", tag=f"codes{b}", align_bytes=64) for b in range(BLOCKS)]
-        w1_scales = [keep.tile([P, PASSES, P], U8, name="w1_scales", tag=f"scales{b}", align_bytes=64) for b in range(BLOCKS)]
-        w2_il = [keep.tile([P, N, PACK], BF16, name=f"w2_il{s}", align_bytes=64) for s in range(PASSES)]
+        w1_il.append(regions.tile([P, PASSES, P, PACK], BF16, name="w1_il_last", offset=0, align_bytes=64))
+        late_at = PASSES * P * PACK * 2 - OVERLAP
+        late_il = regions.tile([P, PASSES, late_cols, PACK], BF16, name="late_il", offset=late_at, align_bytes=64)
+        w2_at = late_at + PASSES * late_cols * PACK * 2 - OVERLAP
+        w2_il = [
+            regions.tile([P, N, PACK], BF16, name="w2_il0", offset=w2_at, align_bytes=64),
+            keep.tile([P, N, PACK], BF16, name="w2_il1", align_bytes=64),
+        ]
+        w1_codes = [keep.tile([P, PASSES, P], U32, name=f"w1_codes{b}", align_bytes=64) for b in range(first_late)]
+        w1_scales = [keep.tile([P, PASSES, P], U8, name=f"w1_scales{b}", align_bytes=64) for b in range(first_late)]
+        late_codes = keep.tile([P, PASSES, late_cols], U32, name="late_codes", align_bytes=64)
+        late_scales = keep.tile([P, PASSES, late_cols], U8, name="late_scales", align_bytes=64)
         w2_codes = [keep.tile([P, N], U32, name=f"w2_codes{s}", align_bytes=64) for s in range(PASSES)]
         w2_scales = {}
+
+        def stationary(b, s):
+            if b < first_late:
+                return w1_codes[b][:, s], w1_scales[b][:, s]
+            cols = slice((b - first_late) * P, (b - first_late + 1) * P)
+            return late_codes[:, s, cols], late_scales[:, s, cols]
 
         def interleave_on_scalar(dst, src):
             nc.scalar.copy(
@@ -104,13 +125,12 @@ def tile_picked_sage_relu_e_kernel(
             )
 
         def interleave_on_gpsimd(dst, src):
-            nc.gpsimd.tensor_scalar(dst, src.rearrange("p j c -> p c j"), 1.0, 0.0, MULT, ADD)
+            nc.gpsimd.tensor_scalar(dst, src, 1.0, 0.0, MULT, ADD)
 
         def interleave_w1(b, s):
             g = [b in group for group in W1_GROUPS].index(True)
             i = b - W1_GROUPS[g][0]
-            move = interleave_on_scalar if b < SCALAR_BLOCKS else interleave_on_gpsimd
-            move(w1_il[b][:, s], w1_raw[g][s][:, :, i * P : (i + 1) * P])
+            interleave_on_scalar(w1_il[b][:, s], w1_raw[g][s][:, :, i * P : (i + 1) * P])
 
         def quantize_w1(b):
             nc.vector.quantize_mx(
@@ -127,12 +147,13 @@ def tile_picked_sage_relu_e_kernel(
             )
 
         def quantize_w2(s, n0, n1, scales):
+            src = w2_il[s][:, n0:n1, :]
             for n in range(n0, n1, P):
                 w2_scales[s, n // P] = scales[:, n - n0 : n - n0 + P]
             nc.vector.quantize_mx(
                 out=w2_codes[s][:, n0:n1].bitcast(FP8X4),
                 scales=scales[:],
-                in_=w2_il[s][:, n0:n1, :].rearrange("p n j -> p (n j)"),
+                in_=src.rearrange("p n j -> p (n j)"),
             )
 
         turned = psum.tile([P, HALVES, P], F32, name="turned", tag="a")
@@ -145,6 +166,11 @@ def tile_picked_sage_relu_e_kernel(
                 for v in range(HALVES):
                     column = gate_cols[:, v, 2 * q + r : 2 * q + r + 1]
                     nc.tensor.transpose(gate_ps[q][:, r, v * P : (v + 1) * P], column.to_broadcast([P, P]), ident[:])
+
+        gate_sb = [keep.tile([P, V], F32, name=f"gate_sb{d}", align_bytes=64) for d in range(D) if d != 1]
+        gate_sb.insert(1, placed.tile([P, V], F32, name="gate_sb1", offset=0, align_bytes=64))
+        for d in range(D):
+            nc.scalar.copy(out=gate_sb[d][:], in_=gate_ps[d // 2][:, d % 2, :])
 
         x_il = [keep.tile([P, S, PACK], BF16, name=f"x_il{s}", align_bytes=64) for s in range(PASSES)]
         x_codes = [
@@ -206,18 +232,16 @@ def tile_picked_sage_relu_e_kernel(
                     part = slice(nodes.start + n0, nodes.start + n0 + step)
                     nc.tensor.matmul_mx(
                         out=acc[:, n0 : n0 + step],
-                        lhsT=w1_codes[b][:, s].bitcast(FP8X4),
-                        lhsT_scale=w1_scales[b][:, s],
+                        lhsT=stationary(b, s)[0].bitcast(FP8X4),
+                        lhsT_scale=stationary(b, s)[1],
                         rhs=x_codes[s][:, part].bitcast(FP8X4),
                         rhs_scale=node_scales(s, part),
                         start=(s == 0),
                         stop=(s == LAST and n0 + step == width),
                     )
 
-        def relu(b, slot=None):
-            if slot:
-                h = keep.tile([P, S], F32, name="h_held", tag=slot, align_bytes=64)
-            else:
+        def relu(b, h=None):
+            if h is None:
                 h = hidden.tile([P, S], F32, name="h")
             for i, (acc, nodes) in enumerate(zip(accs[b], pieces(b))):
                 if b == 0 and i % 2 == 0:
@@ -226,57 +250,86 @@ def tile_picked_sage_relu_e_kernel(
                     nc.scalar.activation(h[:, nodes], acc[:], RELU)
             return h
 
+        def held(slot, width):
+            return keep.tile([P, width], F32, name="held", tag=slot, align_bytes=64)
+
         sums = {}
         last_sums = []
         z_il = [keep.tile([P, V * PACK], BF16, name=f"z_il{s}", align_bytes=64) for s in range(PASSES)]
         z_codes = [keep.tile([P, V], U32, name=f"z_codes{s}", align_bytes=64) for s in range(PASSES)]
         z_scales = {}
 
-        def gather(b, d, h, dst, targets):
-            entries = pos_sb[d][:, targets.start // LIST_COL : targets.stop // LIST_COL]
-            if d < VECTOR_TURNS[b]:
-                nc.vector.tensor_copy(dst, h[:].indirect(entries))
-            else:
-                nc.scalar.activation(dst, h[:].indirect(entries), COPY)
+        def entries(d, n0, n1):
+            return pos_sb[d][:, n0 // LIST_COL : n1 // LIST_COL]
 
-        def add_transposed(acc, d, prod):
-            nc.tensor.matmul(acc, prod, ident[:], start=(d == 0), stop=(d == D - 1), is_transpose=True)
+        def sum_tile(b, v):
+            if b == BLOCKS - 1:
+                return last_sums[v][:]
+            return sums[b // PACK][v][:, (b % PACK) * P : (b % PACK + 1) * P]
 
-        def aggregate(b, h):
-            if b == 0:
-                pairs = [fetched.tile([P, 2, V], F32, name="pair") for q in range(PAIRS)]
-            else:
-                slots = (f"codes{b + 1}", f"scales{b + 1}")
-                pairs = [keep.tile([P, 2, V], F32, name="pair", tag=slot, align_bytes=64) for slot in slots]
-            for d in range(D):
-                gather(b, d, h, pairs[d // 2][:, d % 2, :], slice(0, V))
-            for q, pair in enumerate(pairs):
-                prod = pair
-                ahead = b + 2 + (q if b > 0 else 0)
-                if ahead < BLOCKS and (b, q) != (0, 1):
-                    first = (4 * ahead + 2 * q) * HALF_PAIR
-                    prod = regions.tile([P, 2, V], F32, name=f"prod{b}_{q}", offset=first, align_bytes=64)
-                nc.vector.tensor_tensor(prod[:], pair[:], gate_ps[q][:], MULT)
-                for v in range(HALVES):
-                    acc = sums[b // PACK][v][:, (b % PACK) * P : (b % PACK + 1) * P]
-                    for r in range(2):
-                        add_transposed(acc, 2 * q + r, prod[:, r, v * P : (v + 1) * P])
+        def add_transposed(b, v, prod, start, stop):
+            nc.tensor.matmul(sum_tile(b, v), prod, ident[:], start=start, stop=stop, is_transpose=True)
+
+        def gather_fused(b, d, h, prod=None):
+            if prod is None:
+                prod = prods.tile([P, V], F32, name="prod")
+            nc.vector.tensor_tensor(prod[:], h[:].indirect(pos_sb[d][:]), gate_sb[d][:], MULT)
+            for v in range(HALVES):
+                add_transposed(b, v, prod[:, v * P : (v + 1) * P], d == 0, d == D - 1)
+
+        def multiply_pair(b, q, pair, prod):
+            nc.vector.tensor_tensor(prod[:], pair[:], gate_ps[q][:], MULT)
+            for v in range(HALVES):
+                for r in range(2):
+                    add_transposed(b, v, prod[:, r, v * P : (v + 1) * P], (q, r) == (1, 0), (q, r) == (0, 1))
+
+        def aggregate_shared(b, h):
+            pairs = [fetched.tile([P, 2, V], F32, name="pair") for q in range(PAIRS)]
+            behind_late = b == first_late - 2
+            for r in range(2):
+                nc.scalar.activation(pairs[1][:, r, :], h[:].indirect(pos_sb[2 + r][:]), COPY)
+            if not behind_late:
+                h_next = relu(b + 1)
+            nc.vector.tensor_copy(pairs[0][:, 0, :], h[:].indirect(pos_sb[0][:]))
+            cut = VECTOR_SHARE[b]
+            if cut > 0:
+                nc.vector.tensor_copy(pairs[0][:, 1, :cut], h[:].indirect(entries(1, 0, cut)))
+            if cut < V:
+                nc.scalar.activation(pairs[0][:, 1, cut:], h[:].indirect(entries(1, cut, V)), COPY)
+            prod = pairs[1]
+            if behind_late:
+                h_next = relu(b + 1, raws.tile([P, S], F32, name="h_late", offset=0, align_bytes=64))
+                prod = raws.tile([P, 2, V], F32, name="prod_late", offset=S * 4, align_bytes=64)
+                for s in range(PASSES):
+                    nc.vector.quantize_mx(
+                        out=late_codes[:, s].bitcast(FP8X4),
+                        scales=late_scales[:, s],
+                        in_=late_il[:, s].rearrange("p m j -> p (m j)"),
+                    )
+                for s in range(PASSES):
+                    project(first_late, s)
+                for s in range(PASSES):
+                    interleave_on_gpsimd(w2_il[s][:], w2_raw[s][:].rearrange("p j n -> p n j"))
+            multiply_pair(b, 1, pairs[1], prod)
+            multiply_pair(b, 0, pairs[0], pairs[0])
+            return h_next
 
         def aggregate_half(b, h, v):
             targets = slice(v * P, (v + 1) * P)
-            pairs = []
-            for q in range(PAIRS):
-                if (v, q) == (HALVES - 1, PAIRS - 1):
-                    pairs.append(placed.tile([P, 2, P], F32, name="last_pair", offset=0, align_bytes=64))
+            pair = fetched.tile([P, 2, P], F32, name="pair")
+            for r in range(2):
+                nc.scalar.activation(pair[:, r, :], h[:].indirect(entries(2 + r, targets.start, targets.stop)), COPY)
+            order = (0, 1, "pair") if v == 0 else (0, "pair", 1)
+            for i, d in enumerate(order):
+                if d == "pair":
+                    nc.vector.tensor_tensor(pair[:], pair[:], gate_ps[1][:, :, targets], MULT)
+                    for r in range(2):
+                        add_transposed(b, v, pair[:, r, :], False, i == 2 and r == 1)
                 else:
-                    pairs.append(fetched.tile([P, 2, P], F32, name="pair"))
-            for d in range(D):
-                gather(b, d, h, pairs[d // 2][:, d % 2, :], targets)
-            for q, pair in enumerate(pairs):
-                prod = keep.tile([P, 2, P], F32, name="prod", tag=f"prod{v}_{q}", align_bytes=64)
-                nc.vector.tensor_tensor(prod[:], pair[:], gate_ps[q][:, :, targets], MULT)
-                for r in range(2):
-                    add_transposed(last_sums[v][:], 2 * q + r, prod[:, r, :])
+                    prod = keep.tile([P, P], F32, name="prod_half", tag=f"prod{v}_{d}", align_bytes=64)
+                    window = h[:].indirect(entries(d, targets.start, targets.stop))
+                    nc.vector.tensor_tensor(prod[:], window, gate_sb[d][:, targets], MULT)
+                    add_transposed(b, v, prod[:], i == 0, i == 2)
 
         def round_z(z_rows, s, v, b0, b1):
             first = v * K_PASS
@@ -326,44 +379,57 @@ def tile_picked_sage_relu_e_kernel(
         project(0, LAST)
         interleave_w1(1, 0)
         quantize_w1_pass(1, 0)
-        h = relu(0, "w1_slot1_0")
+        h = relu(0, held("w1_slot1_0", S))
         project(1, 0)
         interleave_w1(1, LAST)
-        quantize_w1_pass(1, LAST)
-        project(1, LAST)
+        open_sums(0)
+        for b in range(FUSED_BLOCKS):
+            gather_fused(b, 0, h)
+            quantize_w1_pass(b + 1, LAST)
+            project(b + 1, LAST)
+            if b == 0:
+                interleave_w1(2, 0)
+                h_next = relu(1, held("w1_slot2_0", S))
+                interleave_w1(2, LAST)
+            else:
+                interleave_w1(3, 0)
+                interleave_w1(4, 0)
+                interleave_w1(3, LAST)
+                h_next = relu(2, held("w1_slot3_0", S))
+                interleave_w1(4, LAST)
+            gather_fused(b, 1, h, held(f"w1_slot{b + 1}_{LAST}", V))
+            gather_fused(b, 2, h)
+            if b == 1:
+                quantize_w1(3)
+                for s in range(PASSES):
+                    project(3, s)
+            gather_fused(b, 3, h)
+            if b == 0:
+                quantize_w1_pass(2, 0)
+                project(2, 0)
+            h = h_next
+        quantize_w1(first_late - 1)
+        for s in range(PASSES):
+            project(first_late - 1, s)
+        interleave_on_gpsimd(late_il[:], late_raw[:].rearrange("p s j m -> p s m j"))
         z_rows = [keep.tile([P, HALVES * K_PASS], BF16, name=f"z_rows{s}", align_bytes=64) for s in range(PASSES)]
-        for b in range(BLOCKS - 1):
-            if b % PACK == 0:
-                open_sums(b // PACK)
-            for ahead in {0: (2,), 1: (3, 4)}.get(b, (b + 3,)):
-                if ahead < BLOCKS:
-                    for s in range(PASSES):
-                        interleave_w1(ahead, s)
-                    quantize_w1(ahead)
-            if b + 2 < BLOCKS:
+        for b in range(FUSED_BLOCKS, BLOCKS - 1):
+            if b == PACK:
+                open_sums(LAST)
+            if first_late < b + 2 < BLOCKS:
                 for s in range(PASSES):
                     project(b + 2, s)
-            elif b + 2 == BLOCKS:
-                for s in range(PASSES):
-                    for n0 in range(0, N, N // 2):
-                        interleave_on_gpsimd(w2_il[s][:, n0 : n0 + N // 2, :], w2_raw[s][:, :, n0 : n0 + N // 2])
-            if b == 0:
-                aggregate(b, h)
-                h = relu(1)
-            else:
-                h_next = relu(b + 1)
-                aggregate(b, h)
-                h = h_next
-            if b in (PACK, PACK + 1):
-                round_z(z_rows[0], 0, b - PACK, 0, PACK)
+            h = aggregate_shared(b, h)
+            if b in (PACK + 1, PACK + 2):
+                round_z(z_rows[0], 0, b - PACK - 1, 0, PACK)
         turn_z(z_rows[0], 0, 0, HALVES, "a")
 
-        for v, bank in enumerate(("b", "h0")):
+        for v, bank in enumerate(("b", "h1")):
             last_sums.append(psum.tile([P, P], F32, name="last_sums", tag=bank))
             aggregate_half(BLOCKS - 1, h, v)
         for v in range(HALVES):
             round_z(z_rows[LAST], LAST, v, 0, PACK - 1)
-        for v, bank in enumerate(("a", "h1")):
+        for v, bank in enumerate(("a", "h0")):
             round_z(z_rows[LAST], LAST, v, PACK - 1, PACK)
             turn_z(z_rows[LAST], LAST, v, v + 1, bank)
 
@@ -391,7 +457,7 @@ def tile_picked_sage_relu_e_kernel(
             for v in range(HALVES):
                 open_out(v, m, ("g0", "g1", "c", "d")[2 * m + v])
         quantize_w2(0, N // 2, N, held_scales("w2_scales0_2", 2 * V, V))
-        for m, bank in ((2, "h0"), (3, "a")):
+        for m, bank in ((2, "h1"), (3, "a")):
             open_out(0, m, bank)
         quantize_w2(LAST, 0, N // 2, held_scales("w2_scales1_0", 3 * V, V))
         z_scales[LAST] = keep.tile([P, V], U8, name="z_scales1", align_bytes=64)
@@ -400,7 +466,7 @@ def tile_picked_sage_relu_e_kernel(
         quantize_z(LAST, 1, 2)
         close_pair(0, 0, (nc.scalar.copy, nc.scalar.copy))
         close_pair(0, 2, (nc.vector.tensor_copy, nc.scalar.copy))
-        for m, bank in ((3, "h1"), (2, "g0")):
+        for m, bank in ((3, "h0"), (2, "g0")):
             open_out(1, m, bank)
         for m0 in (0, 2):
             close_pair(1, m0, (nc.vector.tensor_copy, nc.scalar.copy))

@@ -27,12 +27,11 @@ COPY = mybir.ActivationFunctionType.Copy
 MULT = mybir.AluOpType.mult
 ADD = mybir.AluOpType.add
 
-W1_GROUPS = ((0,), (1,), (2,), (3, 4), (5, 6, 7))
-LATE = len(W1_GROUPS) - 1
-FUSED_BLOCKS = 2
+W1_GROUPS = ((0,), (1,), (2,), (3, 4), (5, 6), (7,))
+FUSED_BLOCKS = 4
 ACC_BANKS = (("a", "b", "c", "d"), ("h0", "h1"), ("c", "d"), ("h0",), ("h1",), ("h0",), ("h1",), ("h0",))
 SUM_BANKS = (("a", "b"), ("c", "d"))
-VECTOR_SHARE = {2: 128, 3: 0, 4: 128, 5: 256, 6: 256}
+VECTOR_SHARE = {4: 128, 5: 128, 6: 256}
 
 
 def tile_picked_sage_relu_e_kernel(
@@ -60,13 +59,13 @@ def tile_picked_sage_relu_e_kernel(
         x_raw = [keep.tile([P, T], F32, name=f"x_raw{j}", tag=f"x_slot{j}", align_bytes=64) for j in range(PACK)]
         w1_raw = [
             [
-                keep.tile([P, PACK, len(group) * P], F32, name="w1_raw", tag=f"w1_slot{g}_{s}", align_bytes=64)
+                raws.tile([P, PACK, P], F32, name="w1_raw_last", offset=V * 4, align_bytes=64)
+                if (group[-1], s) == (BLOCKS - 1, LAST)
+                else keep.tile([P, PACK, len(group) * P], F32, name="w1_raw", tag=f"w1_slot{g}_{s}", align_bytes=64)
                 for s in range(PASSES)
             ]
-            for g, group in enumerate(W1_GROUPS[:LATE])
+            for g, group in enumerate(W1_GROUPS)
         ]
-        late_cols = len(W1_GROUPS[LATE]) * P
-        late_raw = raws.tile([P, PASSES, PACK, late_cols], F32, name="late_raw", offset=0, align_bytes=64)
         w2_raw = [keep.tile([P, PACK, N], F32, name=f"w2_raw{s}", align_bytes=64) for s in range(PASSES)]
         gate_rows = keep.tile([P, V], F32, name="gate_rows")
         nc.gpsimd.memset(gate_rows[:], 0.0)
@@ -83,8 +82,7 @@ def tile_picked_sage_relu_e_kernel(
         for g, group in enumerate(W1_GROUPS):
             for s in range(PASSES):
                 cols = w1[s * K_PASS : (s + 1) * K_PASS, group[0] * P : (group[-1] + 1) * P]
-                dst = late_raw[:, s] if g == LATE else w1_raw[g][s][:]
-                nc.sync.dma_start(out=dst, in_=cols.rearrange("(p j) m -> p j m", j=PACK))
+                nc.sync.dma_start(out=w1_raw[g][s][:], in_=cols.rearrange("(p j) m -> p j m", j=PACK))
             if g == 0:
                 nc.sync.dma_start(pos_sb[0][:], pos1)
             if g == 1:
@@ -94,30 +92,14 @@ def tile_picked_sage_relu_e_kernel(
             rows = w2[s * K_PASS : (s + 1) * K_PASS, :]
             nc.sync.dma_start(out=w2_raw[s][:], in_=rows.rearrange("(p j) n -> p j n", j=PACK))
 
-        first_late = W1_GROUPS[LATE][0]
-        w1_il = [
-            keep.tile([P, PASSES, P, PACK], BF16, name=f"w1_il{b}", align_bytes=64) for b in range(first_late - 1)
-        ]
+        w1_il = [keep.tile([P, PASSES, P, PACK], BF16, name=f"w1_il{b}", align_bytes=64) for b in range(BLOCKS - 1)]
         w1_il.append(regions.tile([P, PASSES, P, PACK], BF16, name="w1_il_last", offset=0, align_bytes=64))
-        late_at = PASSES * P * PACK * 2 - OVERLAP
-        late_il = regions.tile([P, PASSES, late_cols, PACK], BF16, name="late_il", offset=late_at, align_bytes=64)
-        w2_at = late_at + PASSES * late_cols * PACK * 2 - OVERLAP
-        w2_il = [
-            regions.tile([P, N, PACK], BF16, name="w2_il0", offset=w2_at, align_bytes=64),
-            keep.tile([P, N, PACK], BF16, name="w2_il1", align_bytes=64),
-        ]
-        w1_codes = [keep.tile([P, PASSES, P], U32, name=f"w1_codes{b}", align_bytes=64) for b in range(first_late)]
-        w1_scales = [keep.tile([P, PASSES, P], U8, name=f"w1_scales{b}", align_bytes=64) for b in range(first_late)]
-        late_codes = keep.tile([P, PASSES, late_cols], U32, name="late_codes", align_bytes=64)
-        late_scales = keep.tile([P, PASSES, late_cols], U8, name="late_scales", align_bytes=64)
+        w2_at = PASSES * P * PACK * 2 - OVERLAP
+        w2_il = regions.tile([P, PASSES, N, PACK], BF16, name="w2_il", offset=w2_at, align_bytes=64)
+        w1_codes = [keep.tile([P, PASSES, P], U32, name=f"w1_codes{b}", align_bytes=64) for b in range(BLOCKS)]
+        w1_scales = [keep.tile([P, PASSES, P], U8, name=f"w1_scales{b}", align_bytes=64) for b in range(BLOCKS)]
         w2_codes = [keep.tile([P, N], U32, name=f"w2_codes{s}", align_bytes=64) for s in range(PASSES)]
         w2_scales = {}
-
-        def stationary(b, s):
-            if b < first_late:
-                return w1_codes[b][:, s], w1_scales[b][:, s]
-            cols = slice((b - first_late) * P, (b - first_late + 1) * P)
-            return late_codes[:, s, cols], late_scales[:, s, cols]
 
         def interleave_on_scalar(dst, src):
             nc.scalar.copy(
@@ -147,7 +129,7 @@ def tile_picked_sage_relu_e_kernel(
             )
 
         def quantize_w2(s, n0, n1, scales):
-            src = w2_il[s][:, n0:n1, :]
+            src = w2_il[:, s, n0:n1, :]
             for n in range(n0, n1, P):
                 w2_scales[s, n // P] = scales[:, n - n0 : n - n0 + P]
             nc.vector.quantize_mx(
@@ -232,8 +214,8 @@ def tile_picked_sage_relu_e_kernel(
                     part = slice(nodes.start + n0, nodes.start + n0 + step)
                     nc.tensor.matmul_mx(
                         out=acc[:, n0 : n0 + step],
-                        lhsT=stationary(b, s)[0].bitcast(FP8X4),
-                        lhsT_scale=stationary(b, s)[1],
+                        lhsT=w1_codes[b][:, s].bitcast(FP8X4),
+                        lhsT_scale=w1_scales[b][:, s],
                         rhs=x_codes[s][:, part].bitcast(FP8X4),
                         rhs_scale=node_scales(s, part),
                         start=(s == 0),
@@ -283,35 +265,32 @@ def tile_picked_sage_relu_e_kernel(
                 for r in range(2):
                     add_transposed(b, v, prod[:, r, v * P : (v + 1) * P], (q, r) == (1, 0), (q, r) == (0, 1))
 
-        def aggregate_shared(b, h):
-            pairs = [fetched.tile([P, 2, V], F32, name="pair") for q in range(PAIRS)]
-            behind_late = b == first_late - 2
-            for r in range(2):
-                nc.scalar.activation(pairs[1][:, r, :], h[:].indirect(pos_sb[2 + r][:]), COPY)
-            if not behind_late:
-                h_next = relu(b + 1)
-            nc.vector.tensor_copy(pairs[0][:, 0, :], h[:].indirect(pos_sb[0][:]))
+        pairs = {}
+
+        def pair_tile(b, q):
+            if b == FUSED_BLOCKS:
+                return raws.tile([P, 2, V], F32, name=f"pair_held{q}", offset=q * 2 * V * 4, align_bytes=64)
+            return fetched.tile([P, 2, V], F32, name="pair")
+
+        def fetch_on_vector(b, h):
+            pairs[b, 0] = pair_tile(b, 0)
+            nc.vector.tensor_copy(pairs[b, 0][:, 0, :], h[:].indirect(pos_sb[0][:]))
             cut = VECTOR_SHARE[b]
             if cut > 0:
-                nc.vector.tensor_copy(pairs[0][:, 1, :cut], h[:].indirect(entries(1, 0, cut)))
+                nc.vector.tensor_copy(pairs[b, 0][:, 1, :cut], h[:].indirect(entries(1, 0, cut)))
+
+        def aggregate_shared(b, h):
+            pairs[b, 1] = pair_tile(b, 1)
+            for r in range(2):
+                nc.scalar.activation(pairs[b, 1][:, r, :], h[:].indirect(pos_sb[2 + r][:]), COPY)
+            h_next = relu(b + 1)
+            cut = VECTOR_SHARE[b]
             if cut < V:
-                nc.scalar.activation(pairs[0][:, 1, cut:], h[:].indirect(entries(1, cut, V)), COPY)
-            prod = pairs[1]
-            if behind_late:
-                h_next = relu(b + 1, raws.tile([P, S], F32, name="h_late", offset=0, align_bytes=64))
-                prod = raws.tile([P, 2, V], F32, name="prod_late", offset=S * 4, align_bytes=64)
-                for s in range(PASSES):
-                    nc.vector.quantize_mx(
-                        out=late_codes[:, s].bitcast(FP8X4),
-                        scales=late_scales[:, s],
-                        in_=late_il[:, s].rearrange("p m j -> p (m j)"),
-                    )
-                for s in range(PASSES):
-                    project(first_late, s)
-                for s in range(PASSES):
-                    interleave_on_gpsimd(w2_il[s][:], w2_raw[s][:].rearrange("p j n -> p n j"))
-            multiply_pair(b, 1, pairs[1], prod)
-            multiply_pair(b, 0, pairs[0], pairs[0])
+                nc.scalar.activation(pairs[b, 0][:, 1, cut:], h[:].indirect(entries(1, cut, V)), COPY)
+            multiply_pair(b, 1, pairs[b, 1], pairs[b, 1])
+            if b + 1 in VECTOR_SHARE:
+                fetch_on_vector(b + 1, h_next)
+            multiply_pair(b, 0, pairs[b, 0], pairs[b, 0])
             return h_next
 
         def aggregate_half(b, h, v):
@@ -319,12 +298,12 @@ def tile_picked_sage_relu_e_kernel(
             pair = fetched.tile([P, 2, P], F32, name="pair")
             for r in range(2):
                 nc.scalar.activation(pair[:, r, :], h[:].indirect(entries(2 + r, targets.start, targets.stop)), COPY)
-            order = (0, 1, "pair") if v == 0 else (0, "pair", 1)
+            order = ("pair", 0, 1) if v == 0 else (0, "pair", 1)
             for i, d in enumerate(order):
                 if d == "pair":
                     nc.vector.tensor_tensor(pair[:], pair[:], gate_ps[1][:, :, targets], MULT)
                     for r in range(2):
-                        add_transposed(b, v, pair[:, r, :], False, i == 2 and r == 1)
+                        add_transposed(b, v, pair[:, r, :], i == 0 and r == 0, False)
                 else:
                     prod = keep.tile([P, P], F32, name="prod_half", tag=f"prod{v}_{d}", align_bytes=64)
                     window = h[:].indirect(entries(d, targets.start, targets.stop))
@@ -384,44 +363,44 @@ def tile_picked_sage_relu_e_kernel(
         interleave_w1(1, LAST)
         open_sums(0)
         for b in range(FUSED_BLOCKS):
-            gather_fused(b, 0, h)
-            quantize_w1_pass(b + 1, LAST)
-            project(b + 1, LAST)
-            if b == 0:
-                interleave_w1(2, 0)
-                h_next = relu(1, held("w1_slot2_0", S))
-                interleave_w1(2, LAST)
-            else:
-                interleave_w1(3, 0)
-                interleave_w1(4, 0)
-                interleave_w1(3, LAST)
-                h_next = relu(2, held("w1_slot3_0", S))
-                interleave_w1(4, LAST)
-            gather_fused(b, 1, h, held(f"w1_slot{b + 1}_{LAST}", V))
-            gather_fused(b, 2, h)
+            tight = b < 2
+            if tight:
+                gather_fused(b, 0, h)
+                quantize_w1_pass(b + 1, LAST)
+                project(b + 1, LAST)
+            group = W1_GROUPS[b + 2]
+            for member in group:
+                interleave_w1(member, 0)
             if b == 1:
-                quantize_w1(3)
-                for s in range(PASSES):
-                    project(3, s)
-            gather_fused(b, 3, h)
+                interleave_w1(3, LAST)
+            h_next = relu(b + 1, held(f"w1_slot{b + 2}_0", S))
+            for member in group[1:] if b == 1 else group:
+                interleave_w1(member, LAST)
+            for d in range(1 if tight else 0, D):
+                gather_fused(b, d, h, held(f"w1_slot{b + 1}_{LAST}", V) if tight and d == 1 else None)
+                if d == D - 2:
+                    for ahead in {1: (3,), 2: (4,), 3: (5, 6)}.get(b, ()):
+                        quantize_w1(ahead)
+                        for s in range(PASSES):
+                            project(ahead, s)
             if b == 0:
                 quantize_w1_pass(2, 0)
                 project(2, 0)
             h = h_next
-        quantize_w1(first_late - 1)
+        quantize_w1(BLOCKS - 1)
         for s in range(PASSES):
-            project(first_late - 1, s)
-        interleave_on_gpsimd(late_il[:], late_raw[:].rearrange("p s j m -> p s m j"))
+            interleave_on_gpsimd(w2_il[:, s], w2_raw[s][:].rearrange("p j n -> p n j"))
         z_rows = [keep.tile([P, HALVES * K_PASS], BF16, name=f"z_rows{s}", align_bytes=64) for s in range(PASSES)]
+        fetch_on_vector(FUSED_BLOCKS, h)
         for b in range(FUSED_BLOCKS, BLOCKS - 1):
             if b == PACK:
                 open_sums(LAST)
-            if first_late < b + 2 < BLOCKS:
+            if b + 2 == BLOCKS - 1:
                 for s in range(PASSES):
                     project(b + 2, s)
             h = aggregate_shared(b, h)
-            if b in (PACK + 1, PACK + 2):
-                round_z(z_rows[0], 0, b - PACK - 1, 0, PACK)
+            if b in (PACK, PACK + 1):
+                round_z(z_rows[0], 0, b - PACK, 0, PACK)
         turn_z(z_rows[0], 0, 0, HALVES, "a")
 
         for v, bank in enumerate(("b", "h1")):

@@ -31,6 +31,7 @@ W1_GROUPS = ((0,), (1,), (2,), (3, 4), (5, 6), (7,))
 FUSED_BLOCKS = 4
 ACC_BANKS = (("a", "b", "c", "d"), ("h0", "h1"), ("c", "d"), ("h0",), ("h1",), ("h0",), ("h1",), ("h0",))
 SUM_BANKS = (("a", "b"), ("c", "d"))
+LAST_SCALAR_TURN = (2, 3)
 VECTOR_SHARE = {4: 128, 5: 128, 6: 256}
 
 
@@ -149,8 +150,8 @@ def tile_picked_sage_relu_e_kernel(
                     column = gate_cols[:, v, 2 * q + r : 2 * q + r + 1]
                     nc.tensor.transpose(gate_ps[q][:, r, v * P : (v + 1) * P], column.to_broadcast([P, P]), ident[:])
 
-        gate_sb = [keep.tile([P, V], F32, name=f"gate_sb{d}", align_bytes=64) for d in range(D) if d != 1]
-        gate_sb.insert(1, placed.tile([P, V], F32, name="gate_sb1", offset=0, align_bytes=64))
+        gate_sb = [keep.tile([P, V], F32, name=f"gate_sb{d}", align_bytes=64) for d in range(D) if d != 0]
+        gate_sb.insert(0, placed.tile([P, V], F32, name="gate_sb0", offset=0, align_bytes=64))
         for d in range(D):
             nc.scalar.copy(out=gate_sb[d][:], in_=gate_ps[d // 2][:, d % 2, :])
 
@@ -295,20 +296,22 @@ def tile_picked_sage_relu_e_kernel(
 
         def aggregate_half(b, h, v):
             targets = slice(v * P, (v + 1) * P)
-            pair = fetched.tile([P, 2, P], F32, name="pair")
-            for r in range(2):
-                nc.scalar.activation(pair[:, r, :], h[:].indirect(entries(2 + r, targets.start, targets.stop)), COPY)
-            order = ("pair", 0, 1) if v == 0 else (0, "pair", 1)
+            first = LAST_SCALAR_TURN[v]
+            pair = fetched.tile([P, D - first, P], F32, name="pair")
+            for d in range(first, D):
+                nc.scalar.activation(pair[:, d - first, :], h[:].indirect(entries(d, targets.start, targets.stop)), COPY)
+            order = list(range(first - 1, -1, -1))
+            order.insert(v, "pair")
             for i, d in enumerate(order):
                 if d == "pair":
-                    nc.vector.tensor_tensor(pair[:], pair[:], gate_ps[1][:, :, targets], MULT)
-                    for r in range(2):
+                    nc.vector.tensor_tensor(pair[:], pair[:], gate_ps[1][:, first - 2 :, targets], MULT)
+                    for r in range(D - first):
                         add_transposed(b, v, pair[:, r, :], i == 0 and r == 0, False)
                 else:
                     prod = keep.tile([P, P], F32, name="prod_half", tag=f"prod{v}_{d}", align_bytes=64)
                     window = h[:].indirect(entries(d, targets.start, targets.stop))
                     nc.vector.tensor_tensor(prod[:], window, gate_sb[d][:, targets], MULT)
-                    add_transposed(b, v, prod[:], i == 0, i == 2)
+                    add_transposed(b, v, prod[:], i == 0, i == len(order) - 1)
 
         def round_z(z_rows, s, v, b0, b1):
             first = v * K_PASS
@@ -441,7 +444,7 @@ def tile_picked_sage_relu_e_kernel(
         quantize_w2(LAST, 0, N // 2, held_scales("w2_scales1_0", 3 * V, V))
         z_scales[LAST] = keep.tile([P, V], U8, name="z_scales1", align_bytes=64)
         quantize_z(LAST, 0, 1)
-        quantize_w2(LAST, N // 2, N, keep.tile([P, V], U8, name="w2_scales1_2", tag="prod1_0", align_bytes=64))
+        quantize_w2(LAST, N // 2, N, keep.tile([P, V], U8, name="w2_scales1_2", tag="prod1_1", align_bytes=64))
         quantize_z(LAST, 1, 2)
         close_pair(0, 0, (nc.scalar.copy, nc.scalar.copy))
         close_pair(0, 2, (nc.vector.tensor_copy, nc.scalar.copy))

@@ -32,7 +32,7 @@ FUSED_BLOCKS = 4
 ACC_BANKS = (("a", "b", "c", "d"), ("h0", "h1"), ("c", "d"), ("h0",), ("h1",), ("h0",), ("h1",), ("h0",))
 SUM_BANKS = (("a", "b"), ("c", "d"))
 LAST_SCALAR_TURN = (2, 3)
-VECTOR_SHARE = {4: 128, 5: 128, 6: 256}
+VECTOR_SHARE = {4: 0, 5: 128, 6: 256}
 
 
 def tile_picked_sage_relu_e_kernel(
@@ -404,6 +404,7 @@ def tile_picked_sage_relu_e_kernel(
             h = aggregate_shared(b, h)
             if b in (PACK, PACK + 1):
                 round_z(z_rows[0], 0, b - PACK, 0, PACK)
+
         turn_z(z_rows[0], 0, 0, HALVES, "a")
 
         for v, bank in enumerate(("b", "h1")):

@@ -67,7 +67,7 @@ def tile_picked_sage_relu_e_kernel(
             ]
             for g, group in enumerate(W1_GROUPS)
         ]
-        w2_raw = [keep.tile([P, PACK, N], F32, name=f"w2_raw{s}", align_bytes=64) for s in range(PASSES)]
+        w2_raw = keep.tile([P, PASSES, PACK, N], F32, name="w2_raw", align_bytes=64)
         gate_rows = keep.tile([P, V], F32, name="gate_rows")
         nc.gpsimd.memset(gate_rows[:], 0.0)
         gate_cols = keep.tile([P, HALVES, D], F32, name="gate_cols")
@@ -89,9 +89,7 @@ def tile_picked_sage_relu_e_kernel(
             if g == 1:
                 for d, pos in ((1, pos2), (2, pos3), (3, pos4)):
                     nc.sync.dma_start(pos_sb[d][:], pos)
-        for s in range(PASSES):
-            rows = w2[s * K_PASS : (s + 1) * K_PASS, :]
-            nc.sync.dma_start(out=w2_raw[s][:], in_=rows.rearrange("(p j) n -> p j n", j=PACK))
+        nc.sync.dma_start(out=w2_raw[:], in_=w2.rearrange("(s p j) n -> p s j n", p=P, j=PACK))
 
         w1_il = [keep.tile([P, PASSES, P, PACK], BF16, name=f"w1_il{b}", align_bytes=64) for b in range(BLOCKS - 1)]
         w1_il.append(regions.tile([P, PASSES, P, PACK], BF16, name="w1_il_last", offset=0, align_bytes=64))
@@ -391,8 +389,7 @@ def tile_picked_sage_relu_e_kernel(
                 project(2, 0)
             h = h_next
         quantize_w1(BLOCKS - 1)
-        for s in range(PASSES):
-            interleave_on_gpsimd(w2_il[:, s], w2_raw[s][:].rearrange("p j n -> p n j"))
+        interleave_on_gpsimd(w2_il[:], w2_raw[:].rearrange("p s j n -> p s n j"))
         z_rows = [keep.tile([P, HALVES * K_PASS], BF16, name=f"z_rows{s}", align_bytes=64) for s in range(PASSES)]
         fetch_on_vector(FUSED_BLOCKS, h)
         for b in range(FUSED_BLOCKS, BLOCKS - 1):
@@ -434,11 +431,13 @@ def tile_picked_sage_relu_e_kernel(
             return placed.tile([P, width], U8, name=name, offset=first, align_bytes=64)
 
         z_scales[0] = held_scales("z_scales0", 0, V)
-        quantize_z(0, 0, HALVES)
-        for m in range(2):
+        quantize_z(0, 0, 1)
+        for m, bank in enumerate(("g0", "g1")):
             quantize_w2(0, m * P, (m + 1) * P, held_scales(f"w2_scales0_{m}", V + m * P, P))
-            for v in range(HALVES):
-                open_out(v, m, ("g0", "g1", "c", "d")[2 * m + v])
+            open_out(0, m, bank)
+        quantize_z(0, 1, 2)
+        for m, bank in enumerate(("c", "d")):
+            open_out(1, m, bank)
         quantize_w2(0, N // 2, N, held_scales("w2_scales0_2", 2 * V, V))
         for m, bank in ((2, "h1"), (3, "a")):
             open_out(0, m, bank)

@@ -239,6 +239,7 @@ def tile_picked_sage_relu_e_kernel(
         z_il = [keep.tile([P, V * PACK], BF16, name=f"z_il{s}", align_bytes=64) for s in range(PASSES)]
         z_codes = [keep.tile([P, V], U32, name=f"z_codes{s}", align_bytes=64) for s in range(PASSES)]
         z_scales = {}
+        z_rows = {}
 
         def entries(d, n0, n1):
             return pos_sb[d][:, n0 // LIST_COL : n1 // LIST_COL]
@@ -311,22 +312,20 @@ def tile_picked_sage_relu_e_kernel(
                     nc.vector.tensor_tensor(prod[:], window, gate_sb[d][:, targets], MULT)
                     add_transposed(b, v, prod[:], i == 0, i == len(order) - 1)
 
-        def round_z(z_rows, s, v, b0, b1):
-            first = v * K_PASS
+        def round_z(s, v, b0, b1):
             src = last_sums[v][:] if (s, b0) == (LAST, PACK - 1) else sums[s][v][:, b0 * P : b1 * P]
-            dst = z_rows[:, first : first + K_PASS].rearrange("t (u p e) -> t u p e", u=2, e=2)
+            dst = z_rows[s, v][:].rearrange("t (u p e) -> t u p e", u=2, e=2)
             per_block = P // PACK
             nc.scalar.copy(
                 out=dst[:, :, b0 * per_block : b1 * per_block, :],
                 in_=src.rearrange("t (p u e) -> t u p e", u=2, e=2),
             )
 
-        def turn_z(z_rows, s, v0, v1, bank):
+        def turn_z(s, v0, v1, bank):
             words = psum.tile([P, v1 - v0, 2, P], F32, name="words", tag=bank)
             for v in range(v0, v1):
                 for u in range(2):
-                    first = v * K_PASS + u * (K_PASS // 2)
-                    run = z_rows[:, first : first + K_PASS // 2].bitcast(F32)
+                    run = z_rows[s, v][:, u * (K_PASS // 2) : (u + 1) * (K_PASS // 2)].bitcast(F32)
                     nc.tensor.transpose(words[:, v - v0, u, :], run, ident[:])
             nc.scalar.copy(
                 out=z_il[s][:, v0 * K_PASS : v1 * K_PASS].bitcast(F32).rearrange("p (v n u) -> p v n u", n=P, u=2),
@@ -359,9 +358,12 @@ def tile_picked_sage_relu_e_kernel(
         project(0, LAST)
         interleave_w1(1, 0)
         quantize_w1_pass(1, 0)
+        nc.vector.tensor_copy(
+            out=w1_il[1][:, LAST].rearrange("p (c i) j -> p c j i", i=4),
+            in_=w1_raw[1][LAST][:].rearrange("p j (c i) -> p c j i", i=4),
+        )
         h = relu(0, held("w1_slot1_0", S))
         project(1, 0)
-        interleave_w1(1, LAST)
         open_sums(0)
         for b in range(FUSED_BLOCKS):
             tight = b < 2
@@ -372,25 +374,27 @@ def tile_picked_sage_relu_e_kernel(
             group = W1_GROUPS[b + 2]
             for member in group:
                 interleave_w1(member, 0)
-            if b == 1:
-                interleave_w1(3, LAST)
+            before = group if b < 2 else group[:1]
+            for member in before:
+                interleave_w1(member, LAST)
             h_next = relu(b + 1, held(f"w1_slot{b + 2}_0", S))
-            for member in group[1:] if b == 1 else group:
+            for member in group[len(before) :]:
                 interleave_w1(member, LAST)
             for d in range(1 if tight else 0, D):
                 gather_fused(b, d, h, held(f"w1_slot{b + 1}_{LAST}", V) if tight and d == 1 else None)
-                if d == D - 2:
-                    for ahead in {1: (3,), 2: (4,), 3: (5, 6)}.get(b, ()):
-                        quantize_w1(ahead)
-                        for s in range(PASSES):
-                            project(ahead, s)
+                ahead = {(1, 2): 3, (2, 0): 4, (2, 3): 5, (3, 0): 6}.get((b, d))
+                if ahead:
+                    quantize_w1(ahead)
+                    for s in range(PASSES):
+                        project(ahead, s)
             if b == 0:
                 quantize_w1_pass(2, 0)
                 project(2, 0)
             h = h_next
         quantize_w1(BLOCKS - 1)
         interleave_on_gpsimd(w2_il[:], w2_raw[:].rearrange("p s j n -> p s n j"))
-        z_rows = [keep.tile([P, HALVES * K_PASS], BF16, name=f"z_rows{s}", align_bytes=64) for s in range(PASSES)]
+        for s, v in ((0, 0), (0, 1), (LAST, 0)):
+            z_rows[s, v] = keep.tile([P, K_PASS], BF16, name=f"z_rows{s}_{v}", align_bytes=64)
         fetch_on_vector(FUSED_BLOCKS, h)
         for b in range(FUSED_BLOCKS, BLOCKS - 1):
             if b == PACK:
@@ -400,18 +404,19 @@ def tile_picked_sage_relu_e_kernel(
                     project(b + 2, s)
             h = aggregate_shared(b, h)
             if b in (PACK, PACK + 1):
-                round_z(z_rows[0], 0, b - PACK, 0, PACK)
+                round_z(0, b - PACK, 0, PACK)
 
-        turn_z(z_rows[0], 0, 0, HALVES, "a")
+        turn_z(0, 0, HALVES, "a")
 
         for v, bank in enumerate(("b", "h1")):
             last_sums.append(psum.tile([P, P], F32, name="last_sums", tag=bank))
             aggregate_half(BLOCKS - 1, h, v)
+        z_rows[LAST, 1] = keep.tile([P, K_PASS], BF16, name="z_rows_last", tag="prod0_0", align_bytes=64)
         for v in range(HALVES):
-            round_z(z_rows[LAST], LAST, v, 0, PACK - 1)
+            round_z(LAST, v, 0, PACK - 1)
+            round_z(LAST, v, PACK - 1, PACK)
         for v, bank in enumerate(("a", "h0")):
-            round_z(z_rows[LAST], LAST, v, PACK - 1, PACK)
-            turn_z(z_rows[LAST], LAST, v, v + 1, bank)
+            turn_z(LAST, v, v + 1, bank)
 
         out_rows = out.rearrange("(m p) v -> p m v", p=P)
         out_acc = {}
@@ -438,17 +443,17 @@ def tile_picked_sage_relu_e_kernel(
         quantize_z(0, 1, 2)
         for m, bank in enumerate(("c", "d")):
             open_out(1, m, bank)
-        quantize_w2(0, N // 2, N, held_scales("w2_scales0_2", 2 * V, V))
-        for m, bank in ((2, "h1"), (3, "a")):
-            open_out(0, m, bank)
         quantize_w2(LAST, 0, N // 2, held_scales("w2_scales1_0", 3 * V, V))
         z_scales[LAST] = keep.tile([P, V], U8, name="z_scales1", align_bytes=64)
         quantize_z(LAST, 0, 1)
+        close_pair(0, 0, (nc.vector.tensor_copy, nc.scalar.copy))
+        quantize_w2(0, N // 2, N, held_scales("w2_scales0_2", 2 * V, V))
+        for m, bank in ((2, "h1"), (3, "a")):
+            open_out(0, m, bank)
         quantize_w2(LAST, N // 2, N, keep.tile([P, V], U8, name="w2_scales1_2", tag="prod1_1", align_bytes=64))
         quantize_z(LAST, 1, 2)
-        close_pair(0, 0, (nc.scalar.copy, nc.scalar.copy))
         close_pair(0, 2, (nc.vector.tensor_copy, nc.scalar.copy))
-        for m, bank in ((3, "h0"), (2, "g0")):
+        for m, bank in ((3, "h0"), (2, "b")):
             open_out(1, m, bank)
         for m0 in (0, 2):
             close_pair(1, m0, (nc.vector.tensor_copy, nc.scalar.copy))

from contextlib import ExitStack

import concourse.mybir as mybir
from concourse.masks import make_identity

K, T, D, S, V, H, N = 1024, 2048, 4, 512, 256, 1024, 512
P = 128
PACK = 4
K_PASS = P * PACK
PASSES = K // K_PASS
LAST = PASSES - 1
BLOCKS = H // P
HALVES = V // P
PAIRS = D // 2
LIST_COL = 16
OVERLAP = 64
FLOPS = 2 * S * K * H + 2 * V * H * N + 2 * D * V * H

F32 = mybir.dt.float32
BF16 = mybir.dt.bfloat16
U32 = mybir.dt.uint32
U16 = mybir.dt.uint16
U8 = mybir.dt.uint8
FP8X4 = mybir.dt.float8_e4m3fn_x4
RELU = mybir.ActivationFunctionType.Relu
COPY = mybir.ActivationFunctionType.Copy
MULT = mybir.AluOpType.mult
ADD = mybir.AluOpType.add

W1_GROUPS = ((0,), (1,), (2,), (3, 4), (5, 6), (7,))
FUSED_BLOCKS = 4
ACC_BANKS = (("a", "b", "c", "d"), ("h0", "h1"), ("c", "d"), ("h0",), ("h1",), ("h0",), ("h1",), ("h0",))
SUM_BANKS = (("a", "b"), ("c", "d"))
LAST_SCALAR_TURN = (2, 3)
VECTOR_SHARE = {4: 0, 5: 128, 6: 256}


def tile_picked_sage_relu_e_kernel(
    tc, xT, w1, w2, gate, offs, pos1, pos2, pos3, pos4, out
):
    nc = tc.nc
    with ExitStack() as ctx:
        lists = ctx.enter_context(tc.tile_pool(name="lists", bufs=1))
        keep = ctx.enter_context(tc.tile_pool(name="keep", bufs=1))
        placed = ctx.enter_context(tc.tile_pool(name="placed", bufs=1))
        regions = ctx.enter_context(tc.tile_pool(name="regions", bufs=1))
        raws = ctx.enter_context(tc.tile_pool(name="raws", bufs=1))
        hidden = ctx.enter_context(tc.tile_pool(name="hidden", bufs=4))
        fetched = ctx.enter_context(tc.tile_pool(name="fetched", bufs=6))
        prods = ctx.enter_context(tc.tile_pool(name="prods", bufs=6))
        psum = ctx.enter_context(tc.psum_pool(name="psum", bufs=1))

        offs_sb = lists.tile([P, S // LIST_COL], U16, name="offs_sb")
        pos_sb = [lists.tile([P, V // LIST_COL], U16, name=f"pos_sb{d}") for d in range(D)]

        ident = keep.tile([P, P], F32, name="ident")
        make_identity(nc, ident[:])

        x_pairs = [keep.tile([P, 2, T], F32, name=f"x_pair{u}") for u in range(PACK // 2)]
        x_raw = [keep.tile([P, T], F32, name=f"x_raw{j}", tag=f"x_slot{j}", align_bytes=64) for j in range(PACK)]
        w1_raw = [
            [
                raws.tile([P, PACK, P], F32, name="w1_raw_last", offset=V * 4, align_bytes=64)
                if (group[-1], s) == (BLOCKS - 1, LAST)
                else keep.tile([P, PACK, len(group) * P], F32, name="w1_raw", tag=f"w1_slot{g}_{s}", align_bytes=64)
                for s in range(PASSES)
            ]
            for g, group in enumerate(W1_GROUPS)
        ]
        w2_raw = keep.tile([P, PASSES, PACK, N], F32, name="w2_raw", align_bytes=64)
        gate_rows = keep.tile([P, V], F32, name="gate_rows")
        nc.gpsimd.memset(gate_rows[:], 0.0)
        gate_cols = keep.tile([P, HALVES, D], F32, name="gate_cols")

        rows = xT[:K_PASS, :].rearrange("(p j) t -> p j t", j=PACK)
        nc.sync.dma_start(out=x_pairs[0][:], in_=rows[:, :2, :])
        nc.sync.dma_start(offs_sb[:], offs)
        nc.sync.dma_start(out=x_pairs[1][:], in_=rows[:, 2:, :])
        nc.sync.dma_start(out=gate_rows[:D, :], in_=gate[:, 0, :])
        rows = xT[K_PASS:, :].rearrange("(p j) t -> j p t", j=PACK)
        for j in range(PACK):
            nc.sync.dma_start(out=x_raw[j][:], in_=rows[j])
        for g, group in enumerate(W1_GROUPS):
            for s in range(PASSES):
                cols = w1[s * K_PASS : (s + 1) * K_PASS, group[0] * P : (group[-1] + 1) * P]
                nc.sync.dma_start(out=w1_raw[g][s][:], in_=cols.rearrange("(p j) m -> p j m", j=PACK))
            if g == 0:
                nc.sync.dma_start(pos_sb[0][:], pos1)
            if g == 1:
                for d, pos in ((1, pos2), (2, pos3), (3, pos4)):
                    nc.sync.dma_start(pos_sb[d][:], pos)
        nc.sync.dma_start(out=w2_raw[:], in_=w2.rearrange("(s p j) n -> p s j n", p=P, j=PACK))

        w1_il = [keep.tile([P, PASSES, P, PACK], BF16, name=f"w1_il{b}", align_bytes=64) for b in range(BLOCKS - 1)]
        w1_il.append(regions.tile([P, PASSES, P, PACK], BF16, name="w1_il_last", offset=0, align_bytes=64))
        w2_at = PASSES * P * PACK * 2 - OVERLAP
        w2_il = regions.tile([P, PASSES, N, PACK], BF16, name="w2_il", offset=w2_at, align_bytes=64)
        w1_codes = [keep.tile([P, PASSES, P], U32, name=f"w1_codes{b}", align_bytes=64) for b in range(BLOCKS)]
        w1_scales = [keep.tile([P, PASSES, P], U8, name=f"w1_scales{b}", align_bytes=64) for b in range(BLOCKS)]
        w2_codes = [keep.tile([P, N], U32, name=f"w2_codes{s}", align_bytes=64) for s in range(PASSES)]
        w2_scales = {}

        def interleave_on_scalar(dst, src):
            nc.scalar.copy(
                out=dst.rearrange("p (c i) j -> p c j i", i=4), in_=src.rearrange("p j (c i) -> p c j i", i=4)
            )

        def interleave_on_gpsimd(dst, src):
            nc.gpsimd.tensor_scalar(dst, src, 1.0, 0.0, MULT, ADD)

        def interleave_w1(b, s):
            g = [b in group for group in W1_GROUPS].index(True)
            i = b - W1_GROUPS[g][0]
            interleave_on_scalar(w1_il[b][:, s], w1_raw[g][s][:, :, i * P : (i + 1) * P])

        def quantize_w1(b):
            nc.vector.quantize_mx(
                out=w1_codes[b][:].rearrange("p s m -> p (s m)").bitcast(FP8X4),
                scales=w1_scales[b][:].rearrange("p s m -> p (s m)"),
                in_=w1_il[b][:].rearrange("p s m j -> p (s m j)"),
            )

        def quantize_w1_pass(b, s):
            nc.vector.quantize_mx(
                out=w1_codes[b][:, s].bitcast(FP8X4),
                scales=w1_scales[b][:, s],
                in_=w1_il[b][:, s].rearrange("p m j -> p (m j)"),
            )

        def quantize_w2(s, n0, n1, scales):
            src = w2_il[:, s, n0:n1, :]
            for n in range(n0, n1, P):
                w2_scales[s, n // P] = scales[:, n - n0 : n - n0 + P]
            nc.vector.quantize_mx(
                out=w2_codes[s][:, n0:n1].bitcast(FP8X4),
                scales=scales[:],
                in_=src.rearrange("p n j -> p (n j)"),
            )

        turned = psum.tile([P, HALVES, P], F32, name="turned", tag="a")
        for v in range(HALVES):
            nc.tensor.transpose(turned[:, v, :], gate_rows[:, v * P : (v + 1) * P], ident[:])
        nc.scalar.copy(out=gate_cols[:], in_=turned[:, :, :D])
        gate_ps = [psum.tile([P, 2, V], F32, name="gate_ps", tag=f"g{q}") for q in range(PAIRS)]
        for q in range(PAIRS):
            for r in range(2):
                for v in range(HALVES):
                    column = gate_cols[:, v, 2 * q + r : 2 * q + r + 1]
                    nc.tensor.transpose(gate_ps[q][:, r, v * P : (v + 1) * P], column.to_broadcast([P, P]), ident[:])

        gate_sb = [keep.tile([P, V], F32, name=f"gate_sb{d}", align_bytes=64) for d in range(D) if d != 0]
        gate_sb.insert(0, placed.tile([P, V], F32, name="gate_sb0", offset=0, align_bytes=64))
        for d in range(D):
            nc.scalar.copy(out=gate_sb[d][:], in_=gate_ps[d // 2][:, d % 2, :])

        x_il = [keep.tile([P, S, PACK], BF16, name=f"x_il{s}", align_bytes=64) for s in range(PASSES)]
        x_codes = [
            keep.tile([P, S], U32, name="x_codes0", tag="x_slot0", align_bytes=64),
            keep.tile([P, S], U32, name="x_codes1", align_bytes=64),
        ]
        x_scales0 = keep.tile([P, S], U8, name="x_scales0", align_bytes=64)
        x_scales1 = []

        def node_scales(s, nodes):
            if s == 0:
                return x_scales0[:, nodes]
            half = nodes.start // (S // 2)
            return x_scales1[half][:, nodes.start - half * (S // 2) : nodes.stop - half * (S // 2)]

        def quantize_nodes(s, nodes):
            nc.vector.quantize_mx(
                out=x_codes[s][:, nodes].bitcast(FP8X4),
                scales=node_scales(s, nodes),
                in_=x_il[s][:, nodes, :].rearrange("p t j -> p (t j)"),
            )

        picked = keep.tile([P, PACK, S], F32, name="picked")
        for j in range(2):
            nc.vector.tensor_copy(picked[:, j, :], x_pairs[0][:, j, :].indirect(offs_sb[:]))
        for n0 in (0, S // 2):
            nodes = slice(n0, n0 + S // 2)
            entries = offs_sb[:, nodes.start // LIST_COL : nodes.stop // LIST_COL]
            for j in range(2):
                nc.vector.tensor_copy(picked[:, 2 + j, nodes], x_pairs[1][:, j, :].indirect(entries))
            interleave_on_scalar(x_il[0][:, nodes, :], picked[:, :, nodes])
        for j in range(PACK):
            nc.vector.tensor_copy(x_il[LAST][:, :, j], x_raw[j][:].indirect(offs_sb[:]))
            if j == 0:
                quantize_nodes(0, slice(0, S))
        interleave_w1(0, 0)
        interleave_w1(0, LAST)
        quantize_w1_pass(0, 0)
        x_scales1.append(keep.tile([P, S // 2], U8, name="x_scales1", tag="w1_slot0_0", align_bytes=64))
        quantize_nodes(LAST, slice(0, 2 * P))
        quantize_w1_pass(0, LAST)
        x_scales1.append(keep.tile([P, S // 2], U8, name="x_scales1", tag=f"w1_slot0_{LAST}", align_bytes=64))
        quantize_nodes(LAST, slice(2 * P, 3 * P))
        quantize_nodes(LAST, slice(3 * P, S))

        accs = {}

        def pieces(b):
            width = S // len(ACC_BANKS[b])
            return [slice(n0, n0 + width) for n0 in range(0, S, width)]

        def project(b, s):
            if s == 0:
                accs[b] = [psum.tile([P, S // len(ACC_BANKS[b])], F32, name="acc", tag=bank) for bank in ACC_BANKS[b]]
            for acc, nodes in zip(accs[b], pieces(b)):
                width = nodes.stop - nodes.start
                step = width if s == 0 else min(width, S // 2)
                for n0 in range(0, width, step):
                    part = slice(nodes.start + n0, nodes.start + n0 + step)
                    nc.tensor.matmul_mx(
                        out=acc[:, n0 : n0 + step],
                        lhsT=w1_codes[b][:, s].bitcast(FP8X4),
                        lhsT_scale=w1_scales[b][:, s],
                        rhs=x_codes[s][:, part].bitcast(FP8X4),
                        rhs_scale=node_scales(s, part),
                        start=(s == 0),
                        stop=(s == LAST and n0 + step == width),
                    )

        def relu(b, h=None):
            if h is None:
                h = hidden.tile([P, S], F32, name="h")
            for i, (acc, nodes) in enumerate(zip(accs[b], pieces(b))):
                if b == 0 and i % 2 == 0:
                    nc.vector.tensor_relu(h[:, nodes], acc[:])
                else:
                    nc.scalar.activation(h[:, nodes], acc[:], RELU)
            return h

        def held(slot, width):
            return keep.tile([P, width], F32, name="held", tag=slot, align_bytes=64)

        sums = {}
        last_sums = []
        z_il = [keep.tile([P, V * PACK], BF16, name=f"z_il{s}", align_bytes=64) for s in range(PASSES)]
        z_codes = [keep.tile([P, V], U32, name=f"z_codes{s}", align_bytes=64) for s in range(PASSES)]
        z_scales = {}
        z_rows = {}

        def entries(d, n0, n1):
            return pos_sb[d][:, n0 // LIST_COL : n1 // LIST_COL]

        def sum_tile(b, v):
            if b == BLOCKS - 1:
                return last_sums[v][:]
            return sums[b // PACK][v][:, (b % PACK) * P : (b % PACK + 1) * P]

        def add_transposed(b, v, prod, start, stop):
            nc.tensor.matmul(sum_tile(b, v), prod, ident[:], start=start, stop=stop, is_transpose=True)

        def gather_fused(b, d, h, prod=None):
            if prod is None:
                prod = prods.tile([P, V], F32, name="prod")
            nc.vector.tensor_tensor(prod[:], h[:].indirect(pos_sb[d][:]), gate_sb[d][:], MULT)
            for v in range(HALVES):
                add_transposed(b, v, prod[:, v * P : (v + 1) * P], d == 0, d == D - 1)

        def multiply_pair(b, q, pair, prod):
            nc.vector.tensor_tensor(prod[:], pair[:], gate_ps[q][:], MULT)
            for v in range(HALVES):
                for r in range(2):
                    add_transposed(b, v, prod[:, r, v * P : (v + 1) * P], (q, r) == (1, 0), (q, r) == (0, 1))

        pairs = {}

        def pair_tile(b, q):
            if b == FUSED_BLOCKS:
                return raws.tile([P, 2, V], F32, name=f"pair_held{q}", offset=q * 2 * V * 4, align_bytes=64)
            return fetched.tile([P, 2, V], F32, name="pair")

        def fetch_on_vector(b, h):
            pairs[b, 0] = pair_tile(b, 0)
            nc.vector.tensor_copy(pairs[b, 0][:, 0, :], h[:].indirect(pos_sb[0][:]))
            cut = VECTOR_SHARE[b]
            if cut > 0:
                nc.vector.tensor_copy(pairs[b, 0][:, 1, :cut], h[:].indirect(entries(1, 0, cut)))

        def aggregate_shared(b, h):
            pairs[b, 1] = pair_tile(b, 1)
            for r in range(2):
                nc.scalar.activation(pairs[b, 1][:, r, :], h[:].indirect(pos_sb[2 + r][:]), COPY)
            h_next = relu(b + 1)
            cut = VECTOR_SHARE[b]
            if cut < V:
                nc.scalar.activation(pairs[b, 0][:, 1, cut:], h[:].indirect(entries(1, cut, V)), COPY)
            multiply_pair(b, 1, pairs[b, 1], pairs[b, 1])
            if b + 1 in VECTOR_SHARE:
                fetch_on_vector(b + 1, h_next)
            multiply_pair(b, 0, pairs[b, 0], pairs[b, 0])
            return h_next

        def aggregate_half(b, h, v):
            targets = slice(v * P, (v + 1) * P)
            first = LAST_SCALAR_TURN[v]
            pair = fetched.tile([P, D - first, P], F32, name="pair")
            for d in range(first, D):
                nc.scalar.activation(pair[:, d - first, :], h[:].indirect(entries(d, targets.start, targets.stop)), COPY)
            order = list(range(first - 1, -1, -1))
            order.insert(v, "pair")
            for i, d in enumerate(order):
                if d == "pair":
                    nc.vector.tensor_tensor(pair[:], pair[:], gate_ps[1][:, first - 2 :, targets], MULT)
                    for r in range(D - first):
                        add_transposed(b, v, pair[:, r, :], i == 0 and r == 0, False)
                else:
                    prod = keep.tile([P, P], F32, name="prod_half", tag=f"prod{v}_{d}", align_bytes=64)
                    window = h[:].indirect(entries(d, targets.start, targets.stop))
                    nc.vector.tensor_tensor(prod[:], window, gate_sb[d][:, targets], MULT)
                    add_transposed(b, v, prod[:], i == 0, i == len(order) - 1)

        def round_z(s, v, b0, b1):
            src = last_sums[v][:] if (s, b0) == (LAST, PACK - 1) else sums[s][v][:, b0 * P : b1 * P]
            dst = z_rows[s, v][:].rearrange("t (u p e) -> t u p e", u=2, e=2)
            per_block = P // PACK
            nc.scalar.copy(
                out=dst[:, :, b0 * per_block : b1 * per_block, :],
                in_=src.rearrange("t (p u e) -> t u p e", u=2, e=2),
            )

        def turn_z(s, v0, v1, bank):
            words = psum.tile([P, v1 - v0, 2, P], F32, name="words", tag=bank)
            for v in range(v0, v1):
                for u in range(2):
                    run = z_rows[s, v][:, u * (K_PASS // 2) : (u + 1) * (K_PASS // 2)].bitcast(F32)
                    nc.tensor.transpose(words[:, v - v0, u, :], run, ident[:])
            nc.scalar.copy(
                out=z_il[s][:, v0 * K_PASS : v1 * K_PASS].bitcast(F32).rearrange("p (v n u) -> p v n u", n=P, u=2),
                in_=words[:].rearrange("p v u n -> p v n u"),
            )

        def quantize_z(s, v0, v1):
            nc.vector.quantize_mx(
                out=z_codes[s][:, v0 * P : v1 * P].bitcast(FP8X4),
                scales=z_scales[s][:, v0 * P : v1 * P],
                in_=z_il[s][:, v0 * K_PASS : v1 * K_PASS],
            )

        def out_pass(acc, s, m, v, start):
            targets = slice(v * P, (v + 1) * P)
            nc.tensor.matmul_mx(
                out=acc,
                lhsT=w2_codes[s][:, m * P : (m + 1) * P].bitcast(FP8X4),
                lhsT_scale=w2_scales[s, m],
                rhs=z_codes[s][:, targets].bitcast(FP8X4),
                rhs_scale=z_scales[s][:, targets],
                start=start,
                stop=not start,
            )

        def open_sums(s):
            sums[s] = [psum.tile([P, K_PASS], F32, name="sums", tag=bank) for bank in SUM_BANKS[s]]

        project(0, 0)
        project(0, LAST)
        interleave_w1(1, 0)
        quantize_w1_pass(1, 0)
        nc.vector.tensor_copy(
            out=w1_il[1][:, LAST].rearrange("p (c i) j -> p c j i", i=4),
            in_=w1_raw[1][LAST][:].rearrange("p j (c i) -> p c j i", i=4),
        )
        h = relu(0, held("w1_slot1_0", S))
        project(1, 0)
        open_sums(0)
        for b in range(FUSED_BLOCKS):
            tight = b < 2
            if tight:
                gather_fused(b, 0, h)
                quantize_w1_pass(b + 1, LAST)
                project(b + 1, LAST)
            group = W1_GROUPS[b + 2]
            for member in group:
                interleave_w1(member, 0)
            before = group if b < 2 else group[:1]
            for member in before:
                interleave_w1(member, LAST)
            h_next = relu(b + 1, held(f"w1_slot{b + 2}_0", S))
            for member in group[len(before) :]:
                interleave_w1(member, LAST)
            for d in range(1 if tight else 0, D):
                gather_fused(b, d, h, held(f"w1_slot{b + 1}_{LAST}", V) if tight and d == 1 else None)
                ahead = {(1, 2): 3, (2, 0): 4, (2, 3): 5, (3, 0): 6}.get((b, d))
                if ahead:
                    quantize_w1(ahead)
                    for s in range(PASSES):
                        project(ahead, s)
            if b == 0:
                quantize_w1_pass(2, 0)
                project(2, 0)
            h = h_next
        quantize_w1(BLOCKS - 1)
        interleave_on_gpsimd(w2_il[:], w2_raw[:].rearrange("p s j n -> p s n j"))
        for s, v in ((0, 0), (0, 1), (LAST, 0)):
            z_rows[s, v] = keep.tile([P, K_PASS], BF16, name=f"z_rows{s}_{v}", align_bytes=64)
        fetch_on_vector(FUSED_BLOCKS, h)
        for b in range(FUSED_BLOCKS, BLOCKS - 1):
            if b == PACK:
                open_sums(LAST)
            if b + 2 == BLOCKS - 1:
                for s in range(PASSES):
                    project(b + 2, s)
            h = aggregate_shared(b, h)
            if b in (PACK, PACK + 1):
                round_z(0, b - PACK, 0, PACK)

        turn_z(0, 0, HALVES, "a")

        for v, bank in enumerate(("b", "h1")):
            last_sums.append(psum.tile([P, P], F32, name="last_sums", tag=bank))
            aggregate_half(BLOCKS - 1, h, v)
        z_rows[LAST, 1] = keep.tile([P, K_PASS], BF16, name="z_rows_last", tag="prod0_0", align_bytes=64)
        for v in range(HALVES):
            round_z(LAST, v, 0, PACK - 1)
            round_z(LAST, v, PACK - 1, PACK)
        for v, bank in enumerate(("a", "h0")):
            turn_z(LAST, v, v + 1, bank)

        out_rows = out.rearrange("(m p) v -> p m v", p=P)
        out_acc = {}

        def open_out(v, m, bank):
            out_acc[v, m] = psum.tile([P, P], F32, name="out_acc", tag=bank)
            out_pass(out_acc[v, m][:], 0, m, v, True)

        def close_pair(v, m0, copies):
            result = keep.tile([P, 2, P], F32, name=f"result{v}_{m0}")
            for i, copy in enumerate(copies):
                out_pass(out_acc[v, m0 + i][:], LAST, m0 + i, v, False)
                copy(out=result[:, i, :], in_=out_acc[v, m0 + i][:])
            nc.sync.dma_start(out=out_rows[:, m0 : m0 + 2, v * P : (v + 1) * P], in_=result[:])

        def held_scales(name, first, width):
            return placed.tile([P, width], U8, name=name, offset=first, align_bytes=64)

        z_scales[0] = held_scales("z_scales0", 0, V)
        quantize_z(0, 0, 1)
        for m, bank in enumerate(("g0", "g1")):
            quantize_w2(0, m * P, (m + 1) * P, held_scales(f"w2_scales0_{m}", V + m * P, P))
            open_out(0, m, bank)
        quantize_z(0, 1, 2)
        for m, bank in enumerate(("c", "d")):
            open_out(1, m, bank)
        quantize_w2(LAST, 0, N // 2, held_scales("w2_scales1_0", 3 * V, V))
        z_scales[LAST] = keep.tile([P, V], U8, name="z_scales1", align_bytes=64)
        quantize_z(LAST, 0, 1)
        close_pair(0, 0, (nc.vector.tensor_copy, nc.scalar.copy))
        quantize_w2(0, N // 2, N, held_scales("w2_scales0_2", 2 * V, V))
        for m, bank in ((2, "h1"), (3, "a")):
            open_out(0, m, bank)
        quantize_w2(LAST, N // 2, N, keep.tile([P, V], U8, name="w2_scales1_2", tag="prod1_1", align_bytes=64))
        quantize_z(LAST, 1, 2)
        close_pair(0, 2, (nc.vector.tensor_copy, nc.scalar.copy))
        for m, bank in ((3, "h0"), (2, "b")):
            open_out(1, m, bank)
        for m0 in (0, 2):
            close_pair(1, m0, (nc.vector.tensor_copy, nc.scalar.copy))
